import numpy as np
import ml_dtypes


def mxq(x, axis, fmt="e4m3"):
    dtype, down = {"e4m3": (ml_dtypes.float8_e4m3fn, 7), "e5m2": (ml_dtypes.float8_e5m2, 14)}[fmt]
    v = np.moveaxis(np.asarray(x, np.float32).astype(ml_dtypes.bfloat16).astype(np.float64), axis, -1)
    blocks = v.reshape(v.shape[:-1] + (-1, 32))
    amax = np.abs(blocks).max(-1, keepdims=True)
    byte = np.maximum(np.where(amax > 0, np.frexp(amax)[1] - 1 + 127, 0) - down, 1)
    scale = np.exp2(byte - 127.0)
    codes = (blocks / scale).astype(np.float32).astype(dtype).astype(np.float64)
    return np.moveaxis((codes * scale).reshape(v.shape), -1, axis)


WIDE = False


def mx_kscale(k):
    if not WIDE:
        return np.ones(k)
    levels = np.array([10, -10, 5, -5, 0])
    if k % 512:
        return np.exp2(np.random.permutation(np.resize(levels, k // 32))).repeat(32)
    a = np.empty((k // 512, 16))
    for p in range(k // 512):
        a[p, :8] = np.random.permutation(np.resize(levels, 8))
        for g in range(8):
            far = levels[np.abs(levels - a[p, g]) >= 10]
            a[p, g + 8] = far[np.random.randint(len(far))]
    return np.exp2(a.ravel()).repeat(32)


def f64(x):
    return np.asarray(x).astype(np.float64)


def striped(idx):
    return np.tile(idx.reshape(-1, 16).T, (8, 1)).astype(np.uint16)


def unstriped(offs):
    return offs[:16].T.reshape(-1).astype(np.int64)


E2M1 = np.array([0.0, 0.5, 1.0, 1.5, 2.0, 3.0, 4.0, 6.0, -0.0, -0.5, -1.0, -1.5, -2.0, -3.0, -4.0, -6.0])


def pack_weight(w, fmt):
    k, n = w.shape
    w = f64(np.asarray(w, np.float32).astype(ml_dtypes.bfloat16)).reshape(k // 32, 32, n)
    amax = np.abs(w).max(1)
    if fmt == "e4m3":
        byte = np.frexp(amax)[1] - 1 + 127 - 7
    else:
        mant, ex = np.frexp(amax / 6.0)
        byte = np.where(mant > 0.5, ex, ex - 1) + 127
    byte = np.clip(np.where(amax > 0, byte, 1), 1, 254)
    scaled = (w * np.exp2(127.0 - byte)[:, None, :]).reshape(k, n).astype(np.float32)
    by_word = np.ascontiguousarray(scaled.reshape(k // 512, 128, 4, n).transpose(0, 1, 3, 2))
    if fmt == "e4m3":
        words = by_word.astype(ml_dtypes.float8_e4m3fn).view(np.uint8)
    else:
        c = by_word.astype(ml_dtypes.float4_e2m1fn).view(np.uint8) & 0xF
        words = (c[..., 0::2] | (c[..., 1::2] << 4)).reshape(k // 512, 128, 2 * n)
    return np.ascontiguousarray(words), np.ascontiguousarray(byte.astype(np.uint8).reshape(k // 512, 16, n))


def unpack_weight(words, scales, fmt):
    g, _, n = scales.shape
    words = np.ascontiguousarray(words).reshape(g, 128, n, -1)
    if fmt == "e4m3":
        vals = words.view(ml_dtypes.float8_e4m3fn).astype(np.float64)
    else:
        nib = np.empty((g, 128, n, 4), np.uint8)
        nib[..., 0::2] = words & 0xF
        nib[..., 1::2] = words >> 4
        vals = E2M1[nib]
    vals = vals * np.repeat(np.exp2(scales.astype(np.float64) - 127.0), 8, axis=1)[..., None]
    return vals.transpose(0, 1, 3, 2).reshape(g * 512, n)


def gelu(v):
    return 0.5 * v * (1.0 + np.tanh(np.sqrt(2.0 / np.pi) * (v + 0.044715 * v**3)))


def bf(x):
    return np.asarray(x, np.float32).astype(ml_dtypes.bfloat16)

def planes(Y):
    n, m = Y.shape
    b = f64(bf(Y)).reshape(n // 32, 32, m)
    amax = np.abs(b).max(1)
    byte = np.clip(np.where(amax > 0, np.frexp(amax)[1] - 1 + 127 - 7, 1), 1, 254)
    codes = (b * np.exp2(127.0 - byte)[:, None, :]).reshape(n, m).astype(np.float32).astype(ml_dtypes.float8_e4m3fn).view(np.uint8)
    words = codes.reshape(n // 512, 128, 4, m).transpose(0, 1, 3, 2)
    return np.ascontiguousarray(words), np.ascontiguousarray(byte.astype(np.uint8).reshape(n // 512, 16, m))


K, T, S, H, N = 1024, 4096, 1024, 512, 1024

def setup_inputs():
    n = np.random.standard_normal
    s = mx_kscale(K)[:, None]
    u = mx_kscale(H)[:, None]
    tab_words, tab_scales = pack_weight(n((K, T)) * s, "e4m3")
    offs = striped(np.random.permutation(T)[:S])
    ws = (0.8 * n((K, H)) / np.sqrt(K) / s * u.T).astype(np.float32)
    wb_words, wb_scales = pack_weight(0.7 * n((K, H)) / np.sqrt(K) / s * u.T, "e2m1")
    wq_words, wq_scales = pack_weight(0.5 * n((K, H)) / np.sqrt(K) / s, "e4m3")
    gain = np.exp(0.8 * n(N))
    wt = (0.7 * n((H, N)) / np.sqrt(H) / u * gain).astype(np.float32)
    bt = (0.5 * n(N) * gain).astype(np.float32)
    return {"tab_words": tab_words, "tab_scales": tab_scales, "offs": offs, "ws": ws,
            "wb_words": wb_words, "wb_scales": wb_scales,
            "wq_words": wq_words, "wq_scales": wq_scales, "wt": wt, "bt": bt}

def reference(tab_words, tab_scales, offs, ws, wb_words, wb_scales, wq_words, wq_scales, wt, bt):
    v = unpack_weight(tab_words, tab_scales, "e4m3")[:, unstriped(offs)]
    wb = unpack_weight(wb_words, wb_scales, "e2m1")
    wq = unpack_weight(wq_words, wq_scales, "e4m3")
    sig = mxq(f64(ws), 0, "e4m3").T @ v
    bkg = wb.T @ v
    q = wq.T @ v
    h = (sig - bkg) * np.exp(-q)
    y = (mxq(f64(wt), 0, "e4m3").T @ mxq(h, 0, "e4m3")) + f64(bt)[:, None]
    words, scales = planes(y)
    return y, words, scales

@@ -1,0 +1,236 @@
+from contextlib import ExitStack
+
+import concourse.mybir as mybir
+
+K, T, S, H, N = 1024, 4096, 1024, 512, 1024
+FLOPS = 2 * (3 * K * H * S + H * N * S)
+
+F32 = mybir.dt.float32
+BF16 = mybir.dt.bfloat16
+I32 = mybir.dt.int32
+U32 = mybir.dt.uint32
+U16 = mybir.dt.uint16
+U8 = mybir.dt.uint8
+FP8X4 = mybir.dt.float8_e4m3fn_x4
+FP4X4 = mybir.dt.float4_e2m1fn_x4
+ACT = mybir.ActivationFunctionType
+ALU = mybir.AluOpType
+
+P = 128
+PACK = 4
+PASSES = K // (P * PACK)
+GROUPS = N // (P * PACK)
+CHUNK = 128
+CHUNKS = S // CHUNK
+HALF = 512
+BANK = 512
+SPANS = [256, 256, 256, 256]
+V_SC, WQ_SC, WB_SC = 0, S, S + H
+PLANE = S + 2 * H
+
+
+def tile_list_hit_significance_tagging_kernel(
+    tc, tab_words, tab_scales, offs, ws, wb_words, wb_scales, wq_words, wq_scales, wt, bt, out_0, out_1, out_2
+):
+    nc = tc.nc
+    with ExitStack() as ctx:
+        keep = ctx.enter_context(tc.tile_pool(name="keep", bufs=1))
+        psum = ctx.enter_context(tc.psum_pool(name="psum", bufs=1))
+
+        def sb(name, shape, dtype, tag=None):
+            return keep.tile(shape, dtype, name=name, tag=tag or name, align_bytes=64)
+
+        def bank(b):
+            return psum.tile([P, BANK], F32, name="bank%d" % b, tag="bank%d" % b)
+
+        offsets = keep.tile([P, S // 16], U16, name="offsets")
+        nc.sync.dma_start(offsets[:], offs)
+        rows = 16 * PASSES
+        sc_window = sb("sc_window", [P, T], U8)
+        nc.sync.dma_start(out=sc_window[0:rows, :].bitcast(I32), in_=tab_scales.rearrange("a q t -> (a q) t").bitcast(I32))
+        nc.vector.memset(sc_window[32:64, :].bitcast(I32), 0)
+        nc.vector.memset(sc_window[64:128, :].bitcast(I32), 0)
+        wq_sc_raw = sb("wq_sc_raw", [rows, H // 4], I32)
+        nc.scalar.dma_start(out=wq_sc_raw[:], in_=wq_scales.rearrange("a q c -> (a q) c").bitcast(I32))
+        wb_sc_raw = sb("wb_sc_raw", [rows, H // 4], I32)
+        nc.scalar.dma_start(out=wb_sc_raw[:], in_=wb_scales.rearrange("a q c -> (a q) c").bitcast(I32))
+
+        tab = []
+        wq_raw = sb("wq_raw", [P, PASSES, H], I32)
+        bias = sb("bias", [P, GROUPS, PACK], F32)
+
+        def load_tab(a, tag):
+            tab.append(sb("tab%d" % a, [P, T], I32, tag=tag))
+            nc.sync.dma_start(out=tab[a][:], in_=tab_words[a].rearrange("p t i -> p (t i)").bitcast(I32))
+
+        load_tab(0, "tab0")
+        nc.sync.dma_start(out=wq_raw[:], in_=wq_words.rearrange("a p c i -> p a (c i)").bitcast(I32))
+        wb_raw = sb("wb_raw", [P, PASSES, H // 2], I32)
+        nc.sync.dma_start(out=wb_raw[:], in_=wb_words.rearrange("a p c -> p a c").bitcast(I32))
+
+        plane = [sb("plane%d" % a, [P, PLANE], U8) for a in range(PASSES)]
+        for a in range(PASSES):
+            nc.gpsimd.memset(plane[a][:].bitcast(I32), 0)
+        sc_picked = sb("sc_picked", [P, S], U8)
+        nc.vector.tensor_copy(sc_picked[:], sc_window[:].indirect(offsets[:]))
+        stage = sb("stage", [rows, PLANE // 4], I32)
+        nc.vector.tensor_copy(stage[:, 0 : S // 4], sc_picked[0:rows, :].bitcast(I32))
+        for raw, c0 in ((wq_sc_raw, WQ_SC), (wb_sc_raw, WB_SC)):
+            nc.vector.tensor_copy(
+                stage[:, c0 // 4 : (c0 + H) // 4].rearrange("p (t b w) -> p t b w", t=PACK, w=2),
+                raw[:].rearrange("p (b t w) -> p t b w", t=PACK, w=2),
+            )
+        for a in range(PASSES):
+            for q in range(4):
+                (nc.scalar if a == 0 else nc.gpsimd).dma_start(
+                    out=plane[a][32 * q : 32 * q + 4, :].bitcast(I32), in_=stage[16 * a + 4 * q : 16 * a + 4 * q + 4, :]
+                )
+
+        nc.gpsimd.dma_start(out=bias[:], in_=bt.rearrange("(g p t) -> p g t", g=GROUPS, t=PACK))
+        load_tab(1, "wb_sc_raw")
+
+        v = [[sb("v%d_%d" % (a, h), [P, HALF], U32) for h in range(S // HALF)] for a in range(PASSES)]
+
+        def gather(a, h):
+            cols = slice(h * HALF // 16, (h + 1) * HALF // 16)
+            nc.vector.tensor_copy(v[a][h][:], tab[a][:].bitcast(U32).indirect(offsets[:, cols]))
+
+        gather(0, 0)
+        wq = sb("wq", [P, PASSES, H], I32)
+        nc.vector.tensor_copy(
+            wq[:].rearrange("p a (t b w) -> p a t b w", t=PACK, w=8),
+            wq_raw[:].rearrange("p a (b t w) -> p a t b w", t=PACK, w=8),
+        )
+        wb = sb("wb", [P, PASSES, H // 2], I32)
+        nc.vector.tensor_copy(
+            wb[:].rearrange("p a (t b w) -> p a t b w", t=PACK, w=4),
+            wb_raw[:].rearrange("p a (b t w) -> p a t b w", t=PACK, w=4),
+        )
+        ws_raw = [sb("ws_raw%d" % a, [P, PACK, H], F32, tag=("wq_raw", "wb_raw")[a]) for a in range(PASSES)]
+        for a in range(PASSES):
+            nc.sync.dma_start(out=ws_raw[a][:], in_=ws[512 * a : 512 * (a + 1), :].rearrange("(p j) c -> p j c", j=PACK))
+        gather(0, 1)
+        gather(1, 0)
+        gather(1, 1)
+        wt_raw = [sb("wt_raw%d" % g, [P, PACK, 512], F32, tag=("tab0", "wb_sc_raw")[g]) for g in range(GROUPS)]
+        wt_rows = wt.rearrange("(b j i) n -> j b i n", j=PACK, i=8)
+        for g in range(GROUPS):
+            for j in range(PACK):
+                nc.sync.dma_start(out=wt_raw[g][:, j, :], in_=wt_rows[j][:, :, 512 * g : 512 * (g + 1)])
+
+        def first_stage(acc, c, a, words, dtype, width, scales, start, stop):
+            h, o = divmod(c * CHUNK, HALF)
+            for t in range(PACK):
+                nc.tensor.matmul_mx(
+                    out=acc[:, t * CHUNK : (t + 1) * CHUNK],
+                    lhsT=words[:, t * width : (t + 1) * width].bitcast(dtype),
+                    lhsT_scale=scales[:, t * P : (t + 1) * P],
+                    rhs=v[a][h][:, o : o + CHUNK].bitcast(FP8X4),
+                    rhs_scale=plane[a][:, V_SC + c * CHUNK : V_SC + (c + 1) * CHUNK],
+                    start=start and t == 0,
+                    stop=stop and t == PACK - 1,
+                )
+
+        def hit_major(acc):
+            return acc[:].rearrange("p (t j) -> p j t", t=PACK)
+
+        q_acc = [bank(c) for c in range(CHUNKS)]
+        inv_noise = [sb("inv_noise%d" % c, [P, CHUNK, PACK], F32) for c in range(CHUNKS)]
+        for a in range(PASSES):
+            for c in range(CHUNKS):
+                first_stage(q_acc[c], c, a, wq[:, a, :], FP8X4, P, plane[a][:, WQ_SC : WQ_SC + H], a == 0, a == PASSES - 1)
+                if a == PASSES - 1:
+                    nc.scalar.activation(out=inv_noise[c][:], in_=hit_major(q_acc[c]), func=ACT.Exp, scale=-1.0)
+
+        ws_words = [sb("ws_words%d" % a, [P, H], U32) for a in range(PASSES)]
+        ws_sc = [sb("ws_sc%d" % a, [P, H], U8) for a in range(PASSES)]
+        for a in range(PASSES):
+            ws_bf = sb("ws_bf%d" % a, [P, H * PACK], BF16)
+            nc.vector.tensor_scalar(
+                out=ws_bf[:].rearrange("p (t b x) -> p b t x", t=PACK, x=8 * PACK),
+                in0=ws_raw[a][:].rearrange("p j c -> p c j"),
+                scalar1=-1.0,
+                scalar2=None,
+                op0=ALU.mult,
+            )
+            nc.vector.quantize_mx(out=ws_words[a][:].bitcast(FP8X4), scales=ws_sc[a][:], in_=ws_bf[:])
+
+        wt_words = [sb("wt_words%d" % g, [P, 512], U32) for g in range(GROUPS)]
+        wt_sc = [sb("wt_sc%d" % g, [P, 512], U8) for g in range(GROUPS)]
+
+        def prepare_wt(g):
+            wt_bf = sb("wt_bf%d" % g, [P, 512 * PACK], BF16)
+            nc.scalar.copy(
+                out=wt_bf[:].rearrange("p (t m j) -> p m t j", t=PACK, j=PACK),
+                in_=wt_raw[g][:].rearrange("p j (m t) -> p m t j", t=PACK),
+            )
+            nc.vector.quantize_mx(out=wt_words[g][:].bitcast(FP8X4), scales=wt_sc[g][:], in_=wt_bf[:])
+
+        y_sc = sb("y_sc", [P, GROUPS, S], U8)
+        ring = []
+        j0 = 0
+        for s, w in enumerate(SPANS):
+            chunks = list(range(j0 // CHUNK, (j0 + w) // CHUNK))
+            h_bf = sb("h_bf%d" % s, [P, w, PACK], BF16)
+            for i, c in enumerate(chunks):
+                acc = bank(c)
+                for a in range(PASSES):
+                    first_stage(acc, c, a, wb[:, a, :], FP4X4, P // 2, plane[a][:, WB_SC : WB_SC + H], a == 0, False)
+                for a in range(PASSES):
+                    first_stage(acc, c, a, ws_words[a][:], FP8X4, P, ws_sc[a][:], False, a == PASSES - 1)
+                nc.vector.scalar_tensor_tensor(
+                    out=h_bf[:, i * CHUNK : (i + 1) * CHUNK, :],
+                    in0=hit_major(acc),
+                    scalar=-1.0,
+                    in1=inv_noise[c][:],
+                    op0=ALU.mult,
+                    op1=ALU.mult,
+                )
+            h_words = sb("h_words%d" % s, [P, w], U32)
+            h_sc = sb("h_sc%d" % s, [P, w], U8)
+            nc.vector.quantize_mx(out=h_words[:].bitcast(FP8X4), scales=h_sc[:], in_=h_bf[:].rearrange("p j t -> p (j t)"))
+            ring = chunks + ring
+            per_bank = BANK // w
+            for g in range(GROUPS):
+                if s == 0:
+                    prepare_wt(g)
+                y = sb("y%d_%d" % (s, g), [P, PACK, w], F32)
+                for t0 in range(0, PACK, per_bank):
+                    b = ring[0]
+                    ring = ring[1:] + [b]
+                    acc = bank(b)
+                    for t in range(t0, t0 + per_bank):
+                        nc.tensor.matmul_mx(
+                            out=acc[:, (t - t0) * w : (t - t0 + 1) * w],
+                            lhsT=wt_words[g][:, t * P : (t + 1) * P].bitcast(FP8X4),
+                            lhsT_scale=wt_sc[g][:, t * P : (t + 1) * P],
+                            rhs=h_words[:].bitcast(FP8X4),
+                            rhs_scale=h_sc[:],
+                            start=True,
+                            stop=True,
+                        )
+                    for t in range(t0, t0 + per_bank):
+                        nc.scalar.activation(
+                            out=y[:, t, :],
+                            in_=acc[:, (t - t0) * w : (t - t0 + 1) * w],
+                            func=ACT.Identity,
+                            bias=bias[:, g, t : t + 1],
+                        )
+                nc.sync.dma_start(
+                    out=out_0[512 * g : 512 * (g + 1), j0 : j0 + w].rearrange("(p t) j -> p t j", t=PACK), in_=y[:]
+                )
+                y_bf = sb("y_bf%d_%d" % (s, g), [P, w, PACK], BF16)
+                nc.vector.tensor_copy(y_bf[:], y[:].rearrange("p t j -> p j t"))
+                y_words = sb("y_words%d_%d" % (s, g), [P, w], U32)
+                nc.vector.quantize_mx(
+                    out=y_words[:].bitcast(FP8X4), scales=y_sc[:, g, j0 : j0 + w], in_=y_bf[:].rearrange("p j t -> p (j t)")
+                )
+                nc.sync.dma_start(
+                    out=out_1[g].rearrange("p m t -> p (m t)").bitcast(I32)[:, j0 : j0 + w], in_=y_words[:].bitcast(I32)
+                )
+            j0 = j0 + w
+        for q in range(4):
+            nc.sync.dma_start(
+                out=out_2[:, 4 * q : 4 * q + 4, :].rearrange("g r m -> r g m").bitcast(I32),
+                in_=y_sc[32 * q : 32 * q + 4, :, :].bitcast(I32),
+            )

@@ -24,7 +24,7 @@ CHUNK = 128
 CHUNKS = S // CHUNK
 HALF = 512
 BANK = 512
-SPANS = [256, 256, 256, 256]
+SPAN = 256
 V_SC, WQ_SC, WB_SC = 0, S, S + H
 PLANE = S + 2 * H
 
@@ -57,7 +57,6 @@ def tile_list_hit_significance_tagging_kernel(
 
         tab = []
         wq_raw = sb("wq_raw", [P, PASSES, H], I32)
-        bias = sb("bias", [P, GROUPS, PACK], F32)
 
         def load_tab(a, tag):
             tab.append(sb("tab%d" % a, [P, T], I32, tag=tag))
@@ -65,12 +64,10 @@ def tile_list_hit_significance_tagging_kernel(
 
         load_tab(0, "tab0")
         nc.sync.dma_start(out=wq_raw[:], in_=wq_words.rearrange("a p c i -> p a (c i)").bitcast(I32))
-        wb_raw = sb("wb_raw", [P, PASSES, H // 2], I32)
-        nc.sync.dma_start(out=wb_raw[:], in_=wb_words.rearrange("a p c -> p a c").bitcast(I32))
 
         plane = [sb("plane%d" % a, [P, PLANE], U8) for a in range(PASSES)]
         for a in range(PASSES):
-            nc.gpsimd.memset(plane[a][:].bitcast(I32), 0)
+            nc.vector.memset(plane[a][:].bitcast(I32), 0)
         sc_picked = sb("sc_picked", [P, S], U8)
         nc.vector.tensor_copy(sc_picked[:], sc_window[:].indirect(offsets[:]))
         stage = sb("stage", [rows, PLANE // 4], I32)
@@ -80,14 +77,15 @@ def tile_list_hit_significance_tagging_kernel(
                 stage[:, c0 // 4 : (c0 + H) // 4].rearrange("p (t b w) -> p t b w", t=PACK, w=2),
                 raw[:].rearrange("p (b t w) -> p t b w", t=PACK, w=2),
             )
-        for a in range(PASSES):
+        def carry_scales(a):
             for q in range(4):
-                (nc.scalar if a == 0 else nc.gpsimd).dma_start(
+                nc.sync.dma_start(
                     out=plane[a][32 * q : 32 * q + 4, :].bitcast(I32), in_=stage[16 * a + 4 * q : 16 * a + 4 * q + 4, :]
                 )
 
-        nc.gpsimd.dma_start(out=bias[:], in_=bt.rearrange("(g p t) -> p g t", g=GROUPS, t=PACK))
+        carry_scales(0)
         load_tab(1, "wb_sc_raw")
+        carry_scales(1)
 
         v = [[sb("v%d_%d" % (a, h), [P, HALF], U32) for h in range(S // HALF)] for a in range(PASSES)]
 
@@ -101,22 +99,21 @@ def tile_list_hit_significance_tagging_kernel(
             wq[:].rearrange("p a (t b w) -> p a t b w", t=PACK, w=8),
             wq_raw[:].rearrange("p a (b t w) -> p a t b w", t=PACK, w=8),
         )
-        wb = sb("wb", [P, PASSES, H // 2], I32)
-        nc.vector.tensor_copy(
-            wb[:].rearrange("p a (t b w) -> p a t b w", t=PACK, w=4),
-            wb_raw[:].rearrange("p a (b t w) -> p a t b w", t=PACK, w=4),
-        )
-        ws_raw = [sb("ws_raw%d" % a, [P, PACK, H], F32, tag=("wq_raw", "wb_raw")[a]) for a in range(PASSES)]
+        gather(0, 1)
+        ws_raw = [sb("ws_raw%d" % a, [P, PACK, H], F32, tag=("wq_raw", "tab0")[a]) for a in range(PASSES)]
         for a in range(PASSES):
             nc.sync.dma_start(out=ws_raw[a][:], in_=ws[512 * a : 512 * (a + 1), :].rearrange("(p j) c -> p j c", j=PACK))
-        gather(0, 1)
+        wb_raw = sb("wb_raw", [P, PASSES, H // 2], I32, tag="stage")
+        nc.sync.dma_start(out=wb_raw[:], in_=wb_words.rearrange("a p c -> p a c").bitcast(I32))
         gather(1, 0)
         gather(1, 1)
-        wt_raw = [sb("wt_raw%d" % g, [P, PACK, 512], F32, tag=("tab0", "wb_sc_raw")[g]) for g in range(GROUPS)]
+        wt_raw = sb("wt_raw", [P, GROUPS, PACK, 512], F32, tag="wb_sc_raw")
         wt_rows = wt.rearrange("(b j i) n -> j b i n", j=PACK, i=8)
+        bias = sb("bias", [P, GROUPS, PACK], F32, tag="sc_picked")
+        nc.scalar.dma_start(out=bias[:], in_=bt.rearrange("(g p t) -> p g t", g=GROUPS, t=PACK))
         for g in range(GROUPS):
             for j in range(PACK):
-                nc.sync.dma_start(out=wt_raw[g][:, j, :], in_=wt_rows[j][:, :, 512 * g : 512 * (g + 1)])
+                nc.sync.dma_start(out=wt_raw[:, g, j, :], in_=wt_rows[j][:, :, 512 * g : 512 * (g + 1)])
 
         def first_stage(acc, c, a, words, dtype, width, scales, start, stop):
             h, o = divmod(c * CHUNK, HALF)
@@ -155,80 +152,111 @@ def tile_list_hit_significance_tagging_kernel(
             )
             nc.vector.quantize_mx(out=ws_words[a][:].bitcast(FP8X4), scales=ws_sc[a][:], in_=ws_bf[:])
 
+        wb = sb("wb", [P, PASSES, H // 2], I32)
+        nc.vector.tensor_copy(
+            wb[:].rearrange("p a (t b w) -> p a t b w", t=PACK, w=4),
+            wb_raw[:].rearrange("p a (b t w) -> p a t b w", t=PACK, w=4),
+        )
+
         wt_words = [sb("wt_words%d" % g, [P, 512], U32) for g in range(GROUPS)]
         wt_sc = [sb("wt_sc%d" % g, [P, 512], U8) for g in range(GROUPS)]
+        wt_bf = [sb("wt_bf%d" % g, [P, 512 * PACK], BF16) for g in range(GROUPS)]
 
-        def prepare_wt(g):
-            wt_bf = sb("wt_bf%d" % g, [P, 512 * PACK], BF16)
+        def round_wt(g):
             nc.scalar.copy(
-                out=wt_bf[:].rearrange("p (t m j) -> p m t j", t=PACK, j=PACK),
-                in_=wt_raw[g][:].rearrange("p j (m t) -> p m t j", t=PACK),
+                out=wt_bf[g][:].rearrange("p (t m j) -> p m j t", t=PACK, j=PACK),
+                in_=wt_raw[:, g, :, :].rearrange("p j (m t) -> p m j t", t=PACK),
             )
-            nc.vector.quantize_mx(out=wt_words[g][:].bitcast(FP8X4), scales=wt_sc[g][:], in_=wt_bf[:])
 
+        def quantize_wt(g):
+            nc.vector.quantize_mx(out=wt_words[g][:].bitcast(FP8X4), scales=wt_sc[g][:], in_=wt_bf[g][:])
+
+        spans = S // SPAN
+        per_span = SPAN // CHUNK
+        h_bf = [sb("h_bf%d" % s, [P, SPAN, PACK], BF16) for s in range(spans)]
+        h_words = [sb("h_words%d" % s, [P, SPAN], U32) for s in range(spans)]
+        h_sc = [sb("h_sc%d" % s, [P, SPAN], U8) for s in range(spans)]
         y_sc = sb("y_sc", [P, GROUPS, S], U8)
-        ring = []
-        j0 = 0
-        for s, w in enumerate(SPANS):
-            chunks = list(range(j0 // CHUNK, (j0 + w) // CHUNK))
-            h_bf = sb("h_bf%d" % s, [P, w, PACK], BF16)
-            for i, c in enumerate(chunks):
-                acc = bank(c)
-                for a in range(PASSES):
-                    first_stage(acc, c, a, wb[:, a, :], FP4X4, P // 2, plane[a][:, WB_SC : WB_SC + H], a == 0, False)
-                for a in range(PASSES):
-                    first_stage(acc, c, a, ws_words[a][:], FP8X4, P, ws_sc[a][:], False, a == PASSES - 1)
-                nc.vector.scalar_tensor_tensor(
-                    out=h_bf[:, i * CHUNK : (i + 1) * CHUNK, :],
-                    in0=hit_major(acc),
-                    scalar=-1.0,
-                    in1=inv_noise[c][:],
-                    op0=ALU.mult,
-                    op1=ALU.mult,
-                )
-            h_words = sb("h_words%d" % s, [P, w], U32)
-            h_sc = sb("h_sc%d" % s, [P, w], U8)
-            nc.vector.quantize_mx(out=h_words[:].bitcast(FP8X4), scales=h_sc[:], in_=h_bf[:].rearrange("p j t -> p (j t)"))
-            ring = chunks + ring
-            per_bank = BANK // w
-            for g in range(GROUPS):
-                if s == 0:
-                    prepare_wt(g)
-                y = sb("y%d_%d" % (s, g), [P, PACK, w], F32)
-                for t0 in range(0, PACK, per_bank):
-                    b = ring[0]
-                    ring = ring[1:] + [b]
-                    acc = bank(b)
-                    for t in range(t0, t0 + per_bank):
-                        nc.tensor.matmul_mx(
-                            out=acc[:, (t - t0) * w : (t - t0 + 1) * w],
-                            lhsT=wt_words[g][:, t * P : (t + 1) * P].bitcast(FP8X4),
-                            lhsT_scale=wt_sc[g][:, t * P : (t + 1) * P],
-                            rhs=h_words[:].bitcast(FP8X4),
-                            rhs_scale=h_sc[:],
-                            start=True,
-                            stop=True,
-                        )
-                    for t in range(t0, t0 + per_bank):
-                        nc.scalar.activation(
-                            out=y[:, t, :],
-                            in_=acc[:, (t - t0) * w : (t - t0 + 1) * w],
-                            func=ACT.Identity,
-                            bias=bias[:, g, t : t + 1],
-                        )
-                nc.sync.dma_start(
-                    out=out_0[512 * g : 512 * (g + 1), j0 : j0 + w].rearrange("(p t) j -> p t j", t=PACK), in_=y[:]
-                )
-                y_bf = sb("y_bf%d_%d" % (s, g), [P, w, PACK], BF16)
-                nc.vector.tensor_copy(y_bf[:], y[:].rearrange("p t j -> p j t"))
-                y_words = sb("y_words%d_%d" % (s, g), [P, w], U32)
-                nc.vector.quantize_mx(
-                    out=y_words[:].bitcast(FP8X4), scales=y_sc[:, g, j0 : j0 + w], in_=y_bf[:].rearrange("p j t -> p (j t)")
-                )
-                nc.sync.dma_start(
-                    out=out_1[g].rearrange("p m t -> p (m t)").bitcast(I32)[:, j0 : j0 + w], in_=y_words[:].bitcast(I32)
-                )
-            j0 = j0 + w
+        y_bf = {}
+
+        def excess(c):
+            s, i = divmod(c, per_span)
+            acc = bank(c)
+            first_stage(acc, c, 0, ws_words[0][:], FP8X4, P, ws_sc[0][:], True, False)
+            for a in range(PASSES):
+                first_stage(acc, c, a, wb[:, a, :], FP4X4, P // 2, plane[a][:, WB_SC : WB_SC + H], False, False)
+            first_stage(acc, c, 1, ws_words[1][:], FP8X4, P, ws_sc[1][:], False, True)
+            nc.vector.scalar_tensor_tensor(
+                out=h_bf[s][:, i * CHUNK : (i + 1) * CHUNK, :],
+                in0=hit_major(acc),
+                scalar=-1.0,
+                in1=inv_noise[c][:],
+                op0=ALU.mult,
+                op1=ALU.mult,
+            )
+
+        def quantize_h(s):
+            nc.vector.quantize_mx(
+                out=h_words[s][:].bitcast(FP8X4), scales=h_sc[s][:], in_=h_bf[s][:].rearrange("p j t -> p (j t)")
+            )
+
+        def features(s, g):
+            cols = slice(s * SPAN, (s + 1) * SPAN)
+            y = sb("y%d_%d" % (s, g), [P, PACK, SPAN], F32)
+            for pair in range(2):
+                acc = bank(per_span * max(s - g, 0) + pair)
+                for u in range(2):
+                    t = 2 * pair + u
+                    nc.tensor.matmul_mx(
+                        out=acc[:, u * SPAN : (u + 1) * SPAN],
+                        lhsT=wt_words[g][:, t * P : (t + 1) * P].bitcast(FP8X4),
+                        lhsT_scale=wt_sc[g][:, t * P : (t + 1) * P],
+                        rhs=h_words[s][:].bitcast(FP8X4),
+                        rhs_scale=h_sc[s][:],
+                        start=True,
+                        stop=True,
+                    )
+                for u in range(2):
+                    t = 2 * pair + u
+                    nc.scalar.activation(
+                        out=y[:, t, :], in_=acc[:, u * SPAN : (u + 1) * SPAN], func=ACT.Identity, bias=bias[:, g, t : t + 1]
+                    )
+            nc.sync.dma_start(out=out_0[512 * g : 512 * (g + 1), cols].rearrange("(p t) j -> p t j", t=PACK), in_=y[:])
+            y_bf[s, g] = sb("y_bf%d_%d" % (s, g), [P, SPAN, PACK], BF16)
+            nc.vector.tensor_copy(
+                y_bf[s, g][:].rearrange("p (c i) t -> p c t i", i=4), y[:].rearrange("p t (c i) -> p c t i", i=4)
+            )
+
+        def quantize_y(s, g):
+            cols = slice(s * SPAN, (s + 1) * SPAN)
+            y_words = sb("y_words%d_%d" % (s, g), [P, SPAN], U32)
+            nc.vector.quantize_mx(
+                out=y_words[:].bitcast(FP8X4), scales=y_sc[:, g, cols], in_=y_bf[s, g][:].rearrange("p j t -> p (j t)")
+            )
+            nc.sync.dma_start(out=out_1[g].rearrange("p m t -> p (m t)").bitcast(I32)[:, cols], in_=y_words[:].bitcast(I32))
+
+        excess(0)
+        excess(1)
+        round_wt(0)
+        excess(2)
+        quantize_h(0)
+        excess(3)
+        quantize_wt(0)
+        round_wt(1)
+        for s in range(spans):
+            ahead = s + 2 < spans
+            features(s, 0)
+            if s == 0:
+                quantize_wt(1)
+            if s + 1 < spans:
+                quantize_h(s + 1)
+            if ahead:
+                excess(per_span * (s + 2))
+            features(s, 1)
+            quantize_y(s, 0)
+            if ahead:
+                excess(per_span * (s + 2) + 1)
+            quantize_y(s, 1)
         for q in range(4):
             nc.sync.dma_start(
                 out=out_2[:, 4 * q : 4 * q + 4, :].rearrange("g r m -> r g m").bitcast(I32),

@@ -50,13 +50,15 @@ def tile_list_hit_significance_tagging_kernel(
         nc.sync.dma_start(out=sc_window[0:rows, :].bitcast(I32), in_=tab_scales.rearrange("a q t -> (a q) t").bitcast(I32))
         nc.vector.memset(sc_window[32:64, :].bitcast(I32), 0)
         nc.vector.memset(sc_window[64:128, :].bitcast(I32), 0)
-        wq_sc_raw = sb("wq_sc_raw", [rows, H // 4], I32)
-        nc.scalar.dma_start(out=wq_sc_raw[:], in_=wq_scales.rearrange("a q c -> (a q) c").bitcast(I32))
-        wb_sc_raw = sb("wb_sc_raw", [rows, H // 4], I32)
-        nc.scalar.dma_start(out=wb_sc_raw[:], in_=wb_scales.rearrange("a q c -> (a q) c").bitcast(I32))
+        w_sc_raw = sb("w_sc_raw", [P, 2 * H], U8)
+        nc.scalar.dma_start(out=w_sc_raw[0:rows, 0:H].bitcast(I32), in_=wq_scales.rearrange("a q c -> (a q) c").bitcast(I32))
+        nc.scalar.dma_start(out=w_sc_raw[0:rows, H : 2 * H].bitcast(I32), in_=wb_scales.rearrange("a q c -> (a q) c").bitcast(I32))
+        nc.vector.memset(w_sc_raw[32:64, :].bitcast(I32), 0)
+        nc.vector.memset(w_sc_raw[64:128, :].bitcast(I32), 0)
 
         tab = []
         wq_raw = sb("wq_raw", [P, PASSES, H], I32)
+        wb_raw = sb("wb_raw", [P, PASSES, 2 * H], U8)
 
         def load_tab(a, tag):
             tab.append(sb("tab%d" % a, [P, T], I32, tag=tag))
@@ -64,27 +66,28 @@ def tile_list_hit_significance_tagging_kernel(
 
         load_tab(0, "tab0")
         nc.sync.dma_start(out=wq_raw[:], in_=wq_words.rearrange("a p c i -> p a (c i)").bitcast(I32))
+        nc.sync.dma_start(out=wb_raw[:].bitcast(I32), in_=wb_words.rearrange("a p c -> p a c").bitcast(I32))
 
         plane = [sb("plane%d" % a, [P, PLANE], U8) for a in range(PASSES)]
         for a in range(PASSES):
-            nc.vector.memset(plane[a][:].bitcast(I32), 0)
+            nc.gpsimd.memset(plane[a][:].bitcast(I32), 0)
+        stage = sb("stage", [P, PLANE], U8)
+        nc.vector.tensor_copy(
+            stage[:, WQ_SC:PLANE].rearrange("p (x t c i) -> p x c t i", x=2, t=PACK, i=16),
+            w_sc_raw[:].rearrange("p (x c i t) -> p x c t i", x=2, t=PACK, i=16),
+        )
         sc_picked = sb("sc_picked", [P, S], U8)
         nc.vector.tensor_copy(sc_picked[:], sc_window[:].indirect(offsets[:]))
-        stage = sb("stage", [rows, PLANE // 4], I32)
-        nc.vector.tensor_copy(stage[:, 0 : S // 4], sc_picked[0:rows, :].bitcast(I32))
-        for raw, c0 in ((wq_sc_raw, WQ_SC), (wb_sc_raw, WB_SC)):
-            nc.vector.tensor_copy(
-                stage[:, c0 // 4 : (c0 + H) // 4].rearrange("p (t b w) -> p t b w", t=PACK, w=2),
-                raw[:].rearrange("p (b t w) -> p t b w", t=PACK, w=2),
-            )
+        nc.vector.tensor_copy(stage[0:rows, V_SC : V_SC + S].bitcast(I32), sc_picked[0:rows, :].bitcast(I32))
+
         def carry_scales(a):
             for q in range(4):
                 nc.sync.dma_start(
-                    out=plane[a][32 * q : 32 * q + 4, :].bitcast(I32), in_=stage[16 * a + 4 * q : 16 * a + 4 * q + 4, :]
+                    out=plane[a][32 * q : 32 * q + 4, :].bitcast(I32), in_=stage[16 * a + 4 * q : 16 * a + 4 * q + 4, :].bitcast(I32)
                 )
 
         carry_scales(0)
-        load_tab(1, "wb_sc_raw")
+        load_tab(1, "sc_picked")
         carry_scales(1)
 
         v = [[sb("v%d_%d" % (a, h), [P, HALF], U32) for h in range(S // HALF)] for a in range(PASSES)]
@@ -96,24 +99,27 @@ def tile_list_hit_significance_tagging_kernel(
         gather(0, 0)
         wq = sb("wq", [P, PASSES, H], I32)
         nc.vector.tensor_copy(
-            wq[:].rearrange("p a (t b w) -> p a t b w", t=PACK, w=8),
-            wq_raw[:].rearrange("p a (b t w) -> p a t b w", t=PACK, w=8),
+            wq[:].rearrange("p a (t c i) -> p a c t i", t=PACK, i=4),
+            wq_raw[:].rearrange("p a (c i t) -> p a c t i", t=PACK, i=4),
         )
-        gather(0, 1)
-        ws_raw = [sb("ws_raw%d" % a, [P, PACK, H], F32, tag=("wq_raw", "tab0")[a]) for a in range(PASSES)]
+        w_raw = sb("w_raw", [P, PASSES + GROUPS, PACK, 512], F32, tag="wq_raw")
+        ws_raw = [w_raw[:, a, :, :] for a in range(PASSES)]
+        wt_raw = [w_raw[:, PASSES + g, :, :] for g in range(GROUPS)]
         for a in range(PASSES):
-            nc.sync.dma_start(out=ws_raw[a][:], in_=ws[512 * a : 512 * (a + 1), :].rearrange("(p j) c -> p j c", j=PACK))
-        wb_raw = sb("wb_raw", [P, PASSES, H // 2], I32, tag="stage")
-        nc.sync.dma_start(out=wb_raw[:], in_=wb_words.rearrange("a p c -> p a c").bitcast(I32))
+            nc.sync.dma_start(out=ws_raw[a], in_=ws[512 * a : 512 * (a + 1), :].rearrange("(p j) c -> p j c", j=PACK))
+        for g in range(GROUPS):
+            nc.sync.dma_start(out=wt_raw[g], in_=wt[:, 512 * g : 512 * (g + 1)].rearrange("(p j) n -> p j n", j=PACK))
+        gather(0, 1)
+        bias = sb("bias", [P, GROUPS, PACK], F32, tag="tab0")
+        nc.sync.dma_start(out=bias[:], in_=bt.rearrange("(g p t) -> p g t", g=GROUPS, t=PACK))
+        wb = sb("wb", [P, PASSES, 2 * H], U8)
+        for a in range(PASSES):
+            nc.vector.tensor_copy(
+                wb[:, a, :].rearrange("p (t c i e) -> p c t i e", t=PACK, i=8, e=2),
+                wb_raw[:, a, :].rearrange("p (c i t e) -> p c t i e", t=PACK, i=8, e=2),
+            )
         gather(1, 0)
         gather(1, 1)
-        wt_raw = sb("wt_raw", [P, GROUPS, PACK, 512], F32, tag="wb_sc_raw")
-        wt_rows = wt.rearrange("(b j i) n -> j b i n", j=PACK, i=8)
-        bias = sb("bias", [P, GROUPS, PACK], F32, tag="sc_picked")
-        nc.scalar.dma_start(out=bias[:], in_=bt.rearrange("(g p t) -> p g t", g=GROUPS, t=PACK))
-        for g in range(GROUPS):
-            for j in range(PACK):
-                nc.sync.dma_start(out=wt_raw[:, g, j, :], in_=wt_rows[j][:, :, 512 * g : 512 * (g + 1)])
 
         def first_stage(acc, c, a, words, dtype, width, scales, start, stop):
             h, o = divmod(c * CHUNK, HALF)
@@ -144,19 +150,13 @@ def tile_list_hit_significance_tagging_kernel(
         for a in range(PASSES):
             ws_bf = sb("ws_bf%d" % a, [P, H * PACK], BF16)
             nc.vector.tensor_scalar(
-                out=ws_bf[:].rearrange("p (t b x) -> p b t x", t=PACK, x=8 * PACK),
-                in0=ws_raw[a][:].rearrange("p j c -> p c j"),
+                out=ws_bf[:].rearrange("p (t m j) -> p m j t", t=PACK, j=PACK),
+                in0=ws_raw[a].rearrange("p j (m t) -> p m j t", t=PACK),
                 scalar1=-1.0,
                 scalar2=None,
                 op0=ALU.mult,
             )
             nc.vector.quantize_mx(out=ws_words[a][:].bitcast(FP8X4), scales=ws_sc[a][:], in_=ws_bf[:])
-
-        wb = sb("wb", [P, PASSES, H // 2], I32)
-        nc.vector.tensor_copy(
-            wb[:].rearrange("p a (t b w) -> p a t b w", t=PACK, w=4),
-            wb_raw[:].rearrange("p a (b t w) -> p a t b w", t=PACK, w=4),
-        )
 
         wt_words = [sb("wt_words%d" % g, [P, 512], U32) for g in range(GROUPS)]
         wt_sc = [sb("wt_sc%d" % g, [P, 512], U8) for g in range(GROUPS)]
@@ -165,7 +165,7 @@ def tile_list_hit_significance_tagging_kernel(
         def round_wt(g):
             nc.scalar.copy(
                 out=wt_bf[g][:].rearrange("p (t m j) -> p m j t", t=PACK, j=PACK),
-                in_=wt_raw[:, g, :, :].rearrange("p j (m t) -> p m j t", t=PACK),
+                in_=wt_raw[g].rearrange("p j (m t) -> p m j t", t=PACK),
             )
 
         def quantize_wt(g):
@@ -177,15 +177,16 @@ def tile_list_hit_significance_tagging_kernel(
         h_words = [sb("h_words%d" % s, [P, SPAN], U32) for s in range(spans)]
         h_sc = [sb("h_sc%d" % s, [P, SPAN], U8) for s in range(spans)]
         y_sc = sb("y_sc", [P, GROUPS, S], U8)
+        y_tiles = {}
         y_bf = {}
 
         def excess(c):
             s, i = divmod(c, per_span)
             acc = bank(c)
-            first_stage(acc, c, 0, ws_words[0][:], FP8X4, P, ws_sc[0][:], True, False)
             for a in range(PASSES):
-                first_stage(acc, c, a, wb[:, a, :], FP4X4, P // 2, plane[a][:, WB_SC : WB_SC + H], False, False)
-            first_stage(acc, c, 1, ws_words[1][:], FP8X4, P, ws_sc[1][:], False, True)
+                first_stage(acc, c, a, wb[:, a, :], FP4X4, 2 * P, plane[a][:, WB_SC : WB_SC + H], a == 0, False)
+            for a in range(PASSES):
+                first_stage(acc, c, a, ws_words[a][:], FP8X4, P, ws_sc[a][:], False, a == PASSES - 1)
             nc.vector.scalar_tensor_tensor(
                 out=h_bf[s][:, i * CHUNK : (i + 1) * CHUNK, :],
                 in0=hit_major(acc),
@@ -222,6 +223,10 @@ def tile_list_hit_significance_tagging_kernel(
                         out=y[:, t, :], in_=acc[:, u * SPAN : (u + 1) * SPAN], func=ACT.Identity, bias=bias[:, g, t : t + 1]
                     )
             nc.sync.dma_start(out=out_0[512 * g : 512 * (g + 1), cols].rearrange("(p t) j -> p t j", t=PACK), in_=y[:])
+            y_tiles[s, g] = y
+
+        def round_y(s, g):
+            y = y_tiles[s, g]
             y_bf[s, g] = sb("y_bf%d_%d" % (s, g), [P, SPAN, PACK], BF16)
             nc.vector.tensor_copy(
                 y_bf[s, g][:].rearrange("p (c i) t -> p c t i", i=4), y[:].rearrange("p t (c i) -> p c t i", i=4)
@@ -237,26 +242,25 @@ def tile_list_hit_significance_tagging_kernel(
 
         excess(0)
         excess(1)
-        round_wt(0)
-        excess(2)
-        quantize_h(0)
-        excess(3)
-        quantize_wt(0)
-        round_wt(1)
+        for g in range(GROUPS):
+            round_wt(g)
         for s in range(spans):
-            ahead = s + 2 < spans
-            features(s, 0)
-            if s == 0:
-                quantize_wt(1)
-            if s + 1 < spans:
-                quantize_h(s + 1)
+            ahead = s + 1 < spans
             if ahead:
-                excess(per_span * (s + 2))
-            features(s, 1)
-            quantize_y(s, 0)
+                excess(per_span * (s + 1))
+            quantize_h(s)
             if ahead:
-                excess(per_span * (s + 2) + 1)
-            quantize_y(s, 1)
+                excess(per_span * (s + 1) + 1)
+            for g in range(GROUPS):
+                if s == 0:
+                    quantize_wt(g)
+                features(s, g)
+        units = [(s, g) for s in range(spans) for g in range(GROUPS)]
+        for i, unit in enumerate(units):
+            round_y(*unit)
+            if i > 0:
+                quantize_y(*units[i - 1])
+        quantize_y(*units[-1])
         for q in range(4):
             nc.sync.dma_start(
                 out=out_2[:, 4 * q : 4 * q + 4, :].rearrange("g r m -> r g m").bitcast(I32),

@@ -24,7 +24,8 @@ CHUNK = 128
 CHUNKS = S // CHUNK
 HALF = 512
 BANK = 512
-SPAN = 256
+SPANS = [256, 256, 256, 256]
+PARTS = [slice(0, 256), slice(256, 512)]
 V_SC, WQ_SC, WB_SC = 0, S, S + H
 PLANE = S + 2 * H
 
@@ -102,13 +103,20 @@ def tile_list_hit_significance_tagging_kernel(
             wq[:].rearrange("p a (t c i) -> p a c t i", t=PACK, i=4),
             wq_raw[:].rearrange("p a (c i t) -> p a c t i", t=PACK, i=4),
         )
-        w_raw = sb("w_raw", [P, PASSES + GROUPS, PACK, 512], F32, tag="wq_raw")
-        ws_raw = [w_raw[:, a, :, :] for a in range(PASSES)]
-        wt_raw = [w_raw[:, PASSES + g, :, :] for g in range(GROUPS)]
-        for a in range(PASSES):
-            nc.sync.dma_start(out=ws_raw[a], in_=ws[512 * a : 512 * (a + 1), :].rearrange("(p j) c -> p j c", j=PACK))
-        for g in range(GROUPS):
-            nc.sync.dma_start(out=wt_raw[g], in_=wt[:, 512 * g : 512 * (g + 1)].rearrange("(p j) n -> p j n", j=PACK))
+        ws_rows = ws.rearrange("(a p j) c -> a p j c", a=PASSES, j=PACK)
+        wt_rows = wt.rearrange("(p j) (g n) -> g p j n", j=PACK, g=GROUPS)
+        w_raw = sb("w_raw", [P, (PASSES + GROUPS) * PACK * 512], F32, tag="wq_raw")
+        pieces = []
+        for n, (src, parts) in enumerate(
+            ((ws_rows[0], [slice(0, 512)]), (ws_rows[1], PARTS), (wt_rows[0], PARTS), (wt_rows[1], PARTS))
+        ):
+            pieces.append([])
+            for part in parts:
+                at = PACK * (512 * n + part.start)
+                raw = w_raw[:, at : at + PACK * (part.stop - part.start)].rearrange("p (j c) -> p j c", j=PACK)
+                nc.sync.dma_start(out=raw, in_=src[:, :, part])
+                pieces[n].append((part, raw))
+        ws_raw, wt_raw = pieces[:PASSES], pieces[PASSES:]
         gather(0, 1)
         bias = sb("bias", [P, GROUPS, PACK], F32, tag="tab0")
         nc.sync.dma_start(out=bias[:], in_=bt.rearrange("(g p t) -> p g t", g=GROUPS, t=PACK))
@@ -145,43 +153,53 @@ def tile_list_hit_significance_tagging_kernel(
                 if a == PASSES - 1:
                     nc.scalar.activation(out=inv_noise[c][:], in_=hit_major(q_acc[c]), func=ACT.Exp, scale=-1.0)
 
+        def dealt(rounded, part, raw):
+            ms = slice(part.start // PACK, part.stop // PACK)
+            return (
+                rounded[:].rearrange("p (t m j) -> p m j t", t=PACK, j=PACK)[:, ms, :, :],
+                raw.rearrange("p j (m t) -> p m j t", t=PACK),
+            )
+
         ws_words = [sb("ws_words%d" % a, [P, H], U32) for a in range(PASSES)]
         ws_sc = [sb("ws_sc%d" % a, [P, H], U8) for a in range(PASSES)]
         for a in range(PASSES):
             ws_bf = sb("ws_bf%d" % a, [P, H * PACK], BF16)
-            nc.vector.tensor_scalar(
-                out=ws_bf[:].rearrange("p (t m j) -> p m j t", t=PACK, j=PACK),
-                in0=ws_raw[a].rearrange("p j (m t) -> p m j t", t=PACK),
-                scalar1=-1.0,
-                scalar2=None,
-                op0=ALU.mult,
-            )
+            for piece in ws_raw[a]:
+                dst, src = dealt(ws_bf, *piece)
+                nc.vector.tensor_scalar(out=dst, in0=src, scalar1=-1.0, scalar2=None, op0=ALU.mult)
             nc.vector.quantize_mx(out=ws_words[a][:].bitcast(FP8X4), scales=ws_sc[a][:], in_=ws_bf[:])
 
         wt_words = [sb("wt_words%d" % g, [P, 512], U32) for g in range(GROUPS)]
         wt_sc = [sb("wt_sc%d" % g, [P, 512], U8) for g in range(GROUPS)]
         wt_bf = [sb("wt_bf%d" % g, [P, 512 * PACK], BF16) for g in range(GROUPS)]
 
-        def round_wt(g):
-            nc.scalar.copy(
-                out=wt_bf[g][:].rearrange("p (t m j) -> p m j t", t=PACK, j=PACK),
-                in_=wt_raw[g].rearrange("p j (m t) -> p m j t", t=PACK),
-            )
+        def round_wt(g, part, copy):
+            copy(*dealt(wt_bf[g], *wt_raw[g][part]))
 
         def quantize_wt(g):
             nc.vector.quantize_mx(out=wt_words[g][:].bitcast(FP8X4), scales=wt_sc[g][:], in_=wt_bf[g][:])
 
-        spans = S // SPAN
-        per_span = SPAN // CHUNK
-        h_bf = [sb("h_bf%d" % s, [P, SPAN, PACK], BF16) for s in range(spans)]
-        h_words = [sb("h_words%d" % s, [P, SPAN], U32) for s in range(spans)]
-        h_sc = [sb("h_sc%d" % s, [P, SPAN], U8) for s in range(spans)]
+        spans = len(SPANS)
+        first = [sum(SPANS[:s]) for s in range(spans)]
+        chunks_of = [list(range(first[s] // CHUNK, (first[s] + SPANS[s]) // CHUNK)) for s in range(spans)]
+        h_bf = [sb("h_bf%d" % s, [P, SPANS[s], PACK], BF16) for s in range(spans)]
+        h_words = [sb("h_words%d" % s, [P, SPANS[s]], U32) for s in range(spans)]
+        h_sc = [sb("h_sc%d" % s, [P, SPANS[s]], U8) for s in range(spans)]
+        unit_banks = {}
+        ring = []
+        for s in range(spans):
+            ring = chunks_of[s] + ring
+            need = PACK * SPANS[s] // BANK
+            for g in range(GROUPS):
+                unit_banks[s, g] = ring[:need]
+                ring = ring[need:] + ring[:need]
         y_sc = sb("y_sc", [P, GROUPS, S], U8)
         y_tiles = {}
         y_bf = {}
 
         def excess(c):
-            s, i = divmod(c, per_span)
+            s = max(n for n in range(spans) if chunks_of[n][0] <= c)
+            i = c - chunks_of[s][0]
             acc = bank(c)
             for a in range(PASSES):
                 first_stage(acc, c, a, wb[:, a, :], FP4X4, 2 * P, plane[a][:, WB_SC : WB_SC + H], a == 0, False)
@@ -202,14 +220,17 @@ def tile_list_hit_significance_tagging_kernel(
             )
 
         def features(s, g):
-            cols = slice(s * SPAN, (s + 1) * SPAN)
-            y = sb("y%d_%d" % (s, g), [P, PACK, SPAN], F32)
-            for pair in range(2):
-                acc = bank(per_span * max(s - g, 0) + pair)
-                for u in range(2):
-                    t = 2 * pair + u
+            w = SPANS[s]
+            cols = slice(first[s], first[s] + w)
+            y = sb("y%d_%d" % (s, g), [P, PACK, w], F32)
+            per_bank = BANK // w
+            for n, b in enumerate(unit_banks[s, g]):
+                t0 = n * per_bank
+                acc = bank(b)
+                for u in range(per_bank):
+                    t = t0 + u
                     nc.tensor.matmul_mx(
-                        out=acc[:, u * SPAN : (u + 1) * SPAN],
+                        out=acc[:, u * w : (u + 1) * w],
                         lhsT=wt_words[g][:, t * P : (t + 1) * P].bitcast(FP8X4),
                         lhsT_scale=wt_sc[g][:, t * P : (t + 1) * P],
                         rhs=h_words[s][:].bitcast(FP8X4),
@@ -217,44 +238,48 @@ def tile_list_hit_significance_tagging_kernel(
                         start=True,
                         stop=True,
                     )
-                for u in range(2):
-                    t = 2 * pair + u
+                for u in range(per_bank):
+                    t = t0 + u
                     nc.scalar.activation(
-                        out=y[:, t, :], in_=acc[:, u * SPAN : (u + 1) * SPAN], func=ACT.Identity, bias=bias[:, g, t : t + 1]
+                        out=y[:, t, :], in_=acc[:, u * w : (u + 1) * w], func=ACT.Identity, bias=bias[:, g, t : t + 1]
                     )
             nc.sync.dma_start(out=out_0[512 * g : 512 * (g + 1), cols].rearrange("(p t) j -> p t j", t=PACK), in_=y[:])
             y_tiles[s, g] = y
 
         def round_y(s, g):
             y = y_tiles[s, g]
-            y_bf[s, g] = sb("y_bf%d_%d" % (s, g), [P, SPAN, PACK], BF16)
+            y_bf[s, g] = sb("y_bf%d_%d" % (s, g), [P, SPANS[s], PACK], BF16)
             nc.vector.tensor_copy(
                 y_bf[s, g][:].rearrange("p (c i) t -> p c t i", i=4), y[:].rearrange("p t (c i) -> p c t i", i=4)
             )
 
         def quantize_y(s, g):
-            cols = slice(s * SPAN, (s + 1) * SPAN)
-            y_words = sb("y_words%d_%d" % (s, g), [P, SPAN], U32)
+            cols = slice(first[s], first[s] + SPANS[s])
+            y_words = sb("y_words%d_%d" % (s, g), [P, SPANS[s]], U32)
             nc.vector.quantize_mx(
                 out=y_words[:].bitcast(FP8X4), scales=y_sc[:, g, cols], in_=y_bf[s, g][:].rearrange("p j t -> p (j t)")
             )
             nc.sync.dma_start(out=out_1[g].rearrange("p m t -> p (m t)").bitcast(I32)[:, cols], in_=y_words[:].bitcast(I32))
 
-        excess(0)
-        excess(1)
-        for g in range(GROUPS):
-            round_wt(g)
+        for c in chunks_of[0]:
+            excess(c)
+        round_wt(0, 0, nc.scalar.copy)
+        round_wt(0, 1, nc.scalar.copy)
+        round_wt(1, 0, nc.scalar.copy)
         for s in range(spans):
-            ahead = s + 1 < spans
-            if ahead:
-                excess(per_span * (s + 1))
+            ahead = chunks_of[s + 1] if s + 1 < spans else []
+            for c in ahead[:1]:
+                excess(c)
             quantize_h(s)
-            if ahead:
-                excess(per_span * (s + 1) + 1)
-            for g in range(GROUPS):
-                if s == 0:
-                    quantize_wt(g)
-                features(s, g)
+            if s == 0:
+                quantize_wt(0)
+            features(s, 0)
+            for c in ahead[1:]:
+                excess(c)
+            if s == 0:
+                round_wt(1, 1, nc.vector.tensor_copy)
+                quantize_wt(1)
+            features(s, 1)
         units = [(s, g) for s in range(spans) for g in range(GROUPS)]
         for i, unit in enumerate(units):
             round_y(*unit)
@@ -262,7 +287,7 @@ def tile_list_hit_significance_tagging_kernel(
                 quantize_y(*units[i - 1])
         quantize_y(*units[-1])
         for q in range(4):
-            nc.sync.dma_start(
+            nc.scalar.dma_start(
                 out=out_2[:, 4 * q : 4 * q + 4, :].rearrange("g r m -> r g m").bitcast(I32),
                 in_=y_sc[32 * q : 32 * q + 4, :, :].bitcast(I32),
             )

@@ -26,6 +26,8 @@ HALF = 512
 BANK = 512
 SPANS = [256, 256, 256, 256]
 PARTS = [slice(0, 256), slice(256, 512)]
+PIECE = 256
+AHEAD = 4
 V_SC, WQ_SC, WB_SC = 0, S, S + H
 PLANE = S + 2 * H
 
@@ -48,12 +50,12 @@ def tile_list_hit_significance_tagging_kernel(
         nc.sync.dma_start(offsets[:], offs)
         rows = 16 * PASSES
         sc_window = sb("sc_window", [P, T], U8)
-        nc.sync.dma_start(out=sc_window[0:rows, :].bitcast(I32), in_=tab_scales.rearrange("a q t -> (a q) t").bitcast(I32))
+        nc.sync.dma_start(out=sc_window[0:rows, :].bitcast(I32), in_=tab_scales.rearrange("a q t -> q a t").bitcast(I32))
         nc.vector.memset(sc_window[32:64, :].bitcast(I32), 0)
         nc.vector.memset(sc_window[64:128, :].bitcast(I32), 0)
         w_sc_raw = sb("w_sc_raw", [P, 2 * H], U8)
-        nc.scalar.dma_start(out=w_sc_raw[0:rows, 0:H].bitcast(I32), in_=wq_scales.rearrange("a q c -> (a q) c").bitcast(I32))
-        nc.scalar.dma_start(out=w_sc_raw[0:rows, H : 2 * H].bitcast(I32), in_=wb_scales.rearrange("a q c -> (a q) c").bitcast(I32))
+        nc.sync.dma_start(out=w_sc_raw[0:rows, 0:H].bitcast(I32), in_=wq_scales.rearrange("a q c -> q a c").bitcast(I32))
+        nc.sync.dma_start(out=w_sc_raw[0:rows, H : 2 * H].bitcast(I32), in_=wb_scales.rearrange("a q c -> q a c").bitcast(I32))
         nc.vector.memset(w_sc_raw[32:64, :].bitcast(I32), 0)
         nc.vector.memset(w_sc_raw[64:128, :].bitcast(I32), 0)
 
@@ -69,27 +71,20 @@ def tile_list_hit_significance_tagging_kernel(
         nc.sync.dma_start(out=wq_raw[:], in_=wq_words.rearrange("a p c i -> p a (c i)").bitcast(I32))
         nc.sync.dma_start(out=wb_raw[:].bitcast(I32), in_=wb_words.rearrange("a p c -> p a c").bitcast(I32))
 
-        plane = [sb("plane%d" % a, [P, PLANE], U8) for a in range(PASSES)]
-        for a in range(PASSES):
-            nc.gpsimd.memset(plane[a][:].bitcast(I32), 0)
+        planes = sb("planes", [P, PASSES * PLANE], U8)
+        nc.gpsimd.memset(planes[:].bitcast(I32), 0)
+        plane = [planes[:, a * PLANE : (a + 1) * PLANE] for a in range(PASSES)]
         stage = sb("stage", [P, PLANE], U8)
+        sc_picked = sb("sc_picked", [P, S], U8)
+        nc.vector.tensor_copy(sc_picked[:], sc_window[:].indirect(offsets[:]))
         nc.vector.tensor_copy(
             stage[:, WQ_SC:PLANE].rearrange("p (x t c i) -> p x c t i", x=2, t=PACK, i=16),
             w_sc_raw[:].rearrange("p (x c i t) -> p x c t i", x=2, t=PACK, i=16),
         )
-        sc_picked = sb("sc_picked", [P, S], U8)
-        nc.vector.tensor_copy(sc_picked[:], sc_window[:].indirect(offsets[:]))
         nc.vector.tensor_copy(stage[0:rows, V_SC : V_SC + S].bitcast(I32), sc_picked[0:rows, :].bitcast(I32))
-
-        def carry_scales(a):
-            for q in range(4):
-                nc.sync.dma_start(
-                    out=plane[a][32 * q : 32 * q + 4, :].bitcast(I32), in_=stage[16 * a + 4 * q : 16 * a + 4 * q + 4, :].bitcast(I32)
-                )
-
-        carry_scales(0)
+        for q in range(4):
+            nc.sync.dma_start(out=planes[32 * q : 32 * q + 4, :].bitcast(I32), in_=stage[8 * q : 8 * q + 8, :].bitcast(I32))
         load_tab(1, "sc_picked")
-        carry_scales(1)
 
         v = [[sb("v%d_%d" % (a, h), [P, HALF], U32) for h in range(S // HALF)] for a in range(PASSES)]
 
@@ -105,29 +100,24 @@ def tile_list_hit_significance_tagging_kernel(
         )
         ws_rows = ws.rearrange("(a p j) c -> a p j c", a=PASSES, j=PACK)
         wt_rows = wt.rearrange("(p j) (g n) -> g p j n", j=PACK, g=GROUPS)
-        w_raw = sb("w_raw", [P, (PASSES + GROUPS) * PACK * 512], F32, tag="wq_raw")
-        pieces = []
-        for n, (src, parts) in enumerate(
-            ((ws_rows[0], [slice(0, 512)]), (ws_rows[1], PARTS), (wt_rows[0], PARTS), (wt_rows[1], PARTS))
-        ):
-            pieces.append([])
-            for part in parts:
-                at = PACK * (512 * n + part.start)
-                raw = w_raw[:, at : at + PACK * (part.stop - part.start)].rearrange("p (j c) -> p j c", j=PACK)
-                nc.sync.dma_start(out=raw, in_=src[:, :, part])
-                pieces[n].append((part, raw))
-        ws_raw, wt_raw = pieces[:PASSES], pieces[PASSES:]
+        w_raw = sb("w_raw", [P, (PASSES + GROUPS) * PACK * 512 + GROUPS * 8], F32, tag="wq_raw")
+        bias = w_raw[:, (PASSES + GROUPS) * PACK * 512 :].rearrange("p (g t) -> p g t", g=GROUPS)
+        nc.sync.dma_start(out=bias[:, :, 0:PACK], in_=bt.rearrange("(g p t) -> p g t", g=GROUPS, t=PACK))
+        raws = []
+        for n, src in enumerate((ws_rows[0], ws_rows[1], wt_rows[0], wt_rows[1])):
+            raw = w_raw[:, PACK * 512 * n : PACK * 512 * (n + 1)].rearrange("p (j c) -> p j c", j=PACK)
+            nc.sync.dma_start(out=raw, in_=src)
+            raws.append(raw)
+        ws_raw, wt_raw = raws[:PASSES], raws[PASSES:]
         gather(0, 1)
-        bias = sb("bias", [P, GROUPS, PACK], F32, tag="tab0")
-        nc.sync.dma_start(out=bias[:], in_=bt.rearrange("(g p t) -> p g t", g=GROUPS, t=PACK))
+        gather(1, 0)
+        gather(1, 1)
         wb = sb("wb", [P, PASSES, 2 * H], U8)
         for a in range(PASSES):
             nc.vector.tensor_copy(
                 wb[:, a, :].rearrange("p (t c i e) -> p c t i e", t=PACK, i=8, e=2),
                 wb_raw[:, a, :].rearrange("p (c i t e) -> p c t i e", t=PACK, i=8, e=2),
             )
-        gather(1, 0)
-        gather(1, 1)
 
         def first_stage(acc, c, a, words, dtype, width, scales, start, stop):
             h, o = divmod(c * CHUNK, HALF)
@@ -147,26 +137,30 @@ def tile_list_hit_significance_tagging_kernel(
 
         q_acc = [bank(c) for c in range(CHUNKS)]
         inv_noise = [sb("inv_noise%d" % c, [P, CHUNK, PACK], F32) for c in range(CHUNKS)]
-        for a in range(PASSES):
-            for c in range(CHUNKS):
-                first_stage(q_acc[c], c, a, wq[:, a, :], FP8X4, P, plane[a][:, WQ_SC : WQ_SC + H], a == 0, a == PASSES - 1)
-                if a == PASSES - 1:
-                    nc.scalar.activation(out=inv_noise[c][:], in_=hit_major(q_acc[c]), func=ACT.Exp, scale=-1.0)
+
+        def noise(c, a):
+            first_stage(q_acc[c], c, a, wq[:, a, :], FP8X4, P, plane[a][:, WQ_SC : WQ_SC + H], a == 0, a == PASSES - 1)
+            if a == PASSES - 1:
+                nc.scalar.activation(out=inv_noise[c][:], in_=hit_major(q_acc[c]), func=ACT.Exp, scale=-1.0)
+
+        for c in range(CHUNKS):
+            noise(c, 0)
+        for c in range(CHUNKS // 2):
+            noise(c, 1)
 
         def dealt(rounded, part, raw):
             ms = slice(part.start // PACK, part.stop // PACK)
             return (
                 rounded[:].rearrange("p (t m j) -> p m j t", t=PACK, j=PACK)[:, ms, :, :],
-                raw.rearrange("p j (m t) -> p m j t", t=PACK),
+                raw.rearrange("p j (m t) -> p m j t", t=PACK)[:, ms, :, :],
             )
 
         ws_words = [sb("ws_words%d" % a, [P, H], U32) for a in range(PASSES)]
         ws_sc = [sb("ws_sc%d" % a, [P, H], U8) for a in range(PASSES)]
         for a in range(PASSES):
             ws_bf = sb("ws_bf%d" % a, [P, H * PACK], BF16)
-            for piece in ws_raw[a]:
-                dst, src = dealt(ws_bf, *piece)
-                nc.vector.tensor_scalar(out=dst, in0=src, scalar1=-1.0, scalar2=None, op0=ALU.mult)
+            dst, src = dealt(ws_bf, slice(0, 512), ws_raw[a])
+            nc.vector.tensor_scalar(out=dst, in0=src, scalar1=-1.0, scalar2=None, op0=ALU.mult)
             nc.vector.quantize_mx(out=ws_words[a][:].bitcast(FP8X4), scales=ws_sc[a][:], in_=ws_bf[:])
 
         wt_words = [sb("wt_words%d" % g, [P, 512], U32) for g in range(GROUPS)]
@@ -174,7 +168,7 @@ def tile_list_hit_significance_tagging_kernel(
         wt_bf = [sb("wt_bf%d" % g, [P, 512 * PACK], BF16) for g in range(GROUPS)]
 
         def round_wt(g, part, copy):
-            copy(*dealt(wt_bf[g], *wt_raw[g][part]))
+            copy(*dealt(wt_bf[g], PARTS[part], wt_raw[g]))
 
         def quantize_wt(g):
             nc.vector.quantize_mx(out=wt_words[g][:].bitcast(FP8X4), scales=wt_sc[g][:], in_=wt_bf[g][:])
@@ -186,9 +180,8 @@ def tile_list_hit_significance_tagging_kernel(
         h_words = [sb("h_words%d" % s, [P, SPANS[s]], U32) for s in range(spans)]
         h_sc = [sb("h_sc%d" % s, [P, SPANS[s]], U8) for s in range(spans)]
         unit_banks = {}
-        ring = []
+        ring = list(range(AHEAD, CHUNKS))
         for s in range(spans):
-            ring = chunks_of[s] + ring
             need = PACK * SPANS[s] // BANK
             for g in range(GROUPS):
                 unit_banks[s, g] = ring[:need]
@@ -197,14 +190,21 @@ def tile_list_hit_significance_tagging_kernel(
         y_tiles = {}
         y_bf = {}
 
+        d_acc = {}
+
+        def excess_open(c):
+            d_acc[c] = bank(c % AHEAD)
+            for a in range(PASSES):
+                first_stage(d_acc[c], c, a, wb[:, a, :], FP4X4, 2 * P, plane[a][:, WB_SC : WB_SC + H], a == 0, False)
+            first_stage(d_acc[c], c, 0, ws_words[0][:], FP8X4, P, ws_sc[0][:], False, False)
+
         def excess(c):
             s = max(n for n in range(spans) if chunks_of[n][0] <= c)
             i = c - chunks_of[s][0]
-            acc = bank(c)
-            for a in range(PASSES):
-                first_stage(acc, c, a, wb[:, a, :], FP4X4, 2 * P, plane[a][:, WB_SC : WB_SC + H], a == 0, False)
-            for a in range(PASSES):
-                first_stage(acc, c, a, ws_words[a][:], FP8X4, P, ws_sc[a][:], False, a == PASSES - 1)
+            if c not in d_acc:
+                excess_open(c)
+            acc = d_acc[c]
+            first_stage(acc, c, 1, ws_words[1][:], FP8X4, P, ws_sc[1][:], False, True)
             nc.vector.scalar_tensor_tensor(
                 out=h_bf[s][:, i * CHUNK : (i + 1) * CHUNK, :],
                 in0=hit_major(acc),
@@ -243,44 +243,58 @@ def tile_list_hit_significance_tagging_kernel(
                     nc.scalar.activation(
                         out=y[:, t, :], in_=acc[:, u * w : (u + 1) * w], func=ACT.Identity, bias=bias[:, g, t : t + 1]
                     )
-            nc.sync.dma_start(out=out_0[512 * g : 512 * (g + 1), cols].rearrange("(p t) j -> p t j", t=PACK), in_=y[:])
+                done = t0 + per_bank
+                if done % 2 == 0:
+                    rows_out = out_0[512 * g : 512 * (g + 1), cols].rearrange("(p t) j -> p t j", t=PACK)
+                    nc.sync.dma_start(out=rows_out[:, done - 2 : done, :], in_=y[:, done - 2 : done, :])
             y_tiles[s, g] = y
 
-        def round_y(s, g):
-            y = y_tiles[s, g]
-            y_bf[s, g] = sb("y_bf%d_%d" % (s, g), [P, SPANS[s], PACK], BF16)
+        y_words = {}
+
+        def round_y(s, g, o):
+            y_bf[s, g, o] = sb("y_bf%d_%d_%d" % (s, g, o), [P, SPANS[s], PACK], BF16)
             nc.vector.tensor_copy(
-                y_bf[s, g][:].rearrange("p (c i) t -> p c t i", i=4), y[:].rearrange("p t (c i) -> p c t i", i=4)
+                y_bf[s, g, o][:].rearrange("p (c i) t -> p c t i", i=4),
+                y_tiles[s, g][:].rearrange("p t (c i) -> p c t i", i=4),
             )
 
-        def quantize_y(s, g):
-            cols = slice(first[s], first[s] + SPANS[s])
-            y_words = sb("y_words%d_%d" % (s, g), [P, SPANS[s]], U32)
+        def quantize_y(s, g, o):
+            if s == 0:
+                y_words[g] = sb("y_words%d" % g, [P, S], U32)
             nc.vector.quantize_mx(
-                out=y_words[:].bitcast(FP8X4), scales=y_sc[:, g, cols], in_=y_bf[s, g][:].rearrange("p j t -> p (j t)")
+                out=y_words[g][:, first[s] : first[s] + SPANS[s]].bitcast(FP8X4),
+                scales=y_sc[:, g, first[s] : first[s] + SPANS[s]],
+                in_=y_bf[s, g, o][:].rearrange("p j t -> p (j t)"),
             )
-            nc.sync.dma_start(out=out_1[g].rearrange("p m t -> p (m t)").bitcast(I32)[:, cols], in_=y_words[:].bitcast(I32))
+            if s == spans - 1:
+                cols = slice(0, S)
+                nc.sync.dma_start(
+                    out=out_1[g].rearrange("p m t -> p (m t)").bitcast(I32)[:, cols], in_=y_words[g][:].bitcast(I32)
+                )
 
         for c in chunks_of[0]:
-            excess(c)
+            excess_open(c)
         round_wt(0, 0, nc.scalar.copy)
-        round_wt(0, 1, nc.scalar.copy)
-        round_wt(1, 0, nc.scalar.copy)
+        round_wt(0, 1, nc.vector.tensor_copy)
+        for c in chunks_of[0]:
+            excess(c)
+        quantize_wt(0)
+        quantize_h(0)
+        for c in range(CHUNKS // 2, CHUNKS):
+            noise(c, 1)
         for s in range(spans):
             ahead = chunks_of[s + 1] if s + 1 < spans else []
-            for c in ahead[:1]:
-                excess(c)
-            quantize_h(s)
-            if s == 0:
-                quantize_wt(0)
             features(s, 0)
-            for c in ahead[1:]:
-                excess(c)
             if s == 0:
-                round_wt(1, 1, nc.vector.tensor_copy)
+                round_wt(1, 0, nc.scalar.copy)
+                round_wt(1, 1, nc.scalar.copy)
                 quantize_wt(1)
+            for c in ahead:
+                excess(c)
+            if ahead:
+                quantize_h(s + 1)
             features(s, 1)
-        units = [(s, g) for s in range(spans) for g in range(GROUPS)]
+        units = [(s, g, o) for s in range(spans) for g in range(GROUPS) for o in range(1)]
         for i, unit in enumerate(units):
             round_y(*unit)
             if i > 0:

@@ -50,12 +50,12 @@ def tile_list_hit_significance_tagging_kernel(
         nc.sync.dma_start(offsets[:], offs)
         rows = 16 * PASSES
         sc_window = sb("sc_window", [P, T], U8)
-        nc.sync.dma_start(out=sc_window[0:rows, :].bitcast(I32), in_=tab_scales.rearrange("a q t -> q a t").bitcast(I32))
+        nc.sync.dma_start(out=sc_window[0:rows, :].bitcast(I32), in_=tab_scales.rearrange("a q t -> (a q) t").bitcast(I32))
         nc.vector.memset(sc_window[32:64, :].bitcast(I32), 0)
         nc.vector.memset(sc_window[64:128, :].bitcast(I32), 0)
         w_sc_raw = sb("w_sc_raw", [P, 2 * H], U8)
-        nc.sync.dma_start(out=w_sc_raw[0:rows, 0:H].bitcast(I32), in_=wq_scales.rearrange("a q c -> q a c").bitcast(I32))
-        nc.sync.dma_start(out=w_sc_raw[0:rows, H : 2 * H].bitcast(I32), in_=wb_scales.rearrange("a q c -> q a c").bitcast(I32))
+        nc.sync.dma_start(out=w_sc_raw[0:rows, 0:H].bitcast(I32), in_=wq_scales.rearrange("a q c -> (a q) c").bitcast(I32))
+        nc.sync.dma_start(out=w_sc_raw[0:rows, H : 2 * H].bitcast(I32), in_=wb_scales.rearrange("a q c -> (a q) c").bitcast(I32))
         nc.vector.memset(w_sc_raw[32:64, :].bitcast(I32), 0)
         nc.vector.memset(w_sc_raw[64:128, :].bitcast(I32), 0)
 
@@ -71,9 +71,9 @@ def tile_list_hit_significance_tagging_kernel(
         nc.sync.dma_start(out=wq_raw[:], in_=wq_words.rearrange("a p c i -> p a (c i)").bitcast(I32))
         nc.sync.dma_start(out=wb_raw[:].bitcast(I32), in_=wb_words.rearrange("a p c -> p a c").bitcast(I32))
 
-        planes = sb("planes", [P, PASSES * PLANE], U8)
-        nc.gpsimd.memset(planes[:].bitcast(I32), 0)
-        plane = [planes[:, a * PLANE : (a + 1) * PLANE] for a in range(PASSES)]
+        plane = [sb("plane%d" % a, [P, PLANE], U8) for a in range(PASSES)]
+        for a in range(PASSES):
+            nc.gpsimd.memset(plane[a][:].bitcast(I32), 0)
         stage = sb("stage", [P, PLANE], U8)
         sc_picked = sb("sc_picked", [P, S], U8)
         nc.vector.tensor_copy(sc_picked[:], sc_window[:].indirect(offsets[:]))
@@ -82,9 +82,16 @@ def tile_list_hit_significance_tagging_kernel(
             w_sc_raw[:].rearrange("p (x c i t) -> p x c t i", x=2, t=PACK, i=16),
         )
         nc.vector.tensor_copy(stage[0:rows, V_SC : V_SC + S].bitcast(I32), sc_picked[0:rows, :].bitcast(I32))
-        for q in range(4):
-            nc.sync.dma_start(out=planes[32 * q : 32 * q + 4, :].bitcast(I32), in_=stage[8 * q : 8 * q + 8, :].bitcast(I32))
+
+        def carry(a):
+            for r in range(4):
+                nc.sync.dma_start(
+                    out=plane[a][r:P:32, :].bitcast(I32), in_=stage[16 * a + r : 16 * (a + 1) : 4, :].bitcast(I32)
+                )
+
+        carry(0)
         load_tab(1, "sc_picked")
+        carry(1)
 
         v = [[sb("v%d_%d" % (a, h), [P, HALF], U32) for h in range(S // HALF)] for a in range(PASSES)]
 
@@ -173,41 +180,45 @@ def tile_list_hit_significance_tagging_kernel(
         def quantize_wt(g):
             nc.vector.quantize_mx(out=wt_words[g][:].bitcast(FP8X4), scales=wt_sc[g][:], in_=wt_bf[g][:])
 
-        spans = len(SPANS)
-        first = [sum(SPANS[:s]) for s in range(spans)]
-        chunks_of = [list(range(first[s] // CHUNK, (first[s] + SPANS[s]) // CHUNK)) for s in range(spans)]
-        h_bf = [sb("h_bf%d" % s, [P, SPANS[s], PACK], BF16) for s in range(spans)]
-        h_words = [sb("h_words%d" % s, [P, SPANS[s]], U32) for s in range(spans)]
-        h_sc = [sb("h_sc%d" % s, [P, SPANS[s]], U8) for s in range(spans)]
-        unit_banks = {}
-        ring = list(range(AHEAD, CHUNKS))
-        for s in range(spans):
-            need = PACK * SPANS[s] // BANK
-            for g in range(GROUPS):
-                unit_banks[s, g] = ring[:need]
-                ring = ring[need:] + ring[:need]
+        span_w = 256
+        spans = S // span_w
+        h_bf = [sb("h_bf%d" % s, [P, span_w, PACK], BF16) for s in range(spans)]
+        h_words = [sb("h_words%d" % n, [P, HALF], U32) for n in range(S // HALF)]
+        h_sc = [sb("h_sc%d" % n, [P, HALF], U8) for n in range(S // HALF)]
         y_sc = sb("y_sc", [P, GROUPS, S], U8)
+        y_words = sb("y_words", [P, GROUPS, S], U32)
         y_tiles = {}
         y_bf = {}
-
         d_acc = {}
+        free_banks = list(range(AHEAD, CHUNKS))
+
+        def background(c, start, stop):
+            for a in range(PASSES):
+                first_stage(
+                    d_acc[c], c, a, wb[:, a, :], FP4X4, 2 * P, plane[a][:, WB_SC : WB_SC + H],
+                    start and a == 0, stop and a == PASSES - 1,
+                )
+
+        def signal(c, a, start, stop):
+            first_stage(d_acc[c], c, a, ws_words[a][:], FP8X4, P, ws_sc[a][:], start, stop)
 
         def excess_open(c):
             d_acc[c] = bank(c % AHEAD)
-            for a in range(PASSES):
-                first_stage(d_acc[c], c, a, wb[:, a, :], FP4X4, 2 * P, plane[a][:, WB_SC : WB_SC + H], a == 0, False)
-            first_stage(d_acc[c], c, 0, ws_words[0][:], FP8X4, P, ws_sc[0][:], False, False)
+            background(c, True, False)
+            signal(c, 0, False, False)
 
         def excess(c):
-            s = max(n for n in range(spans) if chunks_of[n][0] <= c)
-            i = c - chunks_of[s][0]
-            if c not in d_acc:
-                excess_open(c)
-            acc = d_acc[c]
-            first_stage(acc, c, 1, ws_words[1][:], FP8X4, P, ws_sc[1][:], False, True)
+            s, i = divmod(c * CHUNK, span_w)
+            if c in d_acc:
+                signal(c, 1, False, True)
+            else:
+                d_acc[c] = bank(c % AHEAD)
+                signal(c, 1, True, False)
+                signal(c, 0, False, False)
+                background(c, False, True)
             nc.vector.scalar_tensor_tensor(
-                out=h_bf[s][:, i * CHUNK : (i + 1) * CHUNK, :],
-                in0=hit_major(acc),
+                out=h_bf[s][:, i : i + CHUNK, :],
+                in0=hit_major(d_acc[c]),
                 scalar=-1.0,
                 in1=inv_noise[c][:],
                 op0=ALU.mult,
@@ -215,17 +226,22 @@ def tile_list_hit_significance_tagging_kernel(
             )
 
         def quantize_h(s):
+            n, o = divmod(s * span_w, HALF)
             nc.vector.quantize_mx(
-                out=h_words[s][:].bitcast(FP8X4), scales=h_sc[s][:], in_=h_bf[s][:].rearrange("p j t -> p (j t)")
+                out=h_words[n][:, o : o + span_w].bitcast(FP8X4),
+                scales=h_sc[n][:, o : o + span_w],
+                in_=h_bf[s][:].rearrange("p j t -> p (j t)"),
             )
 
-        def features(s, g):
-            w = SPANS[s]
-            cols = slice(first[s], first[s] + w)
+        def features(s, g, w):
+            n, o = divmod(s * span_w, HALF)
+            cols = slice(s * span_w, s * span_w + w)
             y = sb("y%d_%d" % (s, g), [P, PACK, w], F32)
             per_bank = BANK // w
-            for n, b in enumerate(unit_banks[s, g]):
-                t0 = n * per_bank
+            rows_out = out_0[512 * g : 512 * (g + 1), cols].rearrange("(p t) j -> p t j", t=PACK)
+            for t0 in range(0, PACK, per_bank):
+                b = free_banks.pop(0)
+                free_banks.append(b)
                 acc = bank(b)
                 for u in range(per_bank):
                     t = t0 + u
@@ -233,8 +249,8 @@ def tile_list_hit_significance_tagging_kernel(
                         out=acc[:, u * w : (u + 1) * w],
                         lhsT=wt_words[g][:, t * P : (t + 1) * P].bitcast(FP8X4),
                         lhsT_scale=wt_sc[g][:, t * P : (t + 1) * P],
-                        rhs=h_words[s][:].bitcast(FP8X4),
-                        rhs_scale=h_sc[s][:],
+                        rhs=h_words[n][:, o : o + w].bitcast(FP8X4),
+                        rhs_scale=h_sc[n][:, o : o + w],
                         start=True,
                         stop=True,
                     )
@@ -245,63 +261,80 @@ def tile_list_hit_significance_tagging_kernel(
                     )
                 done = t0 + per_bank
                 if done % 2 == 0:
-                    rows_out = out_0[512 * g : 512 * (g + 1), cols].rearrange("(p t) j -> p t j", t=PACK)
                     nc.sync.dma_start(out=rows_out[:, done - 2 : done, :], in_=y[:, done - 2 : done, :])
-            y_tiles[s, g] = y
+            for i in range(w // span_w):
+                y_tiles[s + i, g] = y[:, :, i * span_w : (i + 1) * span_w]
 
-        y_words = {}
-
-        def round_y(s, g, o):
-            y_bf[s, g, o] = sb("y_bf%d_%d_%d" % (s, g, o), [P, SPANS[s], PACK], BF16)
-            nc.vector.tensor_copy(
-                y_bf[s, g, o][:].rearrange("p (c i) t -> p c t i", i=4),
-                y_tiles[s, g][:].rearrange("p t (c i) -> p c t i", i=4),
+        def round_y(s, g, cols=slice(0, span_w), copy=nc.vector.tensor_copy):
+            if (s, g) not in y_bf:
+                y_bf[s, g] = sb("y_bf%d_%d" % (s, g), [P, span_w, PACK], BF16)
+            copy(
+                y_bf[s, g][:, cols, :].rearrange("p (c i) t -> p c t i", i=4),
+                y_tiles[s, g][:, :, cols].rearrange("p t (c i) -> p c t i", i=4),
             )
 
-        def quantize_y(s, g, o):
-            if s == 0:
-                y_words[g] = sb("y_words%d" % g, [P, S], U32)
+        def quantize_y(s, g):
+            cols = slice(s * span_w, (s + 1) * span_w)
             nc.vector.quantize_mx(
-                out=y_words[g][:, first[s] : first[s] + SPANS[s]].bitcast(FP8X4),
-                scales=y_sc[:, g, first[s] : first[s] + SPANS[s]],
-                in_=y_bf[s, g, o][:].rearrange("p j t -> p (j t)"),
+                out=y_words[:, g, cols].bitcast(FP8X4),
+                scales=y_sc[:, g, cols],
+                in_=y_bf[s, g][:].rearrange("p j t -> p (j t)"),
             )
-            if s == spans - 1:
-                cols = slice(0, S)
-                nc.sync.dma_start(
-                    out=out_1[g].rearrange("p m t -> p (m t)").bitcast(I32)[:, cols], in_=y_words[g][:].bitcast(I32)
-                )
 
-        for c in chunks_of[0]:
-            excess_open(c)
-        round_wt(0, 0, nc.scalar.copy)
-        round_wt(0, 1, nc.vector.tensor_copy)
-        for c in chunks_of[0]:
-            excess(c)
-        quantize_wt(0)
-        quantize_h(0)
+        def store_words(cols):
+            nc.sync.dma_start(
+                out=out_1.rearrange("g p m t -> p g (m t)").bitcast(I32)[:, :, cols], in_=y_words[:, :, cols].bitcast(I32)
+            )
+
         for c in range(CHUNKS // 2, CHUNKS):
             noise(c, 1)
-        for s in range(spans):
-            ahead = chunks_of[s + 1] if s + 1 < spans else []
-            features(s, 0)
-            if s == 0:
-                round_wt(1, 0, nc.scalar.copy)
-                round_wt(1, 1, nc.scalar.copy)
-                quantize_wt(1)
-            for c in ahead:
-                excess(c)
-            if ahead:
-                quantize_h(s + 1)
-            features(s, 1)
-        units = [(s, g, o) for s in range(spans) for g in range(GROUPS) for o in range(1)]
+        for c in range(3):
+            excess_open(c)
+        round_wt(0, 0, nc.scalar.copy)
+        round_wt(0, 1, nc.scalar.copy)
+        excess(0)
+        excess(1)
+        quantize_h(0)
+        quantize_wt(0)
+        excess(2)
+        excess(3)
+        features(0, 0, 256)
+        quantize_h(1)
+        round_wt(1, 0, nc.scalar.copy)
+        round_wt(1, 1, nc.vector.tensor_copy)
+        quantize_wt(1)
+        excess(4)
+        features(1, 0, 256)
+        excess(5)
+        quantize_h(2)
+        excess(6)
+        features(0, 1, 512)
+        excess(7)
+        quantize_h(3)
+        features(2, 0, 256)
+        features(2, 1, 256)
+        features(3, 0, 256)
+        features(3, 1, 256)
+        units = [(0, 0), (1, 0), (0, 1), (1, 1), (2, 0), (2, 1), (3, 0), (3, 1)]
+        word_stores = {(1, 1): slice(0, 512), (2, 1): slice(512, 768), (3, 1): slice(768, S)}
+
+        def finish(unit):
+            quantize_y(*unit)
+            if unit in word_stores:
+                store_words(word_stores[unit])
+
         for i, unit in enumerate(units):
-            round_y(*unit)
+            if i == len(units) - 1:
+                round_y(*unit, cols=slice(0, 128), copy=nc.scalar.copy)
+                round_y(*unit, cols=slice(128, 256))
+            else:
+                round_y(*unit)
             if i > 0:
-                quantize_y(*units[i - 1])
-        quantize_y(*units[-1])
-        for q in range(4):
+                finish(units[i - 1])
+        finish(units[-1])
+
+        for r in range(4):
             nc.scalar.dma_start(
-                out=out_2[:, 4 * q : 4 * q + 4, :].rearrange("g r m -> r g m").bitcast(I32),
-                in_=y_sc[32 * q : 32 * q + 4, :, :].bitcast(I32),
+                out=out_2[:, r:16:4, :].rearrange("g q m -> q g m").bitcast(I32),
+                in_=y_sc[r:P:32, :, :].bitcast(I32),
             )

@@ -47,67 +47,82 @@ def tile_list_hit_significance_tagging_kernel(
             return psum.tile([P, BANK], F32, name="bank%d" % b, tag="bank%d" % b)
 
         offsets = keep.tile([P, S // 16], U16, name="offsets")
-        nc.sync.dma_start(offsets[:], offs)
         rows = 16 * PASSES
         sc_window = sb("sc_window", [P, T], U8)
         nc.sync.dma_start(out=sc_window[0:rows, :].bitcast(I32), in_=tab_scales.rearrange("a q t -> (a q) t").bitcast(I32))
         nc.vector.memset(sc_window[32:64, :].bitcast(I32), 0)
         nc.vector.memset(sc_window[64:128, :].bitcast(I32), 0)
-        w_sc_raw = sb("w_sc_raw", [P, 2 * H], U8)
-        nc.sync.dma_start(out=w_sc_raw[0:rows, 0:H].bitcast(I32), in_=wq_scales.rearrange("a q c -> (a q) c").bitcast(I32))
-        nc.sync.dma_start(out=w_sc_raw[0:rows, H : 2 * H].bitcast(I32), in_=wb_scales.rearrange("a q c -> (a q) c").bitcast(I32))
-        nc.vector.memset(w_sc_raw[32:64, :].bitcast(I32), 0)
-        nc.vector.memset(w_sc_raw[64:128, :].bitcast(I32), 0)
+        nc.sync.dma_start(offsets[:], offs)
+        stage = sb("stage", [P, S + 2 * PASSES * H], U8)
+        for x, w_scales in enumerate((wq_scales, wb_scales)):
+            cols = slice(S + x * PASSES * H, S + (x + 1) * PASSES * H)
+            nc.sync.dma_start(
+                out=stage[0:16, cols].bitcast(I32).rearrange("q (a c) -> q a c", a=PASSES),
+                in_=w_scales.rearrange("a q c -> q a c").bitcast(I32),
+            )
 
         tab = []
-        wq_raw = sb("wq_raw", [P, PASSES, H], I32)
-        wb_raw = sb("wb_raw", [P, PASSES, 2 * H], U8)
+        wq_raw = [sb("wq_raw%d" % a, [P, H], I32) for a in range(PASSES)]
 
         def load_tab(a, tag):
             tab.append(sb("tab%d" % a, [P, T], I32, tag=tag))
             nc.sync.dma_start(out=tab[a][:], in_=tab_words[a].rearrange("p t i -> p (t i)").bitcast(I32))
 
         load_tab(0, "tab0")
-        nc.sync.dma_start(out=wq_raw[:], in_=wq_words.rearrange("a p c i -> p a (c i)").bitcast(I32))
-        nc.sync.dma_start(out=wb_raw[:].bitcast(I32), in_=wb_words.rearrange("a p c -> p a c").bitcast(I32))
+        for a in range(PASSES):
+            nc.sync.dma_start(out=wq_raw[a][:], in_=wq_words[a].rearrange("p c i -> p (c i)").bitcast(I32))
 
-        plane = [sb("plane%d" % a, [P, PLANE], U8) for a in range(PASSES)]
+        widths = [S + 2 * PASSES * H, S]
+        plane = [sb("plane%d" % a, [P, widths[a]], U8) for a in range(PASSES)]
         for a in range(PASSES):
             nc.gpsimd.memset(plane[a][:].bitcast(I32), 0)
-        stage = sb("stage", [P, PLANE], U8)
         sc_picked = sb("sc_picked", [P, S], U8)
         nc.vector.tensor_copy(sc_picked[:], sc_window[:].indirect(offsets[:]))
-        nc.vector.tensor_copy(
-            stage[:, WQ_SC:PLANE].rearrange("p (x t c i) -> p x c t i", x=2, t=PACK, i=16),
-            w_sc_raw[:].rearrange("p (x c i t) -> p x c t i", x=2, t=PACK, i=16),
-        )
-        nc.vector.tensor_copy(stage[0:rows, V_SC : V_SC + S].bitcast(I32), sc_picked[0:rows, :].bitcast(I32))
+        nc.vector.tensor_copy(stage[0:rows, 0:S].bitcast(I32), sc_picked[0:rows, :].bitcast(I32))
 
         def carry(a):
             for r in range(4):
                 nc.sync.dma_start(
-                    out=plane[a][r:P:32, :].bitcast(I32), in_=stage[16 * a + r : 16 * (a + 1) : 4, :].bitcast(I32)
+                    out=plane[a][r:P:32, :].bitcast(I32),
+                    in_=stage[16 * a + r : 16 * (a + 1) : 4, 0 : widths[a]].bitcast(I32),
                 )
 
         carry(0)
         load_tab(1, "sc_picked")
         carry(1)
 
-        v = [[sb("v%d_%d" % (a, h), [P, HALF], U32) for h in range(S // HALF)] for a in range(PASSES)]
+        v = [[None] * (S // HALF) for a in range(PASSES)]
 
-        def gather(a, h):
+        def gather(a, h, tag=None):
+            v[a][h] = sb("v%d_%d" % (a, h), [P, HALF], U32, tag=tag)
             cols = slice(h * HALF // 16, (h + 1) * HALF // 16)
             nc.vector.tensor_copy(v[a][h][:], tab[a][:].bitcast(U32).indirect(offsets[:, cols]))
 
-        gather(0, 0)
         wq = sb("wq", [P, PASSES, H], I32)
-        nc.vector.tensor_copy(
-            wq[:].rearrange("p a (t c i) -> p a c t i", t=PACK, i=4),
-            wq_raw[:].rearrange("p a (c i t) -> p a c t i", t=PACK, i=4),
-        )
+        wq_sc = sb("wq_sc", [P, PASSES * H], U8)
+        wb_sc = sb("wb_sc", [P, PASSES * H], U8)
+
+        def deal_scales(dst, first, count):
+            nc.vector.tensor_copy(
+                dst.rearrange("p (x t c i) -> p x c t i", x=count, t=PACK, i=16),
+                plane[0][:, first : first + count * H].rearrange("p (x c i t) -> p x c t i", x=count, t=PACK, i=16),
+            )
+
+        gather(0, 0)
+        for a in range(PASSES):
+            nc.vector.tensor_copy(
+                wq[:, a, :].rearrange("p (t c i) -> p c t i", t=PACK, i=4),
+                wq_raw[a][:].rearrange("p (c i t) -> p c t i", t=PACK, i=4),
+            )
+        wb_raw = sb("wb_raw", [P, PASSES, 2 * H], U8, tag="wq_raw0")
+        nc.sync.dma_start(out=wb_raw[:].bitcast(I32), in_=wb_words.rearrange("a p c -> p a c").bitcast(I32))
+        for a in range(PASSES):
+            deal_scales(wq_sc[:, a * H : (a + 1) * H], S + a * H, 1)
+        gather(0, 1)
+        deal_scales(wb_sc[:], S + PASSES * H, PASSES)
         ws_rows = ws.rearrange("(a p j) c -> a p j c", a=PASSES, j=PACK)
         wt_rows = wt.rearrange("(p j) (g n) -> g p j n", j=PACK, g=GROUPS)
-        w_raw = sb("w_raw", [P, (PASSES + GROUPS) * PACK * 512 + GROUPS * 8], F32, tag="wq_raw")
+        w_raw = sb("w_raw", [P, (PASSES + GROUPS) * PACK * 512 + GROUPS * 8], F32, tag="wq_raw1")
         bias = w_raw[:, (PASSES + GROUPS) * PACK * 512 :].rearrange("p (g t) -> p g t", g=GROUPS)
         nc.sync.dma_start(out=bias[:, :, 0:PACK], in_=bt.rearrange("(g p t) -> p g t", g=GROUPS, t=PACK))
         raws = []
@@ -116,7 +131,6 @@ def tile_list_hit_significance_tagging_kernel(
             nc.sync.dma_start(out=raw, in_=src)
             raws.append(raw)
         ws_raw, wt_raw = raws[:PASSES], raws[PASSES:]
-        gather(0, 1)
         gather(1, 0)
         gather(1, 1)
         wb = sb("wb", [P, PASSES, 2 * H], U8)
@@ -146,7 +160,7 @@ def tile_list_hit_significance_tagging_kernel(
         inv_noise = [sb("inv_noise%d" % c, [P, CHUNK, PACK], F32) for c in range(CHUNKS)]
 
         def noise(c, a):
-            first_stage(q_acc[c], c, a, wq[:, a, :], FP8X4, P, plane[a][:, WQ_SC : WQ_SC + H], a == 0, a == PASSES - 1)
+            first_stage(q_acc[c], c, a, wq[:, a, :], FP8X4, P, wq_sc[:, a * H : (a + 1) * H], a == 0, a == PASSES - 1)
             if a == PASSES - 1:
                 nc.scalar.activation(out=inv_noise[c][:], in_=hit_major(q_acc[c]), func=ACT.Exp, scale=-1.0)
 
@@ -195,7 +209,7 @@ def tile_list_hit_significance_tagging_kernel(
         def background(c, start, stop):
             for a in range(PASSES):
                 first_stage(
-                    d_acc[c], c, a, wb[:, a, :], FP4X4, 2 * P, plane[a][:, WB_SC : WB_SC + H],
+                    d_acc[c], c, a, wb[:, a, :], FP4X4, 2 * P, wb_sc[:, a * H : (a + 1) * H],
                     start and a == 0, stop and a == PASSES - 1,
                 )
 
@@ -212,7 +226,7 @@ def tile_list_hit_significance_tagging_kernel(
             if c in d_acc:
                 signal(c, 1, False, True)
             else:
-                d_acc[c] = bank(c % AHEAD)
+                d_acc[c] = bank([0, 3, 1, 2][c - AHEAD])
                 signal(c, 1, True, False)
                 signal(c, 0, False, False)
                 background(c, False, True)
@@ -260,8 +274,9 @@ def tile_list_hit_significance_tagging_kernel(
                         out=y[:, t, :], in_=acc[:, u * w : (u + 1) * w], func=ACT.Identity, bias=bias[:, g, t : t + 1]
                     )
                 done = t0 + per_bank
-                if done % 2 == 0:
-                    nc.sync.dma_start(out=rows_out[:, done - 2 : done, :], in_=y[:, done - 2 : done, :])
+                step = 2 if w > span_w or (s, g) in ((0, 0), (spans - 1, GROUPS - 1)) else PACK
+                if done % step == 0:
+                    nc.sync.dma_start(out=rows_out[:, done - step : done, :], in_=y[:, done - step : done, :])
             for i in range(w // span_w):
                 y_tiles[s + i, g] = y[:, :, i * span_w : (i + 1) * span_w]
 
@@ -288,14 +303,14 @@ def tile_list_hit_significance_tagging_kernel(
 
         for c in range(CHUNKS // 2, CHUNKS):
             noise(c, 1)
-        for c in range(3):
+        for c in range(4):
             excess_open(c)
         round_wt(0, 0, nc.scalar.copy)
-        round_wt(0, 1, nc.scalar.copy)
+        round_wt(0, 1, nc.vector.tensor_copy)
         excess(0)
         excess(1)
-        quantize_h(0)
         quantize_wt(0)
+        quantize_h(0)
         excess(2)
         excess(3)
         features(0, 0, 256)

@@ -181,8 +181,17 @@ def tile_list_hit_significance_tagging_kernel(
         for a in range(PASSES):
             ws_bf = sb("ws_bf%d" % a, [P, H * PACK], BF16)
             dst, src = dealt(ws_bf, slice(0, 512), ws_raw[a])
-            nc.vector.tensor_scalar(out=dst, in0=src, scalar1=-1.0, scalar2=None, op0=ALU.mult)
-            nc.vector.quantize_mx(out=ws_words[a][:].bitcast(FP8X4), scales=ws_sc[a][:], in_=ws_bf[:])
+            for t0 in (0, 2):
+                nc.vector.tensor_scalar(
+                    out=dst[:, :, :, t0 : t0 + 2], in0=src[:, :, :, t0 : t0 + 2], scalar1=-1.0, scalar2=None, op0=ALU.mult
+                )
+            for t0 in (0, 2):
+                cols = slice(t0 * P, (t0 + 2) * P)
+                nc.vector.quantize_mx(
+                    out=ws_words[a][:, cols].bitcast(FP8X4),
+                    scales=ws_sc[a][:, cols],
+                    in_=ws_bf[:, t0 * P * PACK : (t0 + 2) * P * PACK],
+                )
 
         wt_words = [sb("wt_words%d" % g, [P, 512], U32) for g in range(GROUPS)]
         wt_sc = [sb("wt_sc%d" % g, [P, 512], U8) for g in range(GROUPS)]
@@ -239,12 +248,13 @@ def tile_list_hit_significance_tagging_kernel(
                 op1=ALU.mult,
             )
 
-        def quantize_h(s):
-            n, o = divmod(s * span_w, HALF)
+        def quantize_h(c):
+            n, o = divmod(c * CHUNK, HALF)
+            s, i = divmod(c * CHUNK, span_w)
             nc.vector.quantize_mx(
-                out=h_words[n][:, o : o + span_w].bitcast(FP8X4),
-                scales=h_sc[n][:, o : o + span_w],
-                in_=h_bf[s][:].rearrange("p j t -> p (j t)"),
+                out=h_words[n][:, o : o + CHUNK].bitcast(FP8X4),
+                scales=h_sc[n][:, o : o + CHUNK],
+                in_=h_bf[s][:, i : i + CHUNK, :].rearrange("p j t -> p (j t)"),
             )
 
         def features(s, g, w):
@@ -309,23 +319,27 @@ def tile_list_hit_significance_tagging_kernel(
         round_wt(0, 1, nc.vector.tensor_copy)
         excess(0)
         excess(1)
-        quantize_wt(0)
         quantize_h(0)
+        quantize_wt(0)
+        quantize_h(1)
         excess(2)
         excess(3)
         features(0, 0, 256)
-        quantize_h(1)
+        quantize_h(2)
         round_wt(1, 0, nc.scalar.copy)
         round_wt(1, 1, nc.vector.tensor_copy)
+        quantize_h(3)
         quantize_wt(1)
         excess(4)
         features(1, 0, 256)
         excess(5)
-        quantize_h(2)
+        quantize_h(4)
         excess(6)
+        quantize_h(5)
         features(0, 1, 512)
         excess(7)
-        quantize_h(3)
+        quantize_h(6)
+        quantize_h(7)
         features(2, 0, 256)
         features(2, 1, 256)
         features(3, 0, 256)
@@ -339,7 +353,9 @@ def tile_list_hit_significance_tagging_kernel(
                 store_words(word_stores[unit])
 
         for i, unit in enumerate(units):
-            if i == len(units) - 1:
+            if i == len(units) - 2:
+                round_y(*unit, copy=nc.scalar.copy)
+            elif i == len(units) - 1:
                 round_y(*unit, cols=slice(0, 128), copy=nc.scalar.copy)
                 round_y(*unit, cols=slice(128, 256))
             else:

@@ -28,8 +28,7 @@ SPANS = [256, 256, 256, 256]
 PARTS = [slice(0, 256), slice(256, 512)]
 PIECE = 256
 AHEAD = 4
-V_SC, WQ_SC, WB_SC = 0, S, S + H
-PLANE = S + 2 * H
+WQ_SC, WB_SC = HALF, HALF + H
 
 
 def tile_list_hit_significance_tagging_kernel(
@@ -49,46 +48,60 @@ def tile_list_hit_significance_tagging_kernel(
         offsets = keep.tile([P, S // 16], U16, name="offsets")
         rows = 16 * PASSES
         sc_window = sb("sc_window", [P, T], U8)
-        nc.sync.dma_start(out=sc_window[0:rows, :].bitcast(I32), in_=tab_scales.rearrange("a q t -> (a q) t").bitcast(I32))
+        nc.sync.dma_start(out=sc_window[0:rows, :].bitcast(I32), in_=tab_scales.rearrange("a q t -> q a t").bitcast(I32))
         nc.vector.memset(sc_window[32:64, :].bitcast(I32), 0)
         nc.vector.memset(sc_window[64:128, :].bitcast(I32), 0)
         nc.sync.dma_start(offsets[:], offs)
-        stage = sb("stage", [P, S + 2 * PASSES * H], U8)
-        for x, w_scales in enumerate((wq_scales, wb_scales)):
-            cols = slice(S + x * PASSES * H, S + (x + 1) * PASSES * H)
+        widths = [HALF + 2 * H, HALF]
+        stage = [sb("stage%d" % h, [P, widths[h]], U8) for h in range(2)]
+        for first, w_scales in ((WQ_SC, wq_scales), (WB_SC, wb_scales)):
             nc.sync.dma_start(
-                out=stage[0:16, cols].bitcast(I32).rearrange("q (a c) -> q a c", a=PASSES),
+                out=stage[0][0:rows, first : first + H].bitcast(I32),
                 in_=w_scales.rearrange("a q c -> q a c").bitcast(I32),
             )
 
         tab = []
-        wq_raw = [sb("wq_raw%d" % a, [P, H], I32) for a in range(PASSES)]
 
         def load_tab(a, tag):
             tab.append(sb("tab%d" % a, [P, T], I32, tag=tag))
             nc.sync.dma_start(out=tab[a][:], in_=tab_words[a].rearrange("p t i -> p (t i)").bitcast(I32))
 
-        load_tab(0, "tab0")
-        for a in range(PASSES):
+        wq_raw = []
+        wb_raw = []
+
+        def load_wq(a, tag):
+            wq_raw.append(sb("wq_raw%d" % a, [P, H], I32, tag=tag))
             nc.sync.dma_start(out=wq_raw[a][:], in_=wq_words[a].rearrange("p c i -> p (c i)").bitcast(I32))
 
-        widths = [S + 2 * PASSES * H, S]
-        plane = [sb("plane%d" % a, [P, widths[a]], U8) for a in range(PASSES)]
-        for a in range(PASSES):
-            nc.gpsimd.memset(plane[a][:].bitcast(I32), 0)
-        sc_picked = sb("sc_picked", [P, S], U8)
-        nc.vector.tensor_copy(sc_picked[:], sc_window[:].indirect(offsets[:]))
-        nc.vector.tensor_copy(stage[0:rows, 0:S].bitcast(I32), sc_picked[0:rows, :].bitcast(I32))
+        def load_wb(a, tag):
+            wb_raw.append(sb("wb_raw%d" % a, [P, H // 2], I32, tag=tag))
+            nc.sync.dma_start(out=wb_raw[a][:], in_=wb_words[a].bitcast(I32))
 
-        def carry(a):
-            for r in range(4):
+        load_tab(0, "tab0")
+        load_wq(0, "wq_raw0")
+        load_wb(0, "wb_raw0")
+
+        planes = [sb("planes%d" % h, [P, PASSES * widths[h]], U8) for h in range(2)]
+        for h in range(2):
+            nc.gpsimd.memset(planes[h][:].bitcast(I32), 0)
+
+        def pick_scales(h):
+            picked = sb("sc_picked%d" % h, [P, HALF], U8, tag="sc_picked")
+            cols = slice(h * HALF // 16, (h + 1) * HALF // 16)
+            nc.vector.tensor_copy(picked[:], sc_window[:].indirect(offsets[:, cols]))
+            nc.vector.tensor_copy(stage[h][0:rows, 0:HALF].bitcast(I32), picked[0:rows, :].bitcast(I32))
+
+        def carry(h):
+            for quad in (0, 2, 1, 3):
                 nc.sync.dma_start(
-                    out=plane[a][r:P:32, :].bitcast(I32),
-                    in_=stage[16 * a + r : 16 * (a + 1) : 4, 0 : widths[a]].bitcast(I32),
+                    out=planes[h][32 * quad : 32 * quad + 4, :].bitcast(I32),
+                    in_=stage[h][8 * quad : 8 * quad + 8, :].bitcast(I32),
                 )
 
+        pick_scales(0)
         carry(0)
-        load_tab(1, "sc_picked")
+        pick_scales(1)
+        load_tab(1, "sc_window")
         carry(1)
 
         v = [[None] * (S // HALF) for a in range(PASSES)]
@@ -99,46 +112,51 @@ def tile_list_hit_significance_tagging_kernel(
             nc.vector.tensor_copy(v[a][h][:], tab[a][:].bitcast(U32).indirect(offsets[:, cols]))
 
         wq = sb("wq", [P, PASSES, H], I32)
-        wq_sc = sb("wq_sc", [P, PASSES * H], U8)
-        wb_sc = sb("wb_sc", [P, PASSES * H], U8)
+        wb = sb("wb", [P, PASSES, 2 * H], U8)
+        w_sc = sb("w_sc", [P, PASSES, 2 * H], U8)
 
-        def deal_scales(dst, first, count):
-            nc.vector.tensor_copy(
-                dst.rearrange("p (x t c i) -> p x c t i", x=count, t=PACK, i=16),
-                plane[0][:, first : first + count * H].rearrange("p (x c i t) -> p x c t i", x=count, t=PACK, i=16),
-            )
-
-        gather(0, 0)
-        for a in range(PASSES):
+        def deal_wq(a):
             nc.vector.tensor_copy(
                 wq[:, a, :].rearrange("p (t c i) -> p c t i", t=PACK, i=4),
                 wq_raw[a][:].rearrange("p (c i t) -> p c t i", t=PACK, i=4),
             )
-        wb_raw = sb("wb_raw", [P, PASSES, 2 * H], U8, tag="wq_raw0")
-        nc.sync.dma_start(out=wb_raw[:].bitcast(I32), in_=wb_words.rearrange("a p c -> p a c").bitcast(I32))
-        for a in range(PASSES):
-            deal_scales(wq_sc[:, a * H : (a + 1) * H], S + a * H, 1)
+
+        def deal_wb(a):
+            nc.vector.tensor_copy(
+                wb[:, a, :].bitcast(U16).rearrange("p (t c i) -> p c t i", t=PACK, i=8),
+                wb_raw[a][:].bitcast(U16).rearrange("p (c i t) -> p c t i", t=PACK, i=8),
+            )
+
+        gather(0, 0)
         gather(0, 1)
-        deal_scales(wb_sc[:], S + PASSES * H, PASSES)
+        deal_wq(0)
+        deal_wb(0)
+        for a in range(PASSES):
+            first = a * widths[0]
+            nc.vector.tensor_copy(
+                w_sc[:, a, :].rearrange("p (x t c i) -> p x c t i", x=2, t=PACK, i=16),
+                planes[0][:, first + WQ_SC : first + widths[0]].rearrange("p (x c i t) -> p x c t i", x=2, t=PACK, i=16),
+            )
+        load_wq(1, "sc_picked")
+        load_wb(1, "tab0")
         ws_rows = ws.rearrange("(a p j) c -> a p j c", a=PASSES, j=PACK)
         wt_rows = wt.rearrange("(p j) (g n) -> g p j n", j=PACK, g=GROUPS)
-        w_raw = sb("w_raw", [P, (PASSES + GROUPS) * PACK * 512 + GROUPS * 8], F32, tag="wq_raw1")
-        bias = w_raw[:, (PASSES + GROUPS) * PACK * 512 :].rearrange("p (g t) -> p g t", g=GROUPS)
-        nc.sync.dma_start(out=bias[:, :, 0:PACK], in_=bt.rearrange("(g p t) -> p g t", g=GROUPS, t=PACK))
-        raws = []
-        for n, src in enumerate((ws_rows[0], ws_rows[1], wt_rows[0], wt_rows[1])):
-            raw = w_raw[:, PACK * 512 * n : PACK * 512 * (n + 1)].rearrange("p (j c) -> p j c", j=PACK)
-            nc.sync.dma_start(out=raw, in_=src)
-            raws.append(raw)
-        ws_raw, wt_raw = raws[:PASSES], raws[PASSES:]
+        ws_raw = []
+        for a, tag in enumerate(("wq_raw0", "wb_raw0")):
+            ws_raw.append(sb("ws_raw%d" % a, [P, PACK, H], F32, tag=tag))
+            nc.sync.dma_start(out=ws_raw[a][:], in_=ws_rows[a])
+        w_raw = sb("w_raw", [P, GROUPS * PACK * 512 + GROUPS * 8], F32, tag="stage1")
+        bias = w_raw[:, GROUPS * PACK * 512 :].rearrange("p (g t) -> p g t", g=GROUPS)
+        wt_raw = []
+        for g in range(GROUPS):
+            wt_raw.append(w_raw[:, PACK * 512 * g : PACK * 512 * (g + 1)].rearrange("p (j c) -> p j c", j=PACK))
+            nc.sync.dma_start(out=wt_raw[g], in_=wt_rows[g])
+            if g == 0:
+                nc.sync.dma_start(out=bias[:, :, 0:PACK], in_=bt.rearrange("(g p t) -> p g t", g=GROUPS, t=PACK))
         gather(1, 0)
-        gather(1, 1)
-        wb = sb("wb", [P, PASSES, 2 * H], U8)
-        for a in range(PASSES):
-            nc.vector.tensor_copy(
-                wb[:, a, :].rearrange("p (t c i e) -> p c t i e", t=PACK, i=8, e=2),
-                wb_raw[:, a, :].rearrange("p (c i t e) -> p c t i e", t=PACK, i=8, e=2),
-            )
+        deal_wq(1)
+        gather(1, 1, tag="sc_picked")
+        deal_wb(1)
 
         def first_stage(acc, c, a, words, dtype, width, scales, start, stop):
             h, o = divmod(c * CHUNK, HALF)
@@ -148,7 +166,7 @@ def tile_list_hit_significance_tagging_kernel(
                     lhsT=words[:, t * width : (t + 1) * width].bitcast(dtype),
                     lhsT_scale=scales[:, t * P : (t + 1) * P],
                     rhs=v[a][h][:, o : o + CHUNK].bitcast(FP8X4),
-                    rhs_scale=plane[a][:, V_SC + c * CHUNK : V_SC + (c + 1) * CHUNK],
+                    rhs_scale=planes[h][:, a * widths[h] + o : a * widths[h] + o + CHUNK],
                     start=start and t == 0,
                     stop=stop and t == PACK - 1,
                 )
@@ -156,94 +174,96 @@ def tile_list_hit_significance_tagging_kernel(
         def hit_major(acc):
             return acc[:].rearrange("p (t j) -> p j t", t=PACK)
 
-        q_acc = [bank(c) for c in range(CHUNKS)]
-        inv_noise = [sb("inv_noise%d" % c, [P, CHUNK, PACK], F32) for c in range(CHUNKS)]
+        q_acc = {}
+        inv_noise = {}
+        q_banks = [0, 1, 2, 3, 0, 1, 4, 5]
+        d_banks = [4, 5, 6, 7, 0, 1, 6, 7]
 
         def noise(c, a):
-            first_stage(q_acc[c], c, a, wq[:, a, :], FP8X4, P, wq_sc[:, a * H : (a + 1) * H], a == 0, a == PASSES - 1)
+            if a == 0:
+                q_acc[c] = bank(q_banks[c])
+            first_stage(q_acc[c], c, a, wq[:, a, :], FP8X4, P, w_sc[:, a, 0:H], a == 0, a == PASSES - 1)
             if a == PASSES - 1:
-                nc.scalar.activation(out=inv_noise[c][:], in_=hit_major(q_acc[c]), func=ACT.Exp, scale=-1.0)
+                if c // 2 not in inv_noise:
+                    inv_noise[c // 2] = sb(
+                        "inv_noise%d" % (c // 2), [P, 2, CHUNK, PACK], F32, tag="wb_raw0" if c == AHEAD else None
+                    )
+                nc.scalar.activation(out=inv_noise[c // 2][:, c % 2], in_=hit_major(q_acc[c]), func=ACT.Exp, scale=-1.0)
 
-        for c in range(CHUNKS):
-            noise(c, 0)
-        for c in range(CHUNKS // 2):
-            noise(c, 1)
-
-        def dealt(rounded, part, raw):
-            ms = slice(part.start // PACK, part.stop // PACK)
+        def dealt(rounded, raw, u):
             return (
-                rounded[:].rearrange("p (t m j) -> p m j t", t=PACK, j=PACK)[:, ms, :, :],
-                raw.rearrange("p j (m t) -> p m j t", t=PACK)[:, ms, :, :],
+                rounded[:].rearrange("p (t m j) -> p m j t", t=2, j=PACK),
+                raw.rearrange("p j (m t) -> p m j t", t=PACK)[:, :, :, 2 * u : 2 * u + 2],
             )
+
+        def quantize_pair(words, scales, rounded, u):
+            cols = slice(2 * u * P, (2 * u + 2) * P)
+            nc.vector.quantize_mx(out=words[:, cols].bitcast(FP8X4), scales=scales[:, cols], in_=rounded[:])
 
         ws_words = [sb("ws_words%d" % a, [P, H], U32) for a in range(PASSES)]
         ws_sc = [sb("ws_sc%d" % a, [P, H], U8) for a in range(PASSES)]
-        for a in range(PASSES):
-            ws_bf = sb("ws_bf%d" % a, [P, H * PACK], BF16)
-            dst, src = dealt(ws_bf, slice(0, 512), ws_raw[a])
-            for t0 in (0, 2):
-                nc.vector.tensor_scalar(
-                    out=dst[:, :, :, t0 : t0 + 2], in0=src[:, :, :, t0 : t0 + 2], scalar1=-1.0, scalar2=None, op0=ALU.mult
-                )
-            for t0 in (0, 2):
-                cols = slice(t0 * P, (t0 + 2) * P)
-                nc.vector.quantize_mx(
-                    out=ws_words[a][:, cols].bitcast(FP8X4),
-                    scales=ws_sc[a][:, cols],
-                    in_=ws_bf[:, t0 * P * PACK : (t0 + 2) * P * PACK],
-                )
+        ws_bf = {}
+
+        def round_ws(a, u, on_scalar=False):
+            ws_bf[a, u] = sb("ws_bf%d_%d" % (a, u), [P, 2 * P * PACK], BF16)
+            dst, src = dealt(ws_bf[a, u], ws_raw[a][:], u)
+            if on_scalar:
+                nc.scalar.activation(out=dst, in_=src, func=ACT.Copy, scale=-1.0)
+            else:
+                nc.vector.tensor_scalar(out=dst, in0=src, scalar1=-1.0, scalar2=None, op0=ALU.mult)
+
+        def quantize_ws(a, u):
+            quantize_pair(ws_words[a], ws_sc[a], ws_bf[a, u], u)
 
         wt_words = [sb("wt_words%d" % g, [P, 512], U32) for g in range(GROUPS)]
         wt_sc = [sb("wt_sc%d" % g, [P, 512], U8) for g in range(GROUPS)]
-        wt_bf = [sb("wt_bf%d" % g, [P, 512 * PACK], BF16) for g in range(GROUPS)]
+        wt_bf = {}
 
-        def round_wt(g, part, copy):
-            copy(*dealt(wt_bf[g], PARTS[part], wt_raw[g]))
+        def round_wt(g, u, copy, tag=None):
+            wt_bf[g, u] = sb("wt_bf%d_%d" % (g, u), [P, 2 * P * PACK], BF16, tag=tag)
+            copy(*dealt(wt_bf[g, u], wt_raw[g], u))
 
-        def quantize_wt(g):
-            nc.vector.quantize_mx(out=wt_words[g][:].bitcast(FP8X4), scales=wt_sc[g][:], in_=wt_bf[g][:])
+        def quantize_wt(g, u):
+            quantize_pair(wt_words[g], wt_sc[g], wt_bf[g, u], u)
 
         span_w = 256
         spans = S // span_w
-        h_bf = [sb("h_bf%d" % s, [P, span_w, PACK], BF16) for s in range(spans)]
+        h_bf = {}
         h_words = [sb("h_words%d" % n, [P, HALF], U32) for n in range(S // HALF)]
         h_sc = [sb("h_sc%d" % n, [P, HALF], U8) for n in range(S // HALF)]
         y_sc = sb("y_sc", [P, GROUPS, S], U8)
         y_words = sb("y_words", [P, GROUPS, S], U32)
         y_tiles = {}
         y_bf = {}
+        y_bf_tags = ["wt_bf1_1", "h_bf2"] + ["inv_noise3", "h_bf3"] * 3
         d_acc = {}
-        free_banks = list(range(AHEAD, CHUNKS))
+        y_banks = [2, 3, 4, 5, 2, 3, 4, 5, 2, 3, 0, 1, 4, 5, 6, 7]
 
-        def background(c, start, stop):
-            for a in range(PASSES):
-                first_stage(
-                    d_acc[c], c, a, wb[:, a, :], FP4X4, 2 * P, wb_sc[:, a * H : (a + 1) * H],
-                    start and a == 0, stop and a == PASSES - 1,
-                )
+        def background(c, a, start, stop):
+            first_stage(d_acc[c], c, a, wb[:, a, :], FP4X4, 2 * P, w_sc[:, a, H : 2 * H], start, stop)
 
         def signal(c, a, start, stop):
             first_stage(d_acc[c], c, a, ws_words[a][:], FP8X4, P, ws_sc[a][:], start, stop)
 
-        def excess_open(c):
-            d_acc[c] = bank(c % AHEAD)
-            background(c, True, False)
-            signal(c, 0, False, False)
-
         def excess(c):
-            s, i = divmod(c * CHUNK, span_w)
-            if c in d_acc:
-                signal(c, 1, False, True)
-            else:
-                d_acc[c] = bank([0, 3, 1, 2][c - AHEAD])
+            if c not in d_acc:
+                d_acc[c] = bank(d_banks[c])
                 signal(c, 1, True, False)
                 signal(c, 0, False, False)
-                background(c, False, True)
+                background(c, 0, False, False)
+                background(c, 1, False, True)
+            else:
+                signal(c, 1, False, True)
+
+        def scale(c):
+            s, i = divmod(c * CHUNK, span_w)
+            if s not in h_bf:
+                h_bf[s] = sb("h_bf%d" % s, [P, span_w, PACK], BF16, tag="wt_bf0_0" if s == 1 else None)
             nc.vector.scalar_tensor_tensor(
                 out=h_bf[s][:, i : i + CHUNK, :],
                 in0=hit_major(d_acc[c]),
                 scalar=-1.0,
-                in1=inv_noise[c][:],
+                in1=inv_noise[c // 2][:, c % 2],
                 op0=ALU.mult,
                 op1=ALU.mult,
             )
@@ -264,9 +284,7 @@ def tile_list_hit_significance_tagging_kernel(
             per_bank = BANK // w
             rows_out = out_0[512 * g : 512 * (g + 1), cols].rearrange("(p t) j -> p t j", t=PACK)
             for t0 in range(0, PACK, per_bank):
-                b = free_banks.pop(0)
-                free_banks.append(b)
-                acc = bank(b)
+                acc = bank(y_banks.pop(0))
                 for u in range(per_bank):
                     t = t0 + u
                     nc.tensor.matmul_mx(
@@ -292,7 +310,7 @@ def tile_list_hit_significance_tagging_kernel(
 
         def round_y(s, g, cols=slice(0, span_w), copy=nc.vector.tensor_copy):
             if (s, g) not in y_bf:
-                y_bf[s, g] = sb("y_bf%d_%d" % (s, g), [P, span_w, PACK], BF16)
+                y_bf[s, g] = sb("y_bf%d_%d" % (s, g), [P, span_w, PACK], BF16, tag=y_bf_tags.pop(0))
             copy(
                 y_bf[s, g][:, cols, :].rearrange("p (c i) t -> p c t i", i=4),
                 y_tiles[s, g][:, :, cols].rearrange("p t (c i) -> p c t i", i=4),
@@ -311,33 +329,63 @@ def tile_list_hit_significance_tagging_kernel(
                 out=out_1.rearrange("g p m t -> p g (m t)").bitcast(I32)[:, :, cols], in_=y_words[:, :, cols].bitcast(I32)
             )
 
-        for c in range(CHUNKS // 2, CHUNKS):
+        for c in range(AHEAD):
+            noise(c, 0)
+        for c in range(AHEAD):
+            d_acc[c] = bank(d_banks[c])
+            background(c, 0, True, False)
+        for c in range(AHEAD):
             noise(c, 1)
-        for c in range(4):
-            excess_open(c)
+        for u in range(2):
+            round_ws(0, u)
+        for u in range(2):
+            quantize_ws(0, u)
+        round_ws(1, 0)
+        round_ws(1, 1, on_scalar=True)
+        for u in range(2):
+            quantize_ws(1, u)
+        for c in range(AHEAD):
+            background(c, 1, False, False)
+        for c in range(AHEAD):
+            signal(c, 0, False, False)
+        for c in range(2):
+            excess(c)
+            scale(c)
+        for c in (4, 5):
+            noise(c, 0)
+            noise(c, 1)
         round_wt(0, 0, nc.scalar.copy)
-        round_wt(0, 1, nc.vector.tensor_copy)
-        excess(0)
-        excess(1)
+        round_wt(0, 1, nc.scalar.copy)
         quantize_h(0)
-        quantize_wt(0)
+        quantize_wt(0, 0)
         quantize_h(1)
         excess(2)
+        scale(2)
+        quantize_wt(0, 1)
         excess(3)
+        scale(3)
+        for c in (6, 7):
+            noise(c, 0)
+            noise(c, 1)
         features(0, 0, 256)
         quantize_h(2)
-        round_wt(1, 0, nc.scalar.copy)
-        round_wt(1, 1, nc.vector.tensor_copy)
         quantize_h(3)
-        quantize_wt(1)
-        excess(4)
+        round_wt(1, 0, nc.vector.tensor_copy, tag="h_bf0")
+        round_wt(1, 1, nc.vector.tensor_copy)
+        quantize_wt(1, 0)
+        quantize_wt(1, 1)
+        for c in (4, 5):
+            excess(c)
+            scale(c)
         features(1, 0, 256)
-        excess(5)
-        quantize_h(4)
         excess(6)
-        quantize_h(5)
-        features(0, 1, 512)
+        features(0, 1, 256)
+        features(1, 1, 256)
         excess(7)
+        quantize_h(4)
+        quantize_h(5)
+        scale(6)
+        scale(7)
         quantize_h(6)
         quantize_h(7)
         features(2, 0, 256)
@@ -353,9 +401,7 @@ def tile_list_hit_significance_tagging_kernel(
                 store_words(word_stores[unit])
 
         for i, unit in enumerate(units):
-            if i == len(units) - 2:
-                round_y(*unit, copy=nc.scalar.copy)
-            elif i == len(units) - 1:
+            if i == len(units) - 1:
                 round_y(*unit, cols=slice(0, 128), copy=nc.scalar.copy)
                 round_y(*unit, cols=slice(128, 256))
             else:

@@ -48,15 +48,14 @@ def tile_list_hit_significance_tagging_kernel(
         offsets = keep.tile([P, S // 16], U16, name="offsets")
         rows = 16 * PASSES
         sc_window = sb("sc_window", [P, T], U8)
-        nc.sync.dma_start(out=sc_window[0:rows, :].bitcast(I32), in_=tab_scales.rearrange("a q t -> q a t").bitcast(I32))
-        nc.vector.memset(sc_window[32:64, :].bitcast(I32), 0)
-        nc.vector.memset(sc_window[64:128, :].bitcast(I32), 0)
+        nc.sync.dma_start(out=sc_window[P - rows : P, :].bitcast(I32), in_=tab_scales.rearrange("a q t -> q a t").bitcast(I32))
+        nc.vector.memset(sc_window[0 : P - rows, :].bitcast(I32), 0)
         nc.sync.dma_start(offsets[:], offs)
         widths = [HALF + 2 * H, HALF]
         stage = [sb("stage%d" % h, [P, widths[h]], U8) for h in range(2)]
         for first, w_scales in ((WQ_SC, wq_scales), (WB_SC, wb_scales)):
             nc.sync.dma_start(
-                out=stage[0][0:rows, first : first + H].bitcast(I32),
+                out=stage[0][P - rows : P, first : first + H].bitcast(I32),
                 in_=w_scales.rearrange("a q c -> q a c").bitcast(I32),
             )
 
@@ -81,21 +80,21 @@ def tile_list_hit_significance_tagging_kernel(
         load_wq(0, "wq_raw0")
         load_wb(0, "wb_raw0")
 
-        planes = [sb("planes%d" % h, [P, PASSES * widths[h]], U8) for h in range(2)]
-        for h in range(2):
-            nc.gpsimd.memset(planes[h][:].bitcast(I32), 0)
+        all_planes = sb("all_planes", [P, PASSES * sum(widths)], U8)
+        nc.vector.memset(all_planes[:].bitcast(I32), 0)
+        planes = [all_planes[:, 0 : PASSES * widths[0]], all_planes[:, PASSES * widths[0] :]]
 
         def pick_scales(h):
             picked = sb("sc_picked%d" % h, [P, HALF], U8, tag="sc_picked")
             cols = slice(h * HALF // 16, (h + 1) * HALF // 16)
             nc.vector.tensor_copy(picked[:], sc_window[:].indirect(offsets[:, cols]))
-            nc.vector.tensor_copy(stage[h][0:rows, 0:HALF].bitcast(I32), picked[0:rows, :].bitcast(I32))
+            nc.vector.tensor_copy(stage[h][P - rows : P, 0:HALF].bitcast(I32), picked[P - rows : P, :].bitcast(I32))
 
         def carry(h):
             for quad in (0, 2, 1, 3):
                 nc.sync.dma_start(
                     out=planes[h][32 * quad : 32 * quad + 4, :].bitcast(I32),
-                    in_=stage[h][8 * quad : 8 * quad + 8, :].bitcast(I32),
+                    in_=stage[h][P - rows + 8 * quad : P - rows + 8 * quad + 8, :].bitcast(I32),
                 )
 
         pick_scales(0)
@@ -235,7 +234,7 @@ def tile_list_hit_significance_tagging_kernel(
         y_words = sb("y_words", [P, GROUPS, S], U32)
         y_tiles = {}
         y_bf = {}
-        y_bf_tags = ["wt_bf1_1", "h_bf2"] + ["inv_noise3", "h_bf3"] * 3
+        y_bf_tags = ["wt_bf1_1", "h_bf2", "inv_noise3", "h_bf3", None, None, None, None]
         d_acc = {}
         y_banks = [2, 3, 4, 5, 2, 3, 4, 5, 2, 3, 0, 1, 4, 5, 6, 7]
 
@@ -402,8 +401,7 @@ def tile_list_hit_significance_tagging_kernel(
 
         for i, unit in enumerate(units):
             if i == len(units) - 1:
-                round_y(*unit, cols=slice(0, 128), copy=nc.scalar.copy)
-                round_y(*unit, cols=slice(128, 256))
+                round_y(*unit, copy=nc.scalar.copy)
             else:
                 round_y(*unit)
             if i > 0:

@@ -244,15 +244,14 @@ def tile_list_hit_significance_tagging_kernel(
         def signal(c, a, start, stop):
             first_stage(d_acc[c], c, a, ws_words[a][:], FP8X4, P, ws_sc[a][:], start, stop)
 
-        def excess(c):
-            if c not in d_acc:
-                d_acc[c] = bank(d_banks[c])
-                signal(c, 1, True, False)
-                signal(c, 0, False, False)
-                background(c, 0, False, False)
-                background(c, 1, False, True)
-            else:
-                signal(c, 1, False, True)
+        def signals(c):
+            d_acc[c] = bank(d_banks[c])
+            signal(c, 1, True, False)
+            signal(c, 0, False, False)
+
+        def backgrounds(c):
+            background(c, 0, False, False)
+            background(c, 1, False, True)
 
         def scale(c):
             s, i = divmod(c * CHUNK, span_w)
@@ -301,9 +300,7 @@ def tile_list_hit_significance_tagging_kernel(
                         out=y[:, t, :], in_=acc[:, u * w : (u + 1) * w], func=ACT.Identity, bias=bias[:, g, t : t + 1]
                     )
                 done = t0 + per_bank
-                step = 2 if w > span_w or (s, g) in ((0, 0), (spans - 1, GROUPS - 1)) else PACK
-                if done % step == 0:
-                    nc.sync.dma_start(out=rows_out[:, done - step : done, :], in_=y[:, done - step : done, :])
+                nc.sync.dma_start(out=rows_out[:, t0:done, :], in_=y[:, t0:done, :])
             for i in range(w // span_w):
                 y_tiles[s + i, g] = y[:, :, i * span_w : (i + 1) * span_w]
 
@@ -323,9 +320,10 @@ def tile_list_hit_significance_tagging_kernel(
                 in_=y_bf[s, g][:].rearrange("p j t -> p (j t)"),
             )
 
-        def store_words(cols):
+        def store_words(groups, cols):
             nc.sync.dma_start(
-                out=out_1.rearrange("g p m t -> p g (m t)").bitcast(I32)[:, :, cols], in_=y_words[:, :, cols].bitcast(I32)
+                out=out_1.rearrange("g p m t -> p g (m t)").bitcast(I32)[:, groups, cols],
+                in_=y_words[:, groups, cols].bitcast(I32),
             )
 
         for c in range(AHEAD):
@@ -348,7 +346,7 @@ def tile_list_hit_significance_tagging_kernel(
         for c in range(AHEAD):
             signal(c, 0, False, False)
         for c in range(2):
-            excess(c)
+            signal(c, 1, False, True)
             scale(c)
         for c in (4, 5):
             noise(c, 0)
@@ -358,10 +356,10 @@ def tile_list_hit_significance_tagging_kernel(
         quantize_h(0)
         quantize_wt(0, 0)
         quantize_h(1)
-        excess(2)
+        signal(2, 1, False, True)
         scale(2)
         quantize_wt(0, 1)
-        excess(3)
+        signal(3, 1, False, True)
         scale(3)
         for c in (6, 7):
             noise(c, 0)
@@ -373,14 +371,19 @@ def tile_list_hit_significance_tagging_kernel(
         round_wt(1, 1, nc.vector.tensor_copy)
         quantize_wt(1, 0)
         quantize_wt(1, 1)
-        for c in (4, 5):
-            excess(c)
-            scale(c)
+        signals(4)
+        backgrounds(4)
+        scale(4)
+        signals(5)
         features(1, 0, 256)
-        excess(6)
+        backgrounds(5)
+        scale(5)
+        signals(6)
         features(0, 1, 256)
+        backgrounds(6)
         features(1, 1, 256)
-        excess(7)
+        signals(7)
+        backgrounds(7)
         quantize_h(4)
         quantize_h(5)
         scale(6)
@@ -392,12 +395,17 @@ def tile_list_hit_significance_tagging_kernel(
         features(3, 0, 256)
         features(3, 1, 256)
         units = [(0, 0), (1, 0), (0, 1), (1, 1), (2, 0), (2, 1), (3, 0), (3, 1)]
-        word_stores = {(1, 1): slice(0, 512), (2, 1): slice(512, 768), (3, 1): slice(768, S)}
+        word_stores = {
+            (1, 0): (slice(0, 1), slice(0, 512)),
+            (1, 1): (slice(1, 2), slice(0, 512)),
+            (2, 1): (slice(0, 2), slice(512, 768)),
+            (3, 1): (slice(0, 2), slice(768, S)),
+        }
 
         def finish(unit):
             quantize_y(*unit)
             if unit in word_stores:
-                store_words(word_stores[unit])
+                store_words(*word_stores[unit])
 
         for i, unit in enumerate(units):
             if i == len(units) - 1:

@@ -18,17 +18,19 @@ ALU = mybir.AluOpType
 
 P = 128
 PACK = 4
-PASSES = K // (P * PACK)
-GROUPS = N // (P * PACK)
+PASS_ROWS = P * PACK
+PASSES = K // PASS_ROWS
+GROUPS = N // PASS_ROWS
+BLOCKS = PASS_ROWS // 32
 CHUNK = 128
-CHUNKS = S // CHUNK
+SPAN = 256
 HALF = 512
 BANK = 512
-SPANS = [256, 256, 256, 256]
-PARTS = [slice(0, 256), slice(256, 512)]
-PIECE = 256
 AHEAD = 4
+LIST_ROWS = 16
+STAGED = slice(P - BLOCKS * PASSES, P)
 WQ_SC, WB_SC = HALF, HALF + H
+BIAS_PITCH = 8
 
 
 def tile_list_hit_significance_tagging_kernel(
@@ -45,17 +47,16 @@ def tile_list_hit_significance_tagging_kernel(
         def bank(b):
             return psum.tile([P, BANK], F32, name="bank%d" % b, tag="bank%d" % b)
 
-        offsets = keep.tile([P, S // 16], U16, name="offsets")
-        rows = 16 * PASSES
+        offsets = keep.tile([P, S // LIST_ROWS], U16, name="offsets")
         sc_window = sb("sc_window", [P, T], U8)
-        nc.sync.dma_start(out=sc_window[P - rows : P, :].bitcast(I32), in_=tab_scales.rearrange("a q t -> q a t").bitcast(I32))
-        nc.vector.memset(sc_window[0 : P - rows, :].bitcast(I32), 0)
+        nc.sync.dma_start(out=sc_window[STAGED, :].bitcast(I32), in_=tab_scales.rearrange("a q t -> q a t").bitcast(I32))
+        nc.vector.memset(sc_window[0 : STAGED.start, :].bitcast(I32), 0)
         nc.sync.dma_start(offsets[:], offs)
         widths = [HALF + 2 * H, HALF]
-        stage = [sb("stage%d" % h, [P, widths[h]], U8) for h in range(2)]
+        stage = [sb("stage%d" % half, [P, widths[half]], U8) for half in range(2)]
         for first, w_scales in ((WQ_SC, wq_scales), (WB_SC, wb_scales)):
             nc.sync.dma_start(
-                out=stage[0][P - rows : P, first : first + H].bitcast(I32),
+                out=stage[0][STAGED, first : first + H].bitcast(I32),
                 in_=w_scales.rearrange("a q c -> q a c").bitcast(I32),
             )
 
@@ -84,17 +85,19 @@ def tile_list_hit_significance_tagging_kernel(
         nc.vector.memset(all_planes[:].bitcast(I32), 0)
         planes = [all_planes[:, 0 : PASSES * widths[0]], all_planes[:, PASSES * widths[0] :]]
 
-        def pick_scales(h):
-            picked = sb("sc_picked%d" % h, [P, HALF], U8, tag="sc_picked")
-            cols = slice(h * HALF // 16, (h + 1) * HALF // 16)
-            nc.vector.tensor_copy(picked[:], sc_window[:].indirect(offsets[:, cols]))
-            nc.vector.tensor_copy(stage[h][P - rows : P, 0:HALF].bitcast(I32), picked[P - rows : P, :].bitcast(I32))
+        def list_half(half):
+            return offsets[:, half * HALF // LIST_ROWS : (half + 1) * HALF // LIST_ROWS]
 
-        def carry(h):
+        def pick_scales(half):
+            picked = sb("sc_picked%d" % half, [P, HALF], U8, tag="sc_picked")
+            nc.vector.tensor_copy(picked[:], sc_window[:].indirect(list_half(half)))
+            nc.vector.tensor_copy(stage[half][STAGED, 0:HALF].bitcast(I32), picked[STAGED, :].bitcast(I32))
+
+        def carry(half):
             for quad in (0, 2, 1, 3):
                 nc.sync.dma_start(
-                    out=planes[h][32 * quad : 32 * quad + 4, :].bitcast(I32),
-                    in_=stage[h][P - rows + 8 * quad : P - rows + 8 * quad + 8, :].bitcast(I32),
+                    out=planes[half][32 * quad : 32 * quad + 4, :].bitcast(I32),
+                    in_=stage[half][STAGED.start + 8 * quad : STAGED.start + 8 * quad + 8, :].bitcast(I32),
                 )
 
         pick_scales(0)
@@ -105,14 +108,14 @@ def tile_list_hit_significance_tagging_kernel(
 
         v = [[None] * (S // HALF) for a in range(PASSES)]
 
-        def gather(a, h, tag=None):
-            v[a][h] = sb("v%d_%d" % (a, h), [P, HALF], U32, tag=tag)
-            cols = slice(h * HALF // 16, (h + 1) * HALF // 16)
-            nc.vector.tensor_copy(v[a][h][:], tab[a][:].bitcast(U32).indirect(offsets[:, cols]))
+        def gather(a, half, tag=None):
+            v[a][half] = sb("v%d_%d" % (a, half), [P, HALF], U32, tag=tag)
+            nc.vector.tensor_copy(v[a][half][:], tab[a][:].bitcast(U32).indirect(list_half(half)))
 
         wq = sb("wq", [P, PASSES, H], I32)
         wb = sb("wb", [P, PASSES, 2 * H], U8)
         w_sc = sb("w_sc", [P, PASSES, 2 * H], U8)
+
 
         def deal_wq(a):
             nc.vector.tensor_copy(
@@ -144,11 +147,12 @@ def tile_list_hit_significance_tagging_kernel(
         for a, tag in enumerate(("wq_raw0", "wb_raw0")):
             ws_raw.append(sb("ws_raw%d" % a, [P, PACK, H], F32, tag=tag))
             nc.sync.dma_start(out=ws_raw[a][:], in_=ws_rows[a])
-        w_raw = sb("w_raw", [P, GROUPS * PACK * 512 + GROUPS * 8], F32, tag="stage1")
-        bias = w_raw[:, GROUPS * PACK * 512 :].rearrange("p (g t) -> p g t", g=GROUPS)
+        w_raw = sb("w_raw", [P, GROUPS * (PACK * PASS_ROWS + BIAS_PITCH)], F32, tag="stage1")
+        bias = w_raw[:, GROUPS * PACK * PASS_ROWS :].rearrange("p (g t) -> p g t", g=GROUPS)
         wt_raw = []
         for g in range(GROUPS):
-            wt_raw.append(w_raw[:, PACK * 512 * g : PACK * 512 * (g + 1)].rearrange("p (j c) -> p j c", j=PACK))
+            room = w_raw[:, PACK * PASS_ROWS * g : PACK * PASS_ROWS * (g + 1)]
+            wt_raw.append(room.rearrange("p (j c) -> p j c", j=PACK))
             nc.sync.dma_start(out=wt_raw[g], in_=wt_rows[g])
             if g == 0:
                 nc.sync.dma_start(out=bias[:, :, 0:PACK], in_=bt.rearrange("(g p t) -> p g t", g=GROUPS, t=PACK))
@@ -158,14 +162,14 @@ def tile_list_hit_significance_tagging_kernel(
         deal_wb(1)
 
         def first_stage(acc, c, a, words, dtype, width, scales, start, stop):
-            h, o = divmod(c * CHUNK, HALF)
+            half, o = divmod(c * CHUNK, HALF)
             for t in range(PACK):
                 nc.tensor.matmul_mx(
                     out=acc[:, t * CHUNK : (t + 1) * CHUNK],
                     lhsT=words[:, t * width : (t + 1) * width].bitcast(dtype),
                     lhsT_scale=scales[:, t * P : (t + 1) * P],
-                    rhs=v[a][h][:, o : o + CHUNK].bitcast(FP8X4),
-                    rhs_scale=planes[h][:, a * widths[h] + o : a * widths[h] + o + CHUNK],
+                    rhs=v[a][half][:, o : o + CHUNK].bitcast(FP8X4),
+                    rhs_scale=planes[half][:, a * widths[half] + o : a * widths[half] + o + CHUNK],
                     start=start and t == 0,
                     stop=stop and t == PACK - 1,
                 )
@@ -177,6 +181,7 @@ def tile_list_hit_significance_tagging_kernel(
         inv_noise = {}
         q_banks = [0, 1, 2, 3, 0, 1, 4, 5]
         d_banks = [4, 5, 6, 7, 0, 1, 6, 7]
+        y_banks = [2, 3, 4, 5, 2, 3, 4, 5, 2, 3, 0, 1, 4, 5, 6, 7]
 
         def noise(c, a):
             if a == 0:
@@ -203,19 +208,21 @@ def tile_list_hit_significance_tagging_kernel(
         ws_sc = [sb("ws_sc%d" % a, [P, H], U8) for a in range(PASSES)]
         ws_bf = {}
 
-        def round_ws(a, u, on_scalar=False):
+        def negate_on_vector(dst, src):
+            nc.vector.tensor_scalar(out=dst, in0=src, scalar1=-1.0, scalar2=None, op0=ALU.mult)
+
+        def negate_on_scalar(dst, src):
+            nc.scalar.activation(out=dst, in_=src, func=ACT.Copy, scale=-1.0)
+
+        def round_ws(a, u, negate):
             ws_bf[a, u] = sb("ws_bf%d_%d" % (a, u), [P, 2 * P * PACK], BF16)
-            dst, src = dealt(ws_bf[a, u], ws_raw[a][:], u)
-            if on_scalar:
-                nc.scalar.activation(out=dst, in_=src, func=ACT.Copy, scale=-1.0)
-            else:
-                nc.vector.tensor_scalar(out=dst, in0=src, scalar1=-1.0, scalar2=None, op0=ALU.mult)
+            negate(*dealt(ws_bf[a, u], ws_raw[a][:], u))
 
         def quantize_ws(a, u):
             quantize_pair(ws_words[a], ws_sc[a], ws_bf[a, u], u)
 
-        wt_words = [sb("wt_words%d" % g, [P, 512], U32) for g in range(GROUPS)]
-        wt_sc = [sb("wt_sc%d" % g, [P, 512], U8) for g in range(GROUPS)]
+        wt_words = [sb("wt_words%d" % g, [P, PASS_ROWS], U32) for g in range(GROUPS)]
+        wt_sc = [sb("wt_sc%d" % g, [P, PASS_ROWS], U8) for g in range(GROUPS)]
         wt_bf = {}
 
         def round_wt(g, u, copy, tag=None):
@@ -225,18 +232,16 @@ def tile_list_hit_significance_tagging_kernel(
         def quantize_wt(g, u):
             quantize_pair(wt_words[g], wt_sc[g], wt_bf[g, u], u)
 
-        span_w = 256
-        spans = S // span_w
         h_bf = {}
-        h_words = [sb("h_words%d" % n, [P, HALF], U32) for n in range(S // HALF)]
-        h_sc = [sb("h_sc%d" % n, [P, HALF], U8) for n in range(S // HALF)]
+        h_words = [sb("h_words%d" % half, [P, HALF], U32) for half in range(S // HALF)]
+        h_sc = [sb("h_sc%d" % half, [P, HALF], U8) for half in range(S // HALF)]
         y_sc = sb("y_sc", [P, GROUPS, S], U8)
         y_words = sb("y_words", [P, GROUPS, S], U32)
         y_tiles = {}
+        y_whole = {}
         y_bf = {}
         y_bf_tags = ["wt_bf1_1", "h_bf2", "inv_noise3", "h_bf3", None, None, None, None]
         d_acc = {}
-        y_banks = [2, 3, 4, 5, 2, 3, 4, 5, 2, 3, 0, 1, 4, 5, 6, 7]
 
         def background(c, a, start, stop):
             first_stage(d_acc[c], c, a, wb[:, a, :], FP4X4, 2 * P, w_sc[:, a, H : 2 * H], start, stop)
@@ -254,9 +259,9 @@ def tile_list_hit_significance_tagging_kernel(
             background(c, 1, False, True)
 
         def scale(c):
-            s, i = divmod(c * CHUNK, span_w)
+            s, i = divmod(c * CHUNK, SPAN)
             if s not in h_bf:
-                h_bf[s] = sb("h_bf%d" % s, [P, span_w, PACK], BF16, tag="wt_bf0_0" if s == 1 else None)
+                h_bf[s] = sb("h_bf%d" % s, [P, SPAN, PACK], BF16, tag="wt_bf0_0" if s == 1 else None)
             nc.vector.scalar_tensor_tensor(
                 out=h_bf[s][:, i : i + CHUNK, :],
                 in0=hit_major(d_acc[c]),
@@ -267,53 +272,57 @@ def tile_list_hit_significance_tagging_kernel(
             )
 
         def quantize_h(c):
-            n, o = divmod(c * CHUNK, HALF)
-            s, i = divmod(c * CHUNK, span_w)
+            half, o = divmod(c * CHUNK, HALF)
+            s, i = divmod(c * CHUNK, SPAN)
             nc.vector.quantize_mx(
-                out=h_words[n][:, o : o + CHUNK].bitcast(FP8X4),
-                scales=h_sc[n][:, o : o + CHUNK],
+                out=h_words[half][:, o : o + CHUNK].bitcast(FP8X4),
+                scales=h_sc[half][:, o : o + CHUNK],
                 in_=h_bf[s][:, i : i + CHUNK, :].rearrange("p j t -> p (j t)"),
             )
 
-        def features(s, g, w):
-            n, o = divmod(s * span_w, HALF)
-            cols = slice(s * span_w, s * span_w + w)
-            y = sb("y%d_%d" % (s, g), [P, PACK, w], F32)
+        def features(s, g, w, slices=range(PACK)):
+            half, o = divmod(s * SPAN, HALF)
+            cols = slice(s * SPAN, s * SPAN + w)
+            if (s, g) not in y_tiles:
+                whole = sb("y%d_%d" % (s, g), [P, PACK, w], F32)
+                y_whole[s, g] = whole
+                for i in range(w // SPAN):
+                    y_tiles[s + i, g] = whole[:, :, i * SPAN : (i + 1) * SPAN]
+            y = y_whole[s, g]
             per_bank = BANK // w
-            rows_out = out_0[512 * g : 512 * (g + 1), cols].rearrange("(p t) j -> p t j", t=PACK)
-            for t0 in range(0, PACK, per_bank):
+            rows_out = out_0[PASS_ROWS * g : PASS_ROWS * (g + 1), cols].rearrange("(p t) j -> p t j", t=PACK)
+            for t0 in range(slices.start, slices.stop, per_bank):
                 acc = bank(y_banks.pop(0))
-                for u in range(per_bank):
-                    t = t0 + u
+                for place in range(per_bank):
+                    t = t0 + place
                     nc.tensor.matmul_mx(
-                        out=acc[:, u * w : (u + 1) * w],
+                        out=acc[:, place * w : (place + 1) * w],
                         lhsT=wt_words[g][:, t * P : (t + 1) * P].bitcast(FP8X4),
                         lhsT_scale=wt_sc[g][:, t * P : (t + 1) * P],
-                        rhs=h_words[n][:, o : o + w].bitcast(FP8X4),
-                        rhs_scale=h_sc[n][:, o : o + w],
+                        rhs=h_words[half][:, o : o + w].bitcast(FP8X4),
+                        rhs_scale=h_sc[half][:, o : o + w],
                         start=True,
                         stop=True,
                     )
-                for u in range(per_bank):
-                    t = t0 + u
+                for place in range(per_bank):
+                    t = t0 + place
                     nc.scalar.activation(
-                        out=y[:, t, :], in_=acc[:, u * w : (u + 1) * w], func=ACT.Identity, bias=bias[:, g, t : t + 1]
+                        out=y[:, t, :],
+                        in_=acc[:, place * w : (place + 1) * w],
+                        func=ACT.Identity,
+                        bias=bias[:, g, t : t + 1],
                     )
-                done = t0 + per_bank
-                nc.sync.dma_start(out=rows_out[:, t0:done, :], in_=y[:, t0:done, :])
-            for i in range(w // span_w):
-                y_tiles[s + i, g] = y[:, :, i * span_w : (i + 1) * span_w]
+                nc.sync.dma_start(out=rows_out[:, t0 : t0 + per_bank, :], in_=y[:, t0 : t0 + per_bank, :])
 
-        def round_y(s, g, cols=slice(0, span_w), copy=nc.vector.tensor_copy):
-            if (s, g) not in y_bf:
-                y_bf[s, g] = sb("y_bf%d_%d" % (s, g), [P, span_w, PACK], BF16, tag=y_bf_tags.pop(0))
+        def round_y(s, g, copy):
+            y_bf[s, g] = sb("y_bf%d_%d" % (s, g), [P, SPAN, PACK], BF16, tag=y_bf_tags.pop(0))
             copy(
-                y_bf[s, g][:, cols, :].rearrange("p (c i) t -> p c t i", i=4),
-                y_tiles[s, g][:, :, cols].rearrange("p t (c i) -> p c t i", i=4),
+                y_bf[s, g][:].rearrange("p (c i) t -> p c t i", i=4),
+                y_tiles[s, g].rearrange("p t (c i) -> p c t i", i=4),
             )
 
         def quantize_y(s, g):
-            cols = slice(s * span_w, (s + 1) * span_w)
+            cols = slice(s * SPAN, (s + 1) * SPAN)
             nc.vector.quantize_mx(
                 out=y_words[:, g, cols].bitcast(FP8X4),
                 scales=y_sc[:, g, cols],
@@ -334,11 +343,11 @@ def tile_list_hit_significance_tagging_kernel(
         for c in range(AHEAD):
             noise(c, 1)
         for u in range(2):
-            round_ws(0, u)
+            round_ws(0, u, negate_on_vector)
         for u in range(2):
             quantize_ws(0, u)
-        round_ws(1, 0)
-        round_ws(1, 1, on_scalar=True)
+        round_ws(1, 0, negate_on_vector)
+        round_ws(1, 1, negate_on_scalar)
         for u in range(2):
             quantize_ws(1, u)
         for c in range(AHEAD):
@@ -348,7 +357,7 @@ def tile_list_hit_significance_tagging_kernel(
         for c in range(2):
             signal(c, 1, False, True)
             scale(c)
-        for c in (4, 5):
+        for c in (AHEAD, AHEAD + 1):
             noise(c, 0)
             noise(c, 1)
         round_wt(0, 0, nc.scalar.copy)
@@ -361,10 +370,10 @@ def tile_list_hit_significance_tagging_kernel(
         quantize_wt(0, 1)
         signal(3, 1, False, True)
         scale(3)
-        for c in (6, 7):
+        for c in (AHEAD + 2, AHEAD + 3):
             noise(c, 0)
             noise(c, 1)
-        features(0, 0, 256)
+        features(0, 0, SPAN)
         quantize_h(2)
         quantize_h(3)
         round_wt(1, 0, nc.vector.tensor_copy, tag="h_bf0")
@@ -375,13 +384,13 @@ def tile_list_hit_significance_tagging_kernel(
         backgrounds(4)
         scale(4)
         signals(5)
-        features(1, 0, 256)
+        features(1, 0, SPAN)
         backgrounds(5)
         scale(5)
         signals(6)
-        features(0, 1, 256)
+        features(0, 1, HALF, range(0, 2))
         backgrounds(6)
-        features(1, 1, 256)
+        features(0, 1, HALF, range(2, PACK))
         signals(7)
         backgrounds(7)
         quantize_h(4)
@@ -390,16 +399,17 @@ def tile_list_hit_significance_tagging_kernel(
         scale(7)
         quantize_h(6)
         quantize_h(7)
-        features(2, 0, 256)
-        features(2, 1, 256)
-        features(3, 0, 256)
-        features(3, 1, 256)
+        features(2, 0, SPAN)
+        features(2, 1, SPAN)
+        features(3, 0, SPAN)
+        features(3, 1, SPAN)
+
         units = [(0, 0), (1, 0), (0, 1), (1, 1), (2, 0), (2, 1), (3, 0), (3, 1)]
         word_stores = {
-            (1, 0): (slice(0, 1), slice(0, 512)),
-            (1, 1): (slice(1, 2), slice(0, 512)),
-            (2, 1): (slice(0, 2), slice(512, 768)),
-            (3, 1): (slice(0, 2), slice(768, S)),
+            (1, 0): (slice(0, 1), slice(0, HALF)),
+            (1, 1): (slice(1, 2), slice(0, HALF)),
+            (2, 1): (slice(0, GROUPS), slice(HALF, HALF + SPAN)),
+            (3, 1): (slice(0, GROUPS), slice(HALF + SPAN, S)),
         }
 
         def finish(unit):
@@ -408,16 +418,13 @@ def tile_list_hit_significance_tagging_kernel(
                 store_words(*word_stores[unit])
 
         for i, unit in enumerate(units):
-            if i == len(units) - 1:
-                round_y(*unit, copy=nc.scalar.copy)
-            else:
-                round_y(*unit)
+            round_y(*unit, nc.scalar.copy if i == len(units) - 1 else nc.vector.tensor_copy)
             if i > 0:
                 finish(units[i - 1])
         finish(units[-1])
 
         for r in range(4):
             nc.scalar.dma_start(
-                out=out_2[:, r:16:4, :].rearrange("g q m -> q g m").bitcast(I32),
+                out=out_2[:, r:BLOCKS:4, :].rearrange("g q m -> q g m").bitcast(I32),
                 in_=y_sc[r:P:32, :, :].bitcast(I32),
             )

@@ -23,14 +23,16 @@ PASSES = K // PASS_ROWS
 GROUPS = N // PASS_ROWS
 BLOCKS = PASS_ROWS // 32
 CHUNK = 128
+CHUNKS = S // CHUNK
 SPAN = 256
 HALF = 512
 BANK = 512
-AHEAD = 4
 LIST_ROWS = 16
 STAGED = slice(P - BLOCKS * PASSES, P)
-WQ_SC, WB_SC = HALF, HALF + H
+WQ_SC, WB_SC = S, S + H
+ROW = S + 2 * H
 BIAS_PITCH = 8
+ALIGN = 64
 
 
 def tile_list_hit_significance_tagging_kernel(
@@ -39,10 +41,14 @@ def tile_list_hit_significance_tagging_kernel(
     nc = tc.nc
     with ExitStack() as ctx:
         keep = ctx.enter_context(tc.tile_pool(name="keep", bufs=1))
+        late = ctx.enter_context(tc.tile_pool(name="late", bufs=1))
         psum = ctx.enter_context(tc.psum_pool(name="psum", bufs=1))
 
         def sb(name, shape, dtype, tag=None):
-            return keep.tile(shape, dtype, name=name, tag=tag or name, align_bytes=64)
+            return keep.tile(shape, dtype, name=name, tag=tag or name, align_bytes=ALIGN)
+
+        def placed(name, shape, dtype, offset):
+            return late.tile(shape, dtype, name=name, tag=name, align_bytes=ALIGN, offset=offset)
 
         def bank(b):
             return psum.tile([P, BANK], F32, name="bank%d" % b, tag="bank%d" % b)
@@ -52,124 +58,116 @@ def tile_list_hit_significance_tagging_kernel(
         nc.sync.dma_start(out=sc_window[STAGED, :].bitcast(I32), in_=tab_scales.rearrange("a q t -> q a t").bitcast(I32))
         nc.vector.memset(sc_window[0 : STAGED.start, :].bitcast(I32), 0)
         nc.sync.dma_start(offsets[:], offs)
-        widths = [HALF + 2 * H, HALF]
-        stage = [sb("stage%d" % half, [P, widths[half]], U8) for half in range(2)]
+        stage = sb("stage", [P, ROW], U8)
         for first, w_scales in ((WQ_SC, wq_scales), (WB_SC, wb_scales)):
             nc.sync.dma_start(
-                out=stage[0][STAGED, first : first + H].bitcast(I32),
+                out=stage[STAGED, first : first + H].bitcast(I32),
                 in_=w_scales.rearrange("a q c -> q a c").bitcast(I32),
             )
 
-        tab = []
+        w_bytes = 4 * PACK * H
+        tab0_at = w_bytes - ALIGN
+        wb_at = w_bytes
+        bias_at = wb_at + PASSES * 2 * H
+        wq1_at = bias_at + ALIGN
+        ws0_at = wq1_at + 4 * H
+        ws1_at = ws0_at + w_bytes
+        last_noise = ws1_at + 2048
 
-        def load_tab(a, tag):
-            tab.append(sb("tab%d" % a, [P, T], I32, tag=tag))
-            nc.sync.dma_start(out=tab[a][:], in_=tab_words[a].rearrange("p t i -> p (t i)").bitcast(I32))
+        tab = [placed("tab0", [P, T], I32, tab0_at)]
+        nc.sync.dma_start(out=tab[0][:], in_=tab_words[0].rearrange("p t i -> p (t i)").bitcast(I32))
+        wq_raw = [sb("wq_raw0", [P, H], I32)]
+        nc.sync.dma_start(out=wq_raw[0][:], in_=wq_words[0].rearrange("p c i -> p (c i)").bitcast(I32))
 
-        wq_raw = []
-        wb_raw = []
+        planes = sb("planes", [P, PASSES * ROW], U8)
+        nc.vector.memset(planes[:].bitcast(I32), 0)
 
-        def load_wq(a, tag):
-            wq_raw.append(sb("wq_raw%d" % a, [P, H], I32, tag=tag))
-            nc.sync.dma_start(out=wq_raw[a][:], in_=wq_words[a].rearrange("p c i -> p (c i)").bitcast(I32))
+        def hits(first, count):
+            return offsets[:, first // LIST_ROWS : (first + count) // LIST_ROWS]
 
-        def load_wb(a, tag):
-            wb_raw.append(sb("wb_raw%d" % a, [P, H // 2], I32, tag=tag))
-            nc.sync.dma_start(out=wb_raw[a][:], in_=wb_words[a].bitcast(I32))
+        picked = sb("sc_picked", [P, S], U8)
+        nc.vector.tensor_copy(picked[:], sc_window[:].indirect(offsets[:]))
+        nc.vector.tensor_copy(stage[STAGED, 0:S].bitcast(I32), picked[STAGED, :].bitcast(I32))
+        for quad in (0, 2, 1, 3):
+            nc.sync.dma_start(
+                out=planes[32 * quad : 32 * quad + 4, :].bitcast(I32),
+                in_=stage[STAGED.start + 8 * quad : STAGED.start + 8 * quad + 8, :].bitcast(I32),
+            )
+        tab.append(sb("tab1", [P, T], I32, tag="sc_picked"))
+        nc.sync.dma_start(out=tab[1][:], in_=tab_words[1].rearrange("p t i -> p (t i)").bitcast(I32))
 
-        load_tab(0, "tab0")
-        load_wq(0, "wq_raw0")
-        load_wb(0, "wb_raw0")
+        widths = [HALF, SPAN]
+        v = [[None] * (S // widths[a]) for a in range(PASSES)]
 
-        all_planes = sb("all_planes", [P, PASSES * sum(widths)], U8)
-        nc.vector.memset(all_planes[:].bitcast(I32), 0)
-        planes = [all_planes[:, 0 : PASSES * widths[0]], all_planes[:, PASSES * widths[0] :]]
+        def gather(a, i):
+            v[a][i] = sb("v%d_%d" % (a, i), [P, widths[a]], U32)
+            nc.vector.tensor_copy(v[a][i][:], tab[a][:].bitcast(U32).indirect(hits(i * widths[a], widths[a])))
 
-        def list_half(half):
-            return offsets[:, half * HALF // LIST_ROWS : (half + 1) * HALF // LIST_ROWS]
+        wq = [sb("wq%d" % a, [P, H], I32) for a in range(PASSES)]
+        wb = [sb("wb%d" % a, [P, 2 * H], U8) for a in range(PASSES)]
+        w_sc = sb("w_sc", [P, PASSES * 2 * H], U8)
 
-        def pick_scales(half):
-            picked = sb("sc_picked%d" % half, [P, HALF], U8, tag="sc_picked")
-            nc.vector.tensor_copy(picked[:], sc_window[:].indirect(list_half(half)))
-            nc.vector.tensor_copy(stage[half][STAGED, 0:HALF].bitcast(I32), picked[STAGED, :].bitcast(I32))
-
-        def carry(half):
-            for quad in (0, 2, 1, 3):
-                nc.sync.dma_start(
-                    out=planes[half][32 * quad : 32 * quad + 4, :].bitcast(I32),
-                    in_=stage[half][STAGED.start + 8 * quad : STAGED.start + 8 * quad + 8, :].bitcast(I32),
-                )
-
-        pick_scales(0)
-        carry(0)
-        pick_scales(1)
-        load_tab(1, "sc_window")
-        carry(1)
-
-        v = [[None] * (S // HALF) for a in range(PASSES)]
-
-        def gather(a, half, tag=None):
-            v[a][half] = sb("v%d_%d" % (a, half), [P, HALF], U32, tag=tag)
-            nc.vector.tensor_copy(v[a][half][:], tab[a][:].bitcast(U32).indirect(list_half(half)))
-
-        wq = sb("wq", [P, PASSES, H], I32)
-        wb = sb("wb", [P, PASSES, 2 * H], U8)
-        w_sc = sb("w_sc", [P, PASSES, 2 * H], U8)
-
-
-        def deal_wq(a):
-            nc.vector.tensor_copy(
-                wq[:, a, :].rearrange("p (t c i) -> p c t i", t=PACK, i=4),
-                wq_raw[a][:].rearrange("p (c i t) -> p c t i", t=PACK, i=4),
+        def deal_wq(a, copy):
+            copy(
+                wq[a][:].bitcast(U32).rearrange("p (t c i) -> p c t i", t=PACK, i=4),
+                wq_raw[a][:].bitcast(U32).rearrange("p (c i t) -> p c t i", t=PACK, i=4),
             )
 
-        def deal_wb(a):
+        def deal_scales(a, first, count):
             nc.vector.tensor_copy(
-                wb[:, a, :].bitcast(U16).rearrange("p (t c i) -> p c t i", t=PACK, i=8),
-                wb_raw[a][:].bitcast(U16).rearrange("p (c i t) -> p c t i", t=PACK, i=8),
+                w_sc[:, (2 * a + first) * H : (2 * a + first + count) * H].rearrange(
+                    "p (x t c i) -> p x c t i", x=count, t=PACK, i=16
+                ),
+                planes[:, a * ROW + S + first * H : a * ROW + S + (first + count) * H].rearrange(
+                    "p (x c i t) -> p x c t i", x=count, t=PACK, i=16
+                ),
             )
 
         gather(0, 0)
         gather(0, 1)
-        deal_wq(0)
-        deal_wb(0)
-        for a in range(PASSES):
-            first = a * widths[0]
-            nc.vector.tensor_copy(
-                w_sc[:, a, :].rearrange("p (x t c i) -> p x c t i", x=2, t=PACK, i=16),
-                planes[0][:, first + WQ_SC : first + widths[0]].rearrange("p (x c i t) -> p x c t i", x=2, t=PACK, i=16),
-            )
-        load_wq(1, "sc_picked")
-        load_wb(1, "tab0")
+        deal_wq(0, nc.vector.tensor_copy)
+        deal_scales(0, 0, 1)
+        deal_scales(1, 0, 2)
+        deal_scales(0, 1, 1)
+
+        wq_raw.append(placed("wq_raw1", [P, H], I32, wq1_at))
+        nc.sync.dma_start(out=wq_raw[1][:], in_=wq_words[1].rearrange("p c i -> p (c i)").bitcast(I32))
+        wb_raw = placed("wb_raw", [P, PASSES, H // 2], I32, wb_at)
+        nc.sync.dma_start(out=wb_raw[:], in_=wb_words.rearrange("a p c -> p a c").bitcast(I32))
         ws_rows = ws.rearrange("(a p j) c -> a p j c", a=PASSES, j=PACK)
         wt_rows = wt.rearrange("(p j) (g n) -> g p j n", j=PACK, g=GROUPS)
         ws_raw = []
-        for a, tag in enumerate(("wq_raw0", "wb_raw0")):
-            ws_raw.append(sb("ws_raw%d" % a, [P, PACK, H], F32, tag=tag))
+        for a, at in enumerate((ws0_at, ws1_at)):
+            ws_raw.append(placed("ws_raw%d" % a, [P, PACK, H], F32, at))
             nc.sync.dma_start(out=ws_raw[a][:], in_=ws_rows[a])
-        w_raw = sb("w_raw", [P, GROUPS * (PACK * PASS_ROWS + BIAS_PITCH)], F32, tag="stage1")
-        bias = w_raw[:, GROUPS * PACK * PASS_ROWS :].rearrange("p (g t) -> p g t", g=GROUPS)
-        wt_raw = []
-        for g in range(GROUPS):
-            room = w_raw[:, PACK * PASS_ROWS * g : PACK * PASS_ROWS * (g + 1)]
-            wt_raw.append(room.rearrange("p (j c) -> p j c", j=PACK))
-            nc.sync.dma_start(out=wt_raw[g], in_=wt_rows[g])
-            if g == 0:
-                nc.sync.dma_start(out=bias[:, :, 0:PACK], in_=bt.rearrange("(g p t) -> p g t", g=GROUPS, t=PACK))
-        gather(1, 0)
-        deal_wq(1)
-        gather(1, 1, tag="sc_picked")
-        deal_wb(1)
+        wt_raw = [placed("wt_raw0", [P, PACK, PASS_ROWS], F32, 0)]
+        nc.sync.dma_start(out=wt_raw[0][:], in_=wt_rows[0])
+        bias = placed("bias", [P, GROUPS, BIAS_PITCH], F32, bias_at)
+        nc.sync.dma_start(out=bias[:, :, 0:PACK], in_=bt.rearrange("(g p t) -> p g t", g=GROUPS, t=PACK))
+        wt_raw.append(sb("wt_raw1", [P, PACK, PASS_ROWS], F32, tag="wq_raw0"))
+        nc.sync.dma_start(out=wt_raw[1][:], in_=wt_rows[1])
+
+        def deal_wb(a, copy):
+            copy(
+                wb[a][:].bitcast(U16).rearrange("p (t c i) -> p c t i", t=PACK, i=8),
+                wb_raw[:, a, :].bitcast(U16).rearrange("p (c i t) -> p c t i", t=PACK, i=8),
+            )
+
+        deal_wq(1, nc.scalar.copy)
+        deal_wb(0, nc.scalar.copy)
+        for i in range(S // SPAN):
+            gather(1, i)
+        deal_wb(1, nc.vector.tensor_copy)
 
         def first_stage(acc, c, a, words, dtype, width, scales, start, stop):
-            half, o = divmod(c * CHUNK, HALF)
+            i, o = divmod(c * CHUNK, widths[a])
             for t in range(PACK):
                 nc.tensor.matmul_mx(
                     out=acc[:, t * CHUNK : (t + 1) * CHUNK],
                     lhsT=words[:, t * width : (t + 1) * width].bitcast(dtype),
                     lhsT_scale=scales[:, t * P : (t + 1) * P],
-                    rhs=v[a][half][:, o : o + CHUNK].bitcast(FP8X4),
-                    rhs_scale=planes[half][:, a * widths[half] + o : a * widths[half] + o + CHUNK],
+                    rhs=v[a][i][:, o : o + CHUNK].bitcast(FP8X4),
+                    rhs_scale=planes[:, a * ROW + c * CHUNK : a * ROW + (c + 1) * CHUNK],
                     start=start and t == 0,
                     stop=stop and t == PACK - 1,
                 )
@@ -178,21 +176,20 @@ def tile_list_hit_significance_tagging_kernel(
             return acc[:].rearrange("p (t j) -> p j t", t=PACK)
 
         q_acc = {}
+        d_acc = {}
         inv_noise = {}
-        q_banks = [0, 1, 2, 3, 0, 1, 4, 5]
-        d_banks = [4, 5, 6, 7, 0, 1, 6, 7]
-        y_banks = [2, 3, 4, 5, 2, 3, 4, 5, 2, 3, 0, 1, 4, 5, 6, 7]
 
         def noise(c, a):
             if a == 0:
-                q_acc[c] = bank(q_banks[c])
-            first_stage(q_acc[c], c, a, wq[:, a, :], FP8X4, P, w_sc[:, a, 0:H], a == 0, a == PASSES - 1)
-            if a == PASSES - 1:
-                if c // 2 not in inv_noise:
-                    inv_noise[c // 2] = sb(
-                        "inv_noise%d" % (c // 2), [P, 2, CHUNK, PACK], F32, tag="wb_raw0" if c == AHEAD else None
-                    )
-                nc.scalar.activation(out=inv_noise[c // 2][:, c % 2], in_=hit_major(q_acc[c]), func=ACT.Exp, scale=-1.0)
+                q_acc[c] = bank(c)
+            first_stage(q_acc[c], c, a, wq[a][:], FP8X4, P, w_sc[:, 2 * a * H : (2 * a + 1) * H], a == 0, a == PASSES - 1)
+
+        def exponential(c):
+            if c >= CHUNKS - 2:
+                inv_noise[c] = placed("inv_noise%d" % c, [P, CHUNK, PACK], F32, last_noise + (CHUNKS - 1 - c) * 5120)
+            else:
+                inv_noise[c] = sb("inv_noise%d" % c, [P, CHUNK, PACK], F32)
+            nc.scalar.activation(out=inv_noise[c][:], in_=hit_major(q_acc[c]), func=ACT.Exp, scale=-1.0)
 
         def dealt(rounded, raw, u):
             return (
@@ -227,30 +224,30 @@ def tile_list_hit_significance_tagging_kernel(
 
         def round_wt(g, u, copy, tag=None):
             wt_bf[g, u] = sb("wt_bf%d_%d" % (g, u), [P, 2 * P * PACK], BF16, tag=tag)
-            copy(*dealt(wt_bf[g, u], wt_raw[g], u))
+            copy(*dealt(wt_bf[g, u], wt_raw[g][:], u))
 
         def quantize_wt(g, u):
             quantize_pair(wt_words[g], wt_sc[g], wt_bf[g, u], u)
 
-        h_bf = {}
+        h_bf = [sb("h_bf%d" % half, [P, HALF * PACK], BF16) for half in range(S // HALF)]
         h_words = [sb("h_words%d" % half, [P, HALF], U32) for half in range(S // HALF)]
         h_sc = [sb("h_sc%d" % half, [P, HALF], U8) for half in range(S // HALF)]
         y_sc = sb("y_sc", [P, GROUPS, S], U8)
         y_words = sb("y_words", [P, GROUPS, S], U32)
-        y_tiles = {}
-        y_whole = {}
+        y = {}
         y_bf = {}
-        y_bf_tags = ["wt_bf1_1", "h_bf2", "inv_noise3", "h_bf3", None, None, None, None]
-        d_acc = {}
 
         def background(c, a, start, stop):
-            first_stage(d_acc[c], c, a, wb[:, a, :], FP4X4, 2 * P, w_sc[:, a, H : 2 * H], start, stop)
+            if start:
+                d_acc[c] = bank(c)
+            first_stage(d_acc[c], c, a, wb[a][:], FP4X4, 2 * P, w_sc[:, (2 * a + 1) * H : (2 * a + 2) * H], start, stop)
 
         def signal(c, a, start, stop):
+            if start:
+                d_acc[c] = bank(c)
             first_stage(d_acc[c], c, a, ws_words[a][:], FP8X4, P, ws_sc[a][:], start, stop)
 
         def signals(c):
-            d_acc[c] = bank(d_banks[c])
             signal(c, 1, True, False)
             signal(c, 0, False, False)
 
@@ -259,169 +256,186 @@ def tile_list_hit_significance_tagging_kernel(
             background(c, 1, False, True)
 
         def scale(c):
-            s, i = divmod(c * CHUNK, SPAN)
-            if s not in h_bf:
-                h_bf[s] = sb("h_bf%d" % s, [P, SPAN, PACK], BF16, tag="wt_bf0_0" if s == 1 else None)
+            half, o = divmod(c * CHUNK, HALF)
             nc.vector.scalar_tensor_tensor(
-                out=h_bf[s][:, i : i + CHUNK, :],
+                out=h_bf[half][:, o * PACK : (o + CHUNK) * PACK].rearrange("p (j t) -> p j t", t=PACK),
                 in0=hit_major(d_acc[c]),
                 scalar=-1.0,
-                in1=inv_noise[c // 2][:, c % 2],
+                in1=inv_noise[c][:],
                 op0=ALU.mult,
                 op1=ALU.mult,
             )
 
-        def quantize_h(c):
+        def quantize_h(c, count):
             half, o = divmod(c * CHUNK, HALF)
-            s, i = divmod(c * CHUNK, SPAN)
+            w = count * CHUNK
             nc.vector.quantize_mx(
-                out=h_words[half][:, o : o + CHUNK].bitcast(FP8X4),
-                scales=h_sc[half][:, o : o + CHUNK],
-                in_=h_bf[s][:, i : i + CHUNK, :].rearrange("p j t -> p (j t)"),
+                out=h_words[half][:, o : o + w].bitcast(FP8X4),
+                scales=h_sc[half][:, o : o + w],
+                in_=h_bf[half][:, o * PACK : (o + w) * PACK],
             )
 
-        def features(s, g, w, slices=range(PACK)):
-            half, o = divmod(s * SPAN, HALF)
-            cols = slice(s * SPAN, s * SPAN + w)
-            if (s, g) not in y_tiles:
-                whole = sb("y%d_%d" % (s, g), [P, PACK, w], F32)
-                y_whole[s, g] = whole
-                for i in range(w // SPAN):
-                    y_tiles[s + i, g] = whole[:, :, i * SPAN : (i + 1) * SPAN]
-            y = y_whole[s, g]
-            per_bank = BANK // w
-            rows_out = out_0[PASS_ROWS * g : PASS_ROWS * (g + 1), cols].rearrange("(p t) j -> p t j", t=PACK)
-            for t0 in range(slices.start, slices.stop, per_bank):
-                acc = bank(y_banks.pop(0))
-                for place in range(per_bank):
-                    t = t0 + place
-                    nc.tensor.matmul_mx(
-                        out=acc[:, place * w : (place + 1) * w],
-                        lhsT=wt_words[g][:, t * P : (t + 1) * P].bitcast(FP8X4),
-                        lhsT_scale=wt_sc[g][:, t * P : (t + 1) * P],
-                        rhs=h_words[half][:, o : o + w].bitcast(FP8X4),
-                        rhs_scale=h_sc[half][:, o : o + w],
-                        start=True,
-                        stop=True,
-                    )
-                for place in range(per_bank):
-                    t = t0 + place
-                    nc.scalar.activation(
-                        out=y[:, t, :],
-                        in_=acc[:, place * w : (place + 1) * w],
-                        func=ACT.Identity,
-                        bias=bias[:, g, t : t + 1],
-                    )
-                nc.sync.dma_start(out=rows_out[:, t0 : t0 + per_bank, :], in_=y[:, t0 : t0 + per_bank, :])
+        def features(half, g, t, b, stored):
+            if t == 0:
+                y[half, g] = sb("y%d_%d" % (half, g), [P, PACK, HALF], F32)
+            acc = bank(b)
+            nc.tensor.matmul_mx(
+                out=acc[:],
+                lhsT=wt_words[g][:, t * P : (t + 1) * P].bitcast(FP8X4),
+                lhsT_scale=wt_sc[g][:, t * P : (t + 1) * P],
+                rhs=h_words[half][:].bitcast(FP8X4),
+                rhs_scale=h_sc[half][:],
+                start=True,
+                stop=True,
+            )
+            nc.scalar.activation(out=y[half, g][:, t, :], in_=acc[:], func=ACT.Identity, bias=bias[:, g, t : t + 1])
+            if stored:
+                rows_out = out_0[PASS_ROWS * g : PASS_ROWS * (g + 1), half * HALF : (half + 1) * HALF]
+                nc.sync.dma_start(
+                    out=rows_out.rearrange("(p t) j -> p t j", t=PACK)[:, t + 1 - stored : t + 1, :],
+                    in_=y[half, g][:, t + 1 - stored : t + 1, :],
+                )
 
-        def round_y(s, g, copy):
-            y_bf[s, g] = sb("y_bf%d_%d" % (s, g), [P, SPAN, PACK], BF16, tag=y_bf_tags.pop(0))
+        def narrow_features(s, u, b):
+            half, o = divmod(s * SPAN, HALF)
+            if (half, 0) not in y:
+                y[half, 0] = sb("y%d_0" % half, [P, PACK, HALF], F32)
+            acc = bank(b)
+            cols = slice(o, o + SPAN)
+            for place in range(2):
+                t = 2 * u + place
+                nc.tensor.matmul_mx(
+                    out=acc[:, place * SPAN : (place + 1) * SPAN],
+                    lhsT=wt_words[0][:, t * P : (t + 1) * P].bitcast(FP8X4),
+                    lhsT_scale=wt_sc[0][:, t * P : (t + 1) * P],
+                    rhs=h_words[half][:, cols].bitcast(FP8X4),
+                    rhs_scale=h_sc[half][:, cols],
+                    start=True,
+                    stop=True,
+                )
+            for place in range(2):
+                t = 2 * u + place
+                nc.scalar.activation(
+                    out=y[half, 0][:, t, cols],
+                    in_=acc[:, place * SPAN : (place + 1) * SPAN],
+                    func=ACT.Identity,
+                    bias=bias[:, 0, t : t + 1],
+                )
+            nc.sync.dma_start(
+                out=out_0[0:PASS_ROWS, s * SPAN : (s + 1) * SPAN].rearrange("(p t) j -> p t j", t=PACK)[
+                    :, 2 * u : 2 * u + 2, :
+                ],
+                in_=y[half, 0][:, 2 * u : 2 * u + 2, cols],
+            )
+
+        def round_y(s, w, g, copy, offset=None):
+            half, o = divmod(s * SPAN, HALF)
+            name = "y_bf%d_%d" % (s, g)
+            if offset is None:
+                y_bf[s, g] = sb(name, [P, w * SPAN, PACK], BF16)
+            else:
+                y_bf[s, g] = placed(name, [P, w * SPAN, PACK], BF16, offset)
             copy(
                 y_bf[s, g][:].rearrange("p (c i) t -> p c t i", i=4),
-                y_tiles[s, g].rearrange("p t (c i) -> p c t i", i=4),
+                y[half, g][:, :, o : o + w * SPAN].rearrange("p t (c i) -> p c t i", i=4),
             )
 
-        def quantize_y(s, g):
-            cols = slice(s * SPAN, (s + 1) * SPAN)
+        def quantize_y(s, w, g):
+            cols = slice(s * SPAN, (s + w) * SPAN)
             nc.vector.quantize_mx(
                 out=y_words[:, g, cols].bitcast(FP8X4),
                 scales=y_sc[:, g, cols],
                 in_=y_bf[s, g][:].rearrange("p j t -> p (j t)"),
             )
 
-        def store_words(groups, cols):
+        def store_words(half, groups):
+            cols = slice(half * HALF, (half + 1) * HALF)
             nc.sync.dma_start(
                 out=out_1.rearrange("g p m t -> p g (m t)").bitcast(I32)[:, groups, cols],
                 in_=y_words[:, groups, cols].bitcast(I32),
             )
 
-        for c in range(AHEAD):
+        for c in range(CHUNKS):
             noise(c, 0)
-        for c in range(AHEAD):
-            d_acc[c] = bank(d_banks[c])
-            background(c, 0, True, False)
-        for c in range(AHEAD):
+        for c in range(CHUNKS):
             noise(c, 1)
+            if c < CHUNKS - 2:
+                exponential(c)
         for u in range(2):
             round_ws(0, u, negate_on_vector)
         for u in range(2):
             quantize_ws(0, u)
         round_ws(1, 0, negate_on_vector)
         round_ws(1, 1, negate_on_scalar)
+        exponential(CHUNKS - 2)
+        exponential(CHUNKS - 1)
         for u in range(2):
             quantize_ws(1, u)
-        for c in range(AHEAD):
+        first = range(CHUNKS // 2)
+        for c in first:
+            background(c, 0, True, False)
+        for c in first:
             background(c, 1, False, False)
-        for c in range(AHEAD):
+        for c in range(3):
             signal(c, 0, False, False)
-        for c in range(2):
+        for c in range(3):
             signal(c, 1, False, True)
-            scale(c)
-        for c in (AHEAD, AHEAD + 1):
-            noise(c, 0)
-            noise(c, 1)
+        signal(3, 1, False, False)
+        signal(3, 0, False, True)
         round_wt(0, 0, nc.scalar.copy)
         round_wt(0, 1, nc.scalar.copy)
-        quantize_h(0)
-        quantize_wt(0, 0)
-        quantize_h(1)
-        signal(2, 1, False, True)
+        scale(0)
+        scale(1)
         scale(2)
-        quantize_wt(0, 1)
-        signal(3, 1, False, True)
+        quantize_h(0, 2)
+        quantize_wt(0, 0)
+        narrow_features(0, 0, 0)
         scale(3)
-        for c in (AHEAD + 2, AHEAD + 3):
-            noise(c, 0)
-            noise(c, 1)
-        features(0, 0, SPAN)
-        quantize_h(2)
-        quantize_h(3)
-        round_wt(1, 0, nc.vector.tensor_copy, tag="h_bf0")
+        quantize_wt(0, 1)
+        narrow_features(0, 1, 1)
+        quantize_h(2, 2)
+        narrow_features(1, 0, 2)
+        narrow_features(1, 1, 3)
+        round_wt(1, 0, nc.vector.tensor_copy)
         round_wt(1, 1, nc.vector.tensor_copy)
         quantize_wt(1, 0)
         quantize_wt(1, 1)
-        signals(4)
-        backgrounds(4)
-        scale(4)
-        signals(5)
-        features(1, 0, SPAN)
-        backgrounds(5)
-        scale(5)
-        signals(6)
-        features(0, 1, HALF, range(0, 2))
-        backgrounds(6)
-        features(0, 1, HALF, range(2, PACK))
+        for c in (4, 5, 6):
+            signals(c)
+            backgrounds(c)
+            scale(c)
+        features(0, 1, 0, 0, 1)
         signals(7)
+        features(0, 1, 1, 1, 1)
+        features(0, 1, 2, 2, 1)
         backgrounds(7)
-        quantize_h(4)
-        quantize_h(5)
-        scale(6)
+        features(0, 1, 3, 3, 1)
+        quantize_h(4, 2)
+        narrow_features(2, 0, 4)
+        narrow_features(2, 1, 5)
         scale(7)
-        quantize_h(6)
-        quantize_h(7)
-        features(2, 0, SPAN)
-        features(2, 1, SPAN)
-        features(3, 0, SPAN)
-        features(3, 1, SPAN)
+        quantize_h(6, 1)
+        quantize_h(7, 1)
+        narrow_features(3, 0, 6)
+        narrow_features(3, 1, 7)
+        for t in range(PACK):
+            features(1, 1, t, t, 1)
 
-        units = [(0, 0), (1, 0), (0, 1), (1, 1), (2, 0), (2, 1), (3, 0), (3, 1)]
-        word_stores = {
-            (1, 0): (slice(0, 1), slice(0, HALF)),
-            (1, 1): (slice(1, 2), slice(0, HALF)),
-            (2, 1): (slice(0, GROUPS), slice(HALF, HALF + SPAN)),
-            (3, 1): (slice(0, GROUPS), slice(HALF + SPAN, S)),
-        }
-
-        def finish(unit):
-            quantize_y(*unit)
-            if unit in word_stores:
-                store_words(*word_stores[unit])
-
-        for i, unit in enumerate(units):
-            round_y(*unit, nc.scalar.copy if i == len(units) - 1 else nc.vector.tensor_copy)
-            if i > 0:
-                finish(units[i - 1])
-        finish(units[-1])
+        round_y(0, 1, 0, nc.vector.tensor_copy)
+        round_y(1, 1, 0, nc.vector.tensor_copy, last_noise + ALIGN * 16 - 2 * SPAN * PACK)
+        quantize_y(0, 1, 0)
+        round_y(0, 2, 1, nc.vector.tensor_copy, last_noise + ALIGN * 16)
+        quantize_y(1, 1, 0)
+        round_y(2, 2, 0, nc.vector.tensor_copy)
+        quantize_y(0, 2, 1)
+        store_words(0, slice(0, 2))
+        quantize_y(2, 2, 0)
+        store_words(1, slice(0, 1))
+        round_y(2, 1, 1, nc.vector.tensor_copy)
+        round_y(3, 1, 1, nc.scalar.copy)
+        quantize_y(2, 1, 1)
+        quantize_y(3, 1, 1)
+        store_words(1, slice(1, 2))
 
         for r in range(4):
             nc.scalar.dma_start(

@@ -29,9 +29,8 @@ HALF = 512
 BANK = 512
 LIST_ROWS = 16
 STAGED = slice(P - BLOCKS * PASSES, P)
-WQ_SC, WB_SC = S, S + H
-ROW = S + 2 * H
-BIAS_PITCH = 8
+WQ_SC, WB_SC = S, S + PASSES * H
+ROW = S + 2 * PASSES * H
 ALIGN = 64
 
 
@@ -55,22 +54,23 @@ def tile_list_hit_significance_tagging_kernel(
 
         offsets = keep.tile([P, S // LIST_ROWS], U16, name="offsets")
         sc_window = sb("sc_window", [P, T], U8)
-        nc.sync.dma_start(out=sc_window[STAGED, :].bitcast(I32), in_=tab_scales.rearrange("a q t -> q a t").bitcast(I32))
+        nc.sync.dma_start(out=sc_window[STAGED, :].bitcast(I32), in_=tab_scales.rearrange("a q t -> (a q) t").bitcast(I32))
         nc.vector.memset(sc_window[0 : STAGED.start, :].bitcast(I32), 0)
         nc.sync.dma_start(offsets[:], offs)
         stage = sb("stage", [P, ROW], U8)
         for first, w_scales in ((WQ_SC, wq_scales), (WB_SC, wb_scales)):
             nc.sync.dma_start(
-                out=stage[STAGED, first : first + H].bitcast(I32),
+                out=stage[STAGED.start : STAGED.start + BLOCKS, first : first + PASSES * H].bitcast(I32),
                 in_=w_scales.rearrange("a q c -> q a c").bitcast(I32),
             )
 
         w_bytes = 4 * PACK * H
         tab0_at = w_bytes - ALIGN
         wb_at = w_bytes
-        bias_at = wb_at + PASSES * 2 * H
-        wq1_at = bias_at + ALIGN
-        ws0_at = wq1_at + 4 * H
+        wq1_at = wb_at + PASSES * 2 * H + ALIGN
+        bias_at = [wq1_at - ALIGN, wq1_at + 4 * H, wq1_at + 4 * H + ALIGN]
+        ws0_at = bias_at[2] + ALIGN
+        words_at = {(0, 0): bias_at[0] + ALIGN - 4 * HALF, (0, 1): bias_at[1] + ALIGN - 4 * HALF, (1, 0): bias_at[2]}
         ws1_at = ws0_at + w_bytes
         last_noise = ws1_at + 2048
 
@@ -79,7 +79,7 @@ def tile_list_hit_significance_tagging_kernel(
         wq_raw = [sb("wq_raw0", [P, H], I32)]
         nc.sync.dma_start(out=wq_raw[0][:], in_=wq_words[0].rearrange("p c i -> p (c i)").bitcast(I32))
 
-        planes = sb("planes", [P, PASSES * ROW], U8)
+        planes = sb("planes", [P, ROW + S], U8)
         nc.vector.memset(planes[:].bitcast(I32), 0)
 
         def hits(first, count):
@@ -88,13 +88,19 @@ def tile_list_hit_significance_tagging_kernel(
         picked = sb("sc_picked", [P, S], U8)
         nc.vector.tensor_copy(picked[:], sc_window[:].indirect(offsets[:]))
         nc.vector.tensor_copy(stage[STAGED, 0:S].bitcast(I32), picked[STAGED, :].bitcast(I32))
-        for quad in (0, 2, 1, 3):
-            nc.sync.dma_start(
-                out=planes[32 * quad : 32 * quad + 4, :].bitcast(I32),
-                in_=stage[STAGED.start + 8 * quad : STAGED.start + 8 * quad + 8, :].bitcast(I32),
-            )
+
+        def carry(a, width):
+            first = STAGED.start + BLOCKS * a
+            for r in range(4):
+                nc.sync.dma_start(
+                    out=planes[r:P:32, a * ROW : a * ROW + width].bitcast(I32),
+                    in_=stage[first + r : first + BLOCKS : 4, 0:width].bitcast(I32),
+                )
+
+        carry(0, ROW)
         tab.append(sb("tab1", [P, T], I32, tag="sc_picked"))
         nc.sync.dma_start(out=tab[1][:], in_=tab_words[1].rearrange("p t i -> p (t i)").bitcast(I32))
+        carry(1, S)
 
         widths = [HALF, SPAN]
         v = [[None] * (S // widths[a]) for a in range(PASSES)]
@@ -113,12 +119,10 @@ def tile_list_hit_significance_tagging_kernel(
                 wq_raw[a][:].bitcast(U32).rearrange("p (c i t) -> p c t i", t=PACK, i=4),
             )
 
-        def deal_scales(a, first, count):
+        def deal_scales(first, count):
             nc.vector.tensor_copy(
-                w_sc[:, (2 * a + first) * H : (2 * a + first + count) * H].rearrange(
-                    "p (x t c i) -> p x c t i", x=count, t=PACK, i=16
-                ),
-                planes[:, a * ROW + S + first * H : a * ROW + S + (first + count) * H].rearrange(
+                w_sc[:, first * H : (first + count) * H].rearrange("p (x t c i) -> p x c t i", x=count, t=PACK, i=16),
+                planes[:, S + first * H : S + (first + count) * H].rearrange(
                     "p (x c i t) -> p x c t i", x=count, t=PACK, i=16
                 ),
             )
@@ -126,9 +130,9 @@ def tile_list_hit_significance_tagging_kernel(
         gather(0, 0)
         gather(0, 1)
         deal_wq(0, nc.vector.tensor_copy)
-        deal_scales(0, 0, 1)
-        deal_scales(1, 0, 2)
-        deal_scales(0, 1, 1)
+        deal_scales(0, 1)
+        deal_scales(1, 1)
+        deal_scales(2, 2)
 
         wq_raw.append(placed("wq_raw1", [P, H], I32, wq1_at))
         nc.sync.dma_start(out=wq_raw[1][:], in_=wq_words[1].rearrange("p c i -> p (c i)").bitcast(I32))
@@ -142,8 +146,13 @@ def tile_list_hit_significance_tagging_kernel(
             nc.sync.dma_start(out=ws_raw[a][:], in_=ws_rows[a])
         wt_raw = [placed("wt_raw0", [P, PACK, PASS_ROWS], F32, 0)]
         nc.sync.dma_start(out=wt_raw[0][:], in_=wt_rows[0])
-        bias = placed("bias", [P, GROUPS, BIAS_PITCH], F32, bias_at)
-        nc.sync.dma_start(out=bias[:, :, 0:PACK], in_=bt.rearrange("(g p t) -> p g t", g=GROUPS, t=PACK))
+        bias = {}
+        bt_rows = bt.rearrange("(g p t) -> g p t", g=GROUPS, t=PACK)
+        for at, g, first, count in ((bias_at[0], 0, 0, 4), (bias_at[1], 1, 0, 2), (bias_at[2], 1, 2, 2)):
+            piece = placed("bias%d_%d" % (g, first), [P, count], F32, at)
+            nc.sync.dma_start(out=piece[:], in_=bt_rows[g][:, first : first + count])
+            for t in range(count):
+                bias[g, first + t] = piece[:, t : t + 1]
         wt_raw.append(sb("wt_raw1", [P, PACK, PASS_ROWS], F32, tag="wq_raw0"))
         nc.sync.dma_start(out=wt_raw[1][:], in_=wt_rows[1])
 
@@ -154,9 +163,9 @@ def tile_list_hit_significance_tagging_kernel(
             )
 
         deal_wq(1, nc.scalar.copy)
-        deal_wb(0, nc.scalar.copy)
         for i in range(S // SPAN):
             gather(1, i)
+        deal_wb(0, nc.vector.tensor_copy)
         deal_wb(1, nc.vector.tensor_copy)
 
         def first_stage(acc, c, a, words, dtype, width, scales, start, stop):
@@ -182,7 +191,7 @@ def tile_list_hit_significance_tagging_kernel(
         def noise(c, a):
             if a == 0:
                 q_acc[c] = bank(c)
-            first_stage(q_acc[c], c, a, wq[a][:], FP8X4, P, w_sc[:, 2 * a * H : (2 * a + 1) * H], a == 0, a == PASSES - 1)
+            first_stage(q_acc[c], c, a, wq[a][:], FP8X4, P, w_sc[:, a * H : (a + 1) * H], a == 0, a == PASSES - 1)
 
         def exponential(c):
             if c >= CHUNKS - 2:
@@ -233,14 +242,14 @@ def tile_list_hit_significance_tagging_kernel(
         h_words = [sb("h_words%d" % half, [P, HALF], U32) for half in range(S // HALF)]
         h_sc = [sb("h_sc%d" % half, [P, HALF], U8) for half in range(S // HALF)]
         y_sc = sb("y_sc", [P, GROUPS, S], U8)
-        y_words = sb("y_words", [P, GROUPS, S], U32)
+        y_words = {}
         y = {}
         y_bf = {}
 
         def background(c, a, start, stop):
             if start:
                 d_acc[c] = bank(c)
-            first_stage(d_acc[c], c, a, wb[a][:], FP4X4, 2 * P, w_sc[:, (2 * a + 1) * H : (2 * a + 2) * H], start, stop)
+            first_stage(d_acc[c], c, a, wb[a][:], FP4X4, 2 * P, w_sc[:, (PASSES + a) * H : (PASSES + a + 1) * H], start, stop)
 
         def signal(c, a, start, stop):
             if start:
@@ -275,8 +284,14 @@ def tile_list_hit_significance_tagging_kernel(
                 in_=h_bf[half][:, o * PACK : (o + w) * PACK],
             )
 
-        def features(half, g, t, b, stored):
-            if t == 0:
+        def bias_on_scalar(dst, acc, column):
+            nc.scalar.activation(out=dst, in_=acc, func=ACT.Identity, bias=column)
+
+        def bias_on_vector(dst, acc, column):
+            nc.vector.tensor_scalar(out=dst, in0=acc, scalar1=column, scalar2=None, op0=ALU.add)
+
+        def features(half, g, t, b, add_bias):
+            if (half, g) not in y:
                 y[half, g] = sb("y%d_%d" % (half, g), [P, PACK, HALF], F32)
             acc = bank(b)
             nc.tensor.matmul_mx(
@@ -288,13 +303,9 @@ def tile_list_hit_significance_tagging_kernel(
                 start=True,
                 stop=True,
             )
-            nc.scalar.activation(out=y[half, g][:, t, :], in_=acc[:], func=ACT.Identity, bias=bias[:, g, t : t + 1])
-            if stored:
-                rows_out = out_0[PASS_ROWS * g : PASS_ROWS * (g + 1), half * HALF : (half + 1) * HALF]
-                nc.sync.dma_start(
-                    out=rows_out.rearrange("(p t) j -> p t j", t=PACK)[:, t + 1 - stored : t + 1, :],
-                    in_=y[half, g][:, t + 1 - stored : t + 1, :],
-                )
+            add_bias(y[half, g][:, t, :], acc[:], bias[g, t])
+            rows_out = out_0[PASS_ROWS * g : PASS_ROWS * (g + 1), half * HALF : (half + 1) * HALF]
+            nc.sync.dma_start(out=rows_out.rearrange("(p t) j -> p t j", t=PACK)[:, t, :], in_=y[half, g][:, t, :])
 
         def narrow_features(s, u, b):
             half, o = divmod(s * SPAN, HALF)
@@ -319,7 +330,7 @@ def tile_list_hit_significance_tagging_kernel(
                     out=y[half, 0][:, t, cols],
                     in_=acc[:, place * SPAN : (place + 1) * SPAN],
                     func=ACT.Identity,
-                    bias=bias[:, 0, t : t + 1],
+                    bias=bias[0, t],
                 )
             nc.sync.dma_start(
                 out=out_0[0:PASS_ROWS, s * SPAN : (s + 1) * SPAN].rearrange("(p t) j -> p t j", t=PACK)[
@@ -342,17 +353,23 @@ def tile_list_hit_significance_tagging_kernel(
 
         def quantize_y(s, w, g):
             cols = slice(s * SPAN, (s + w) * SPAN)
+            half, o = divmod(s * SPAN, HALF)
+            if (half, g) not in y_words:
+                name = "y_words%d_%d" % (half, g)
+                if (half, g) in words_at:
+                    y_words[half, g] = placed(name, [P, HALF], U32, words_at[half, g])
+                else:
+                    y_words[half, g] = sb(name, [P, HALF], U32)
             nc.vector.quantize_mx(
-                out=y_words[:, g, cols].bitcast(FP8X4),
+                out=y_words[half, g][:, o : o + w * SPAN].bitcast(FP8X4),
                 scales=y_sc[:, g, cols],
                 in_=y_bf[s, g][:].rearrange("p j t -> p (j t)"),
             )
 
-        def store_words(half, groups):
-            cols = slice(half * HALF, (half + 1) * HALF)
+        def store_words(half, g):
             nc.sync.dma_start(
-                out=out_1.rearrange("g p m t -> p g (m t)").bitcast(I32)[:, groups, cols],
-                in_=y_words[:, groups, cols].bitcast(I32),
+                out=out_1[g].rearrange("p m t -> p (m t)").bitcast(I32)[:, half * HALF : (half + 1) * HALF],
+                in_=y_words[half, g][:].bitcast(I32),
             )
 
         for c in range(CHUNKS):
@@ -404,12 +421,12 @@ def tile_list_hit_significance_tagging_kernel(
             signals(c)
             backgrounds(c)
             scale(c)
-        features(0, 1, 0, 0, 1)
+        features(0, 1, 0, 0, bias_on_scalar)
         signals(7)
-        features(0, 1, 1, 1, 1)
-        features(0, 1, 2, 2, 1)
+        features(0, 1, 1, 1, bias_on_scalar)
+        features(0, 1, 2, 2, bias_on_scalar)
         backgrounds(7)
-        features(0, 1, 3, 3, 1)
+        features(0, 1, 3, 3, bias_on_scalar)
         quantize_h(4, 2)
         narrow_features(2, 0, 4)
         narrow_features(2, 1, 5)
@@ -418,24 +435,26 @@ def tile_list_hit_significance_tagging_kernel(
         quantize_h(7, 1)
         narrow_features(3, 0, 6)
         narrow_features(3, 1, 7)
-        for t in range(PACK):
-            features(1, 1, t, t, 1)
-
         round_y(0, 1, 0, nc.vector.tensor_copy)
         round_y(1, 1, 0, nc.vector.tensor_copy, last_noise + ALIGN * 16 - 2 * SPAN * PACK)
-        quantize_y(0, 1, 0)
         round_y(0, 2, 1, nc.vector.tensor_copy, last_noise + ALIGN * 16)
+        features(1, 1, 3, 3, bias_on_vector)
+        for t in range(PACK - 1):
+            features(1, 1, t, t, bias_on_scalar)
+
+        quantize_y(0, 1, 0)
         quantize_y(1, 1, 0)
+        store_words(0, 0)
         round_y(2, 2, 0, nc.vector.tensor_copy)
         quantize_y(0, 2, 1)
-        store_words(0, slice(0, 2))
+        store_words(0, 1)
         quantize_y(2, 2, 0)
-        store_words(1, slice(0, 1))
+        store_words(1, 0)
         round_y(2, 1, 1, nc.vector.tensor_copy)
         round_y(3, 1, 1, nc.scalar.copy)
         quantize_y(2, 1, 1)
         quantize_y(3, 1, 1)
-        store_words(1, slice(1, 2))
+        store_words(1, 1)
 
         for r in range(4):
             nc.scalar.dma_start(

@@ -24,7 +24,9 @@ GROUPS = N // PASS_ROWS
 BLOCKS = PASS_ROWS // 32
 CHUNK = 128
 CHUNKS = S // CHUNK
+RUN = 2
 SPAN = 256
+SPANS = S // SPAN
 HALF = 512
 BANK = 512
 LIST_ROWS = 16
@@ -57,10 +59,10 @@ def tile_list_hit_significance_tagging_kernel(
         nc.sync.dma_start(out=sc_window[STAGED, :].bitcast(I32), in_=tab_scales.rearrange("a q t -> (a q) t").bitcast(I32))
         nc.vector.memset(sc_window[0 : STAGED.start, :].bitcast(I32), 0)
         nc.sync.dma_start(offsets[:], offs)
-        stage = sb("stage", [P, ROW], U8)
+        stage = [sb("stage0", [P, ROW], U8), sb("stage1", [P, S], U8)]
         for first, w_scales in ((WQ_SC, wq_scales), (WB_SC, wb_scales)):
             nc.sync.dma_start(
-                out=stage[STAGED.start : STAGED.start + BLOCKS, first : first + PASSES * H].bitcast(I32),
+                out=stage[0][STAGED.start : STAGED.start + BLOCKS, first : first + PASSES * H].bitcast(I32),
                 in_=w_scales.rearrange("a q c -> q a c").bitcast(I32),
             )
 
@@ -87,14 +89,15 @@ def tile_list_hit_significance_tagging_kernel(
 
         picked = sb("sc_picked", [P, S], U8)
         nc.vector.tensor_copy(picked[:], sc_window[:].indirect(offsets[:]))
-        nc.vector.tensor_copy(stage[STAGED, 0:S].bitcast(I32), picked[STAGED, :].bitcast(I32))
+        for a in range(PASSES):
+            nc.vector.tensor_copy(stage[a][STAGED, 0:S].bitcast(I32), picked[STAGED, :].bitcast(I32))
 
         def carry(a, width):
             first = STAGED.start + BLOCKS * a
             for r in range(4):
                 nc.sync.dma_start(
                     out=planes[r:P:32, a * ROW : a * ROW + width].bitcast(I32),
-                    in_=stage[first + r : first + BLOCKS : 4, 0:width].bitcast(I32),
+                    in_=stage[a][first + r : first + BLOCKS : 4, 0:width].bitcast(I32),
                 )
 
         carry(0, ROW)
@@ -106,7 +109,7 @@ def tile_list_hit_significance_tagging_kernel(
         v = [[None] * (S // widths[a]) for a in range(PASSES)]
 
         def gather(a, i):
-            v[a][i] = sb("v%d_%d" % (a, i), [P, widths[a]], U32)
+            v[a][i] = sb("v%d_%d" % (a, i), [P, widths[a]], U32, tag="stage0" if (a, i) == (0, 1) else None)
             nc.vector.tensor_copy(v[a][i][:], tab[a][:].bitcast(U32).indirect(hits(i * widths[a], widths[a])))
 
         wq = [sb("wq%d" % a, [P, H], I32) for a in range(PASSES)]
@@ -128,9 +131,9 @@ def tile_list_hit_significance_tagging_kernel(
             )
 
         gather(0, 0)
-        gather(0, 1)
         deal_wq(0, nc.vector.tensor_copy)
         deal_scales(0, 1)
+        gather(0, 1)
         deal_scales(1, 1)
         deal_scales(2, 2)
 
@@ -181,24 +184,38 @@ def tile_list_hit_significance_tagging_kernel(
                     stop=stop and t == PACK - 1,
                 )
 
-        def hit_major(acc):
-            return acc[:].rearrange("p (t j) -> p j t", t=PACK)
-
         q_acc = {}
         d_acc = {}
         inv_noise = {}
 
-        def noise(c, a):
-            if a == 0:
-                q_acc[c] = bank(c)
-            first_stage(q_acc[c], c, a, wq[a][:], FP8X4, P, w_sc[:, a * H : (a + 1) * H], a == 0, a == PASSES - 1)
+        def noise(s, a):
+            i, o = divmod(s * SPAN, widths[a])
+            for t in range(PACK):
+                u, place = divmod(t, 2)
+                if a == 0 and place == 0:
+                    q_acc[s, u] = bank(2 * s + u)
+                nc.tensor.matmul_mx(
+                    out=q_acc[s, u][:, place * SPAN : (place + 1) * SPAN],
+                    lhsT=wq[a][:, t * P : (t + 1) * P].bitcast(FP8X4),
+                    lhsT_scale=w_sc[:, a * H + t * P : a * H + (t + 1) * P],
+                    rhs=v[a][i][:, o : o + SPAN].bitcast(FP8X4),
+                    rhs_scale=planes[:, a * ROW + s * SPAN : a * ROW + (s + 1) * SPAN],
+                    start=a == 0 and place == 0,
+                    stop=a == PASSES - 1 and place == 1,
+                )
 
-        def exponential(c):
-            if c >= CHUNKS - 2:
-                inv_noise[c] = placed("inv_noise%d" % c, [P, CHUNK, PACK], F32, last_noise + (CHUNKS - 1 - c) * 5120)
+        def exponentials(s):
+            if s == SPANS - 1:
+                inv_noise[s] = placed("inv_noise%d" % s, [P, PACK, SPAN], F32, last_noise)
             else:
-                inv_noise[c] = sb("inv_noise%d" % c, [P, CHUNK, PACK], F32)
-            nc.scalar.activation(out=inv_noise[c][:], in_=hit_major(q_acc[c]), func=ACT.Exp, scale=-1.0)
+                inv_noise[s] = sb("inv_noise%d" % s, [P, PACK, SPAN], F32)
+            for u in range(2):
+                nc.scalar.activation(
+                    out=inv_noise[s][:, 2 * u : 2 * u + 2, :].rearrange("p t j -> p (t j)"),
+                    in_=q_acc[s, u][:],
+                    func=ACT.Exp,
+                    scale=-1.0,
+                )
 
         def dealt(rounded, raw, u):
             return (
@@ -266,13 +283,12 @@ def tile_list_hit_significance_tagging_kernel(
 
         def scale(c):
             half, o = divmod(c * CHUNK, HALF)
-            nc.vector.scalar_tensor_tensor(
-                out=h_bf[half][:, o * PACK : (o + CHUNK) * PACK].rearrange("p (j t) -> p j t", t=PACK),
-                in0=hit_major(d_acc[c]),
-                scalar=-1.0,
-                in1=inv_noise[c][:],
-                op0=ALU.mult,
-                op1=ALU.mult,
+            s, i = divmod(c * CHUNK, SPAN)
+            nc.vector.tensor_tensor(
+                h_bf[half][:, o * PACK : (o + CHUNK) * PACK].rearrange("p (c i t) -> p c t i", t=PACK, i=RUN),
+                d_acc[c][:].rearrange("p (t c i) -> p c t i", t=PACK, i=RUN),
+                inv_noise[s][:, :, i : i + CHUNK].rearrange("p t (c i) -> p c t i", i=RUN),
+                ALU.mult,
             )
 
         def quantize_h(c, count):
@@ -372,20 +388,19 @@ def tile_list_hit_significance_tagging_kernel(
                 in_=y_words[half, g][:].bitcast(I32),
             )
 
-        for c in range(CHUNKS):
-            noise(c, 0)
-        for c in range(CHUNKS):
-            noise(c, 1)
-            if c < CHUNKS - 2:
-                exponential(c)
+        for s in range(SPANS):
+            noise(s, 0)
+        for s in range(SPANS):
+            noise(s, 1)
+            if s < SPANS - 1:
+                exponentials(s)
         for u in range(2):
             round_ws(0, u, negate_on_vector)
         for u in range(2):
             quantize_ws(0, u)
         round_ws(1, 0, negate_on_vector)
         round_ws(1, 1, negate_on_scalar)
-        exponential(CHUNKS - 2)
-        exponential(CHUNKS - 1)
+        exponentials(SPANS - 1)
         for u in range(2):
             quantize_ws(1, u)
         first = range(CHUNKS // 2)
@@ -399,8 +414,8 @@ def tile_list_hit_significance_tagging_kernel(
             signal(c, 1, False, True)
         signal(3, 1, False, False)
         signal(3, 0, False, True)
-        round_wt(0, 0, nc.scalar.copy)
-        round_wt(0, 1, nc.scalar.copy)
+        round_wt(0, 0, negate_on_scalar)
+        round_wt(0, 1, negate_on_scalar)
         scale(0)
         scale(1)
         scale(2)
@@ -413,8 +428,8 @@ def tile_list_hit_significance_tagging_kernel(
         quantize_h(2, 2)
         narrow_features(1, 0, 2)
         narrow_features(1, 1, 3)
-        round_wt(1, 0, nc.vector.tensor_copy)
-        round_wt(1, 1, nc.vector.tensor_copy)
+        round_wt(1, 0, negate_on_vector)
+        round_wt(1, 1, negate_on_vector)
         quantize_wt(1, 0)
         quantize_wt(1, 1)
         for c in (4, 5, 6):

@@ -34,6 +34,7 @@ STAGED = slice(P - BLOCKS * PASSES, P)
 WQ_SC, WB_SC = S, S + PASSES * H
 ROW = S + 2 * PASSES * H
 ALIGN = 64
+BIAS_PITCH = 8
 
 
 def tile_list_hit_significance_tagging_kernel(
@@ -69,10 +70,9 @@ def tile_list_hit_significance_tagging_kernel(
         w_bytes = 4 * PACK * H
         tab0_at = w_bytes - ALIGN
         wb_at = w_bytes
-        wq1_at = wb_at + PASSES * 2 * H + ALIGN
-        bias_at = [wq1_at - ALIGN, wq1_at + 4 * H, wq1_at + 4 * H + ALIGN]
-        ws0_at = bias_at[2] + ALIGN
-        words_at = {(0, 0): bias_at[0] + ALIGN - 4 * HALF, (0, 1): bias_at[1] + ALIGN - 4 * HALF, (1, 0): bias_at[2]}
+        bias_at = wb_at + PASSES * 2 * H
+        wq1_at = bias_at + ALIGN
+        ws0_at = wq1_at + 4 * H
         ws1_at = ws0_at + w_bytes
         last_noise = ws1_at + 2048
 
@@ -149,13 +149,8 @@ def tile_list_hit_significance_tagging_kernel(
             nc.sync.dma_start(out=ws_raw[a][:], in_=ws_rows[a])
         wt_raw = [placed("wt_raw0", [P, PACK, PASS_ROWS], F32, 0)]
         nc.sync.dma_start(out=wt_raw[0][:], in_=wt_rows[0])
-        bias = {}
-        bt_rows = bt.rearrange("(g p t) -> g p t", g=GROUPS, t=PACK)
-        for at, g, first, count in ((bias_at[0], 0, 0, 4), (bias_at[1], 1, 0, 2), (bias_at[2], 1, 2, 2)):
-            piece = placed("bias%d_%d" % (g, first), [P, count], F32, at)
-            nc.sync.dma_start(out=piece[:], in_=bt_rows[g][:, first : first + count])
-            for t in range(count):
-                bias[g, first + t] = piece[:, t : t + 1]
+        bias = placed("bias", [P, GROUPS, BIAS_PITCH], F32, bias_at)
+        nc.sync.dma_start(out=bias[:, :, 0:PACK], in_=bt.rearrange("(g p t) -> p g t", g=GROUPS, t=PACK))
         wt_raw.append(sb("wt_raw1", [P, PACK, PASS_ROWS], F32, tag="wq_raw0"))
         nc.sync.dma_start(out=wt_raw[1][:], in_=wt_rows[1])
 
@@ -259,7 +254,7 @@ def tile_list_hit_significance_tagging_kernel(
         h_words = [sb("h_words%d" % half, [P, HALF], U32) for half in range(S // HALF)]
         h_sc = [sb("h_sc%d" % half, [P, HALF], U8) for half in range(S // HALF)]
         y_sc = sb("y_sc", [P, GROUPS, S], U8)
-        y_words = {}
+        y_words = sb("y_words", [P, GROUPS, S], U32)
         y = {}
         y_bf = {}
 
@@ -300,92 +295,61 @@ def tile_list_hit_significance_tagging_kernel(
                 in_=h_bf[half][:, o * PACK : (o + w) * PACK],
             )
 
-        def bias_on_scalar(dst, acc, column):
-            nc.scalar.activation(out=dst, in_=acc, func=ACT.Identity, bias=column)
-
-        def bias_on_vector(dst, acc, column):
-            nc.vector.tensor_scalar(out=dst, in0=acc, scalar1=column, scalar2=None, op0=ALU.add)
-
-        def features(half, g, t, b, add_bias):
+        def features(g, first, width, slices, b):
+            half, o = divmod(first, HALF)
             if (half, g) not in y:
                 y[half, g] = sb("y%d_%d" % (half, g), [P, PACK, HALF], F32)
             acc = bank(b)
-            nc.tensor.matmul_mx(
-                out=acc[:],
-                lhsT=wt_words[g][:, t * P : (t + 1) * P].bitcast(FP8X4),
-                lhsT_scale=wt_sc[g][:, t * P : (t + 1) * P],
-                rhs=h_words[half][:].bitcast(FP8X4),
-                rhs_scale=h_sc[half][:],
-                start=True,
-                stop=True,
-            )
-            add_bias(y[half, g][:, t, :], acc[:], bias[g, t])
-            rows_out = out_0[PASS_ROWS * g : PASS_ROWS * (g + 1), half * HALF : (half + 1) * HALF]
-            nc.sync.dma_start(out=rows_out.rearrange("(p t) j -> p t j", t=PACK)[:, t, :], in_=y[half, g][:, t, :])
-
-        def narrow_features(s, u, b):
-            half, o = divmod(s * SPAN, HALF)
-            if (half, 0) not in y:
-                y[half, 0] = sb("y%d_0" % half, [P, PACK, HALF], F32)
-            acc = bank(b)
-            cols = slice(o, o + SPAN)
-            for place in range(2):
-                t = 2 * u + place
+            cols = slice(o, o + width)
+            for place, t in enumerate(slices):
                 nc.tensor.matmul_mx(
-                    out=acc[:, place * SPAN : (place + 1) * SPAN],
-                    lhsT=wt_words[0][:, t * P : (t + 1) * P].bitcast(FP8X4),
-                    lhsT_scale=wt_sc[0][:, t * P : (t + 1) * P],
+                    out=acc[:, place * width : (place + 1) * width],
+                    lhsT=wt_words[g][:, t * P : (t + 1) * P].bitcast(FP8X4),
+                    lhsT_scale=wt_sc[g][:, t * P : (t + 1) * P],
                     rhs=h_words[half][:, cols].bitcast(FP8X4),
                     rhs_scale=h_sc[half][:, cols],
                     start=True,
                     stop=True,
                 )
-            for place in range(2):
-                t = 2 * u + place
+            for place, t in enumerate(slices):
                 nc.scalar.activation(
-                    out=y[half, 0][:, t, cols],
-                    in_=acc[:, place * SPAN : (place + 1) * SPAN],
+                    out=y[half, g][:, t, cols],
+                    in_=acc[:, place * width : (place + 1) * width],
                     func=ACT.Identity,
-                    bias=bias[0, t],
+                    bias=bias[:, g, t : t + 1],
                 )
+            rows_out = out_0[PASS_ROWS * g : PASS_ROWS * (g + 1), first : first + width]
             nc.sync.dma_start(
-                out=out_0[0:PASS_ROWS, s * SPAN : (s + 1) * SPAN].rearrange("(p t) j -> p t j", t=PACK)[
-                    :, 2 * u : 2 * u + 2, :
-                ],
-                in_=y[half, 0][:, 2 * u : 2 * u + 2, cols],
+                out=rows_out.rearrange("(p t) j -> p t j", t=PACK)[:, slices.start : slices.stop, :],
+                in_=y[half, g][:, slices.start : slices.stop, cols],
             )
 
-        def round_y(s, w, g, copy, offset=None):
+        def narrow(g, s, u, b):
+            features(g, s * SPAN, SPAN, range(2 * u, 2 * u + 2), b)
+
+        def wide(g, half, t, b):
+            features(g, half * HALF, HALF, range(t, t + 1), b)
+
+        def round_y(g, s, w, copy, tag=None):
             half, o = divmod(s * SPAN, HALF)
-            name = "y_bf%d_%d" % (s, g)
-            if offset is None:
-                y_bf[s, g] = sb(name, [P, w * SPAN, PACK], BF16)
-            else:
-                y_bf[s, g] = placed(name, [P, w * SPAN, PACK], BF16, offset)
+            y_bf[g, s] = sb("y_bf%d_%d" % (g, s), [P, w * SPAN, PACK], BF16, tag=tag)
             copy(
-                y_bf[s, g][:].rearrange("p (c i) t -> p c t i", i=4),
+                y_bf[g, s][:].rearrange("p (c i) t -> p c t i", i=4),
                 y[half, g][:, :, o : o + w * SPAN].rearrange("p t (c i) -> p c t i", i=4),
             )
 
-        def quantize_y(s, w, g):
+        def quantize_y(g, s, w):
             cols = slice(s * SPAN, (s + w) * SPAN)
-            half, o = divmod(s * SPAN, HALF)
-            if (half, g) not in y_words:
-                name = "y_words%d_%d" % (half, g)
-                if (half, g) in words_at:
-                    y_words[half, g] = placed(name, [P, HALF], U32, words_at[half, g])
-                else:
-                    y_words[half, g] = sb(name, [P, HALF], U32)
             nc.vector.quantize_mx(
-                out=y_words[half, g][:, o : o + w * SPAN].bitcast(FP8X4),
+                out=y_words[:, g, cols].bitcast(FP8X4),
                 scales=y_sc[:, g, cols],
-                in_=y_bf[s, g][:].rearrange("p j t -> p (j t)"),
+                in_=y_bf[g, s][:].rearrange("p j t -> p (j t)"),
             )
 
-        def store_words(half, g):
+        def store_words(groups, cols):
             nc.sync.dma_start(
-                out=out_1[g].rearrange("p m t -> p (m t)").bitcast(I32)[:, half * HALF : (half + 1) * HALF],
-                in_=y_words[half, g][:].bitcast(I32),
+                out=out_1.rearrange("g p m t -> p g (m t)").bitcast(I32)[:, groups, cols],
+                in_=y_words[:, groups, cols].bitcast(I32),
             )
 
         for s in range(SPANS):
@@ -421,55 +385,59 @@ def tile_list_hit_significance_tagging_kernel(
         scale(2)
         quantize_h(0, 2)
         quantize_wt(0, 0)
-        narrow_features(0, 0, 0)
+        narrow(0, 0, 0, 0)
         scale(3)
         quantize_wt(0, 1)
-        narrow_features(0, 1, 1)
+        narrow(0, 0, 1, 1)
         quantize_h(2, 2)
-        narrow_features(1, 0, 2)
-        narrow_features(1, 1, 3)
+        narrow(0, 1, 0, 2)
+        narrow(0, 1, 1, 3)
         round_wt(1, 0, negate_on_vector)
         round_wt(1, 1, negate_on_vector)
         quantize_wt(1, 0)
         quantize_wt(1, 1)
-        for c in (4, 5, 6):
+        for c in (4, 5):
             signals(c)
             backgrounds(c)
             scale(c)
-        features(0, 1, 0, 0, bias_on_scalar)
-        signals(7)
-        features(0, 1, 1, 1, bias_on_scalar)
-        features(0, 1, 2, 2, bias_on_scalar)
-        backgrounds(7)
-        features(0, 1, 3, 3, bias_on_scalar)
+        round_y(0, 0, 1, nc.vector.tensor_copy)
         quantize_h(4, 2)
-        narrow_features(2, 0, 4)
-        narrow_features(2, 1, 5)
+        round_y(0, 1, 1, nc.vector.tensor_copy)
+        signals(6)
+        backgrounds(6)
+        wide(1, 0, 0, 0)
+        wide(1, 0, 1, 1)
+        signals(7)
+        wide(1, 0, 2, 2)
+        wide(1, 0, 3, 3)
+        narrow(0, 2, 0, 4)
+        narrow(0, 2, 1, 5)
+        backgrounds(7)
+        narrow(1, 2, 0, 0)
+        narrow(1, 2, 1, 1)
+        scale(6)
+        quantize_y(0, 0, 1)
         scale(7)
-        quantize_h(6, 1)
-        quantize_h(7, 1)
-        narrow_features(3, 0, 6)
-        narrow_features(3, 1, 7)
-        round_y(0, 1, 0, nc.vector.tensor_copy)
-        round_y(1, 1, 0, nc.vector.tensor_copy, last_noise + ALIGN * 16 - 2 * SPAN * PACK)
-        round_y(0, 2, 1, nc.vector.tensor_copy, last_noise + ALIGN * 16)
-        features(1, 1, 3, 3, bias_on_vector)
-        for t in range(PACK - 1):
-            features(1, 1, t, t, bias_on_scalar)
-
-        quantize_y(0, 1, 0)
-        quantize_y(1, 1, 0)
-        store_words(0, 0)
-        round_y(2, 2, 0, nc.vector.tensor_copy)
+        quantize_y(0, 1, 1)
+        store_words(slice(0, 1), slice(0, HALF))
+        quantize_h(6, 2)
+        narrow(0, 3, 0, 2)
+        narrow(0, 3, 1, 3)
+        narrow(1, 3, 0, 6)
+        narrow(1, 3, 1, 7)
+        round_y(1, 0, 2, nc.vector.tensor_copy, tag="h_bf1")
+        round_y(0, 2, 1, nc.vector.tensor_copy, tag="y_bf0_1")
+        quantize_y(1, 0, 2)
+        store_words(slice(1, 2), slice(0, HALF))
+        round_y(1, 2, 1, nc.vector.tensor_copy)
         quantize_y(0, 2, 1)
-        store_words(0, 1)
-        quantize_y(2, 2, 0)
-        store_words(1, 0)
-        round_y(2, 1, 1, nc.vector.tensor_copy)
-        round_y(3, 1, 1, nc.scalar.copy)
-        quantize_y(2, 1, 1)
-        quantize_y(3, 1, 1)
-        store_words(1, 1)
+        round_y(0, 3, 1, nc.vector.tensor_copy)
+        quantize_y(1, 2, 1)
+        store_words(slice(0, GROUPS), slice(HALF, HALF + SPAN))
+        round_y(1, 3, 1, nc.scalar.copy)
+        quantize_y(0, 3, 1)
+        quantize_y(1, 3, 1)
+        store_words(slice(0, GROUPS), slice(HALF + SPAN, S))
 
         for r in range(4):
             nc.scalar.dma_start(

@@ -24,7 +24,7 @@ GROUPS = N // PASS_ROWS
 BLOCKS = PASS_ROWS // 32
 CHUNK = 128
 CHUNKS = S // CHUNK
-RUN = 2
+RUN = 4
 SPAN = 256
 SPANS = S // SPAN
 HALF = 512

@@ -34,6 +34,8 @@ STAGED = slice(P - BLOCKS * PASSES, P)
 WQ_SC, WB_SC = S, S + PASSES * H
 ROW = S + 2 * PASSES * H
 ALIGN = 64
+MID = 128
+LAST = 128
 BIAS_PITCH = 8
 
 
@@ -250,7 +252,7 @@ def tile_list_hit_significance_tagging_kernel(
         def quantize_wt(g, u):
             quantize_pair(wt_words[g], wt_sc[g], wt_bf[g, u], u)
 
-        h_bf = [sb("h_bf%d" % half, [P, HALF * PACK], BF16) for half in range(S // HALF)]
+        h_bf = [sb("h_bf%d" % s, [P, SPAN * PACK], BF16) for s in range(SPANS)]
         h_words = [sb("h_words%d" % half, [P, HALF], U32) for half in range(S // HALF)]
         h_sc = [sb("h_sc%d" % half, [P, HALF], U8) for half in range(S // HALF)]
         y_sc = sb("y_sc", [P, GROUPS, S], U8)
@@ -277,12 +279,11 @@ def tile_list_hit_significance_tagging_kernel(
             background(c, 1, False, True)
 
         def scale(c):
-            half, o = divmod(c * CHUNK, HALF)
             s, i = divmod(c * CHUNK, SPAN)
             nc.vector.tensor_tensor(
-                h_bf[half][:, o * PACK : (o + CHUNK) * PACK].rearrange("p (c i t) -> p c t i", t=PACK, i=RUN),
-                d_acc[c][:].rearrange("p (t c i) -> p c t i", t=PACK, i=RUN),
+                h_bf[s][:, i * PACK : (i + CHUNK) * PACK].rearrange("p (c i t) -> p c t i", t=PACK, i=RUN),
                 inv_noise[s][:, :, i : i + CHUNK].rearrange("p t (c i) -> p c t i", i=RUN),
+                d_acc[c][:].rearrange("p (t c i) -> p c t i", t=PACK, i=RUN),
                 ALU.mult,
             )
 
@@ -292,7 +293,7 @@ def tile_list_hit_significance_tagging_kernel(
             nc.vector.quantize_mx(
                 out=h_words[half][:, o : o + w].bitcast(FP8X4),
                 scales=h_sc[half][:, o : o + w],
-                in_=h_bf[half][:, o * PACK : (o + w) * PACK],
+                in_=h_bf[c // 2][:],
             )
 
         def features(g, first, width, slices, b):
@@ -330,20 +331,22 @@ def tile_list_hit_significance_tagging_kernel(
         def wide(g, half, t, b):
             features(g, half * HALF, HALF, range(t, t + 1), b)
 
-        def round_y(g, s, w, copy, tag=None):
-            half, o = divmod(s * SPAN, HALF)
-            y_bf[g, s] = sb("y_bf%d_%d" % (g, s), [P, w * SPAN, PACK], BF16, tag=tag)
+        def round_y(g, first, width, copy, tag=None, part=None):
+            half, o = divmod(first, HALF)
+            if (g, first) not in y_bf:
+                y_bf[g, first] = sb("y_bf%d_%d" % (g, first), [P, width, PACK], BF16, tag=tag)
+            part = part or range(width)
             copy(
-                y_bf[g, s][:].rearrange("p (c i) t -> p c t i", i=4),
-                y[half, g][:, :, o : o + w * SPAN].rearrange("p t (c i) -> p c t i", i=4),
+                y_bf[g, first][:, part.start : part.stop, :].rearrange("p (c i) t -> p c t i", i=4),
+                y[half, g][:, :, o + part.start : o + part.stop].rearrange("p t (c i) -> p c t i", i=4),
             )
 
-        def quantize_y(g, s, w):
-            cols = slice(s * SPAN, (s + w) * SPAN)
+        def quantize_y(g, first, width):
+            cols = slice(first, first + width)
             nc.vector.quantize_mx(
                 out=y_words[:, g, cols].bitcast(FP8X4),
                 scales=y_sc[:, g, cols],
-                in_=y_bf[g, s][:].rearrange("p j t -> p (j t)"),
+                in_=y_bf[g, first][:].rearrange("p j t -> p (j t)"),
             )
 
         def store_words(groups, cols):
@@ -392,51 +395,59 @@ def tile_list_hit_significance_tagging_kernel(
         quantize_h(2, 2)
         narrow(0, 1, 0, 2)
         narrow(0, 1, 1, 3)
+        round_y(0, 1 * SPAN, 1 * SPAN, nc.scalar.copy, part=range(MID))
         round_wt(1, 0, negate_on_vector)
         round_wt(1, 1, negate_on_vector)
         quantize_wt(1, 0)
         quantize_wt(1, 1)
-        for c in (4, 5):
-            signals(c)
-            backgrounds(c)
-            scale(c)
-        round_y(0, 0, 1, nc.vector.tensor_copy)
-        quantize_h(4, 2)
-        round_y(0, 1, 1, nc.vector.tensor_copy)
-        signals(6)
-        backgrounds(6)
+        round_y(0, 0 * SPAN, 1 * SPAN, nc.vector.tensor_copy, tag="wt_bf1_1")
+        signals(4)
+        backgrounds(4)
+        scale(4)
+        round_y(0, 1 * SPAN, 1 * SPAN, nc.vector.tensor_copy, part=range(MID, SPAN))
+        quantize_y(0, 0 * SPAN, 1 * SPAN)
+        store_words(slice(0, 1), slice(0, SPAN))
         wide(1, 0, 0, 0)
         wide(1, 0, 1, 1)
-        signals(7)
+        signals(5)
+        backgrounds(5)
+        scale(5)
+        quantize_y(0, 1 * SPAN, 1 * SPAN)
+        store_words(slice(0, 1), slice(SPAN, HALF))
+        quantize_h(4, 2)
         wide(1, 0, 2, 2)
+        signals(6)
         wide(1, 0, 3, 3)
+        backgrounds(6)
+        signals(7)
+        backgrounds(7)
         narrow(0, 2, 0, 4)
         narrow(0, 2, 1, 5)
-        backgrounds(7)
         narrow(1, 2, 0, 0)
         narrow(1, 2, 1, 1)
+        y_bf[1, 0] = sb("y_bf1_0", [P, SPAN, PACK], BF16, tag="h_bf2")
+        nc.gpsimd.tensor_copy(y_bf[1, 0][:], y[0, 1][:, :, 0:SPAN].rearrange("p t j -> p j t"))
         scale(6)
-        quantize_y(0, 0, 1)
         scale(7)
-        quantize_y(0, 1, 1)
-        store_words(slice(0, 1), slice(0, HALF))
         quantize_h(6, 2)
         narrow(0, 3, 0, 2)
         narrow(0, 3, 1, 3)
         narrow(1, 3, 0, 6)
         narrow(1, 3, 1, 7)
-        round_y(1, 0, 2, nc.vector.tensor_copy, tag="h_bf1")
-        round_y(0, 2, 1, nc.vector.tensor_copy, tag="y_bf0_1")
-        quantize_y(1, 0, 2)
+        round_y(1, SPAN, SPAN, nc.vector.tensor_copy, tag="h_bf3")
+        quantize_y(1, 0, SPAN)
+        round_y(0, 2 * SPAN, 1 * SPAN, nc.vector.tensor_copy, tag="h_bf2")
+        quantize_y(1, SPAN, SPAN)
         store_words(slice(1, 2), slice(0, HALF))
-        round_y(1, 2, 1, nc.vector.tensor_copy)
-        quantize_y(0, 2, 1)
-        round_y(0, 3, 1, nc.vector.tensor_copy)
-        quantize_y(1, 2, 1)
+        round_y(1, 2 * SPAN, 1 * SPAN, nc.vector.tensor_copy)
+        quantize_y(0, 2 * SPAN, 1 * SPAN)
+        round_y(0, 3 * SPAN, 1 * SPAN, nc.vector.tensor_copy)
+        quantize_y(1, 2 * SPAN, 1 * SPAN)
         store_words(slice(0, GROUPS), slice(HALF, HALF + SPAN))
-        round_y(1, 3, 1, nc.scalar.copy)
-        quantize_y(0, 3, 1)
-        quantize_y(1, 3, 1)
+        round_y(1, 3 * SPAN, 1 * SPAN, nc.scalar.copy, part=range(LAST))
+        round_y(1, 3 * SPAN, 1 * SPAN, nc.vector.tensor_copy, part=range(LAST, SPAN))
+        quantize_y(0, 3 * SPAN, 1 * SPAN)
+        quantize_y(1, 3 * SPAN, 1 * SPAN)
         store_words(slice(0, GROUPS), slice(HALF + SPAN, S))
 
         for r in range(4):

@@ -34,7 +34,7 @@ STAGED = slice(P - BLOCKS * PASSES, P)
 WQ_SC, WB_SC = S, S + PASSES * H
 ROW = S + 2 * PASSES * H
 ALIGN = 64
-MID = 128
+MID = 96
 LAST = 128
 BIAS_PITCH = 8
 
@@ -252,11 +252,13 @@ def tile_list_hit_significance_tagging_kernel(
         def quantize_wt(g, u):
             quantize_pair(wt_words[g], wt_sc[g], wt_bf[g, u], u)
 
-        h_bf = [sb("h_bf%d" % s, [P, SPAN * PACK], BF16) for s in range(SPANS)]
+        h_bf = [sb("h_bf%d" % s, [P, SPAN * PACK], BF16) for s in range(SPANS - 1)]
+        behind_h = ws1_at + w_bytes
+        h_bf.append(placed("h_bf3", [P, SPAN * PACK], BF16, behind_h + 1024))
         h_words = [sb("h_words%d" % half, [P, HALF], U32) for half in range(S // HALF)]
         h_sc = [sb("h_sc%d" % half, [P, HALF], U8) for half in range(S // HALF)]
         y_sc = sb("y_sc", [P, GROUPS, S], U8)
-        y_words = sb("y_words", [P, GROUPS, S], U32)
+        y_words = {}
         y = {}
         y_bf = {}
 
@@ -319,20 +321,35 @@ def tile_list_hit_significance_tagging_kernel(
                     func=ACT.Identity,
                     bias=bias[:, g, t : t + 1],
                 )
+
+        def store_y(g, first, width, slices):
+            half, o = divmod(first, HALF)
             rows_out = out_0[PASS_ROWS * g : PASS_ROWS * (g + 1), first : first + width]
             nc.sync.dma_start(
                 out=rows_out.rearrange("(p t) j -> p t j", t=PACK)[:, slices.start : slices.stop, :],
-                in_=y[half, g][:, slices.start : slices.stop, cols],
+                in_=y[half, g][:, slices.start : slices.stop, o : o + width],
             )
 
-        def narrow(g, s, u, b):
+        def kept(g, s, u, b):
             features(g, s * SPAN, SPAN, range(2 * u, 2 * u + 2), b)
+
+        def narrow(g, s, u, b):
+            kept(g, s, u, b)
+            store_y(g, s * SPAN, SPAN, range(2 * u, 2 * u + 2))
 
         def wide(g, half, t, b):
             features(g, half * HALF, HALF, range(t, t + 1), b)
+            store_y(g, half * HALF, HALF, range(t, t + 1))
 
-        def round_y(g, first, width, copy, tag=None, part=None):
+        def round_on_gpsimd(g, s, tag):
+            half, o = divmod(s * SPAN, HALF)
+            y_bf[g, s * SPAN] = sb("y_bf%d_%d" % (g, s * SPAN), [P, SPAN, PACK], BF16, tag=tag)
+            nc.gpsimd.tensor_copy(y_bf[g, s * SPAN][:], y[half, g][:, :, o : o + SPAN].rearrange("p t j -> p j t"))
+
+        def round_y(g, first, width, copy, tag=None, part=None, at=None):
             half, o = divmod(first, HALF)
+            if at is not None:
+                y_bf[g, first] = placed("y_bf%d_%d" % (g, first), [P, width, PACK], BF16, at)
             if (g, first) not in y_bf:
                 y_bf[g, first] = sb("y_bf%d_%d" % (g, first), [P, width, PACK], BF16, tag=tag)
             part = part or range(width)
@@ -341,18 +358,23 @@ def tile_list_hit_significance_tagging_kernel(
                 y[half, g][:, :, o + part.start : o + part.stop].rearrange("p t (c i) -> p c t i", i=4),
             )
 
-        def quantize_y(g, first, width):
+        def quantize_y(g, first, width, tag=None, at=None):
             cols = slice(first, first + width)
+            half, o = divmod(first, HALF)
+            if at is not None:
+                y_words[half, g] = placed("y_words%d_%d" % (half, g), [P, HALF], U32, at)
+            if (half, g) not in y_words:
+                y_words[half, g] = sb("y_words%d_%d" % (half, g), [P, HALF], U32, tag=tag)
             nc.vector.quantize_mx(
-                out=y_words[:, g, cols].bitcast(FP8X4),
+                out=y_words[half, g][:, o : o + width].bitcast(FP8X4),
                 scales=y_sc[:, g, cols],
                 in_=y_bf[g, first][:].rearrange("p j t -> p (j t)"),
             )
 
-        def store_words(groups, cols):
+        def store_words(half, g):
             nc.sync.dma_start(
-                out=out_1.rearrange("g p m t -> p g (m t)").bitcast(I32)[:, groups, cols],
-                in_=y_words[:, groups, cols].bitcast(I32),
+                out=out_1[g].rearrange("p m t -> p (m t)").bitcast(I32)[:, half * HALF : (half + 1) * HALF],
+                in_=y_words[half, g][:].bitcast(I32),
             )
 
         for s in range(SPANS):
@@ -375,12 +397,10 @@ def tile_list_hit_significance_tagging_kernel(
             background(c, 0, True, False)
         for c in first:
             background(c, 1, False, False)
-        for c in range(3):
+        for c in first:
             signal(c, 0, False, False)
-        for c in range(3):
+        for c in first:
             signal(c, 1, False, True)
-        signal(3, 1, False, False)
-        signal(3, 0, False, True)
         round_wt(0, 0, negate_on_scalar)
         round_wt(0, 1, negate_on_scalar)
         scale(0)
@@ -388,67 +408,71 @@ def tile_list_hit_significance_tagging_kernel(
         scale(2)
         quantize_h(0, 2)
         quantize_wt(0, 0)
+        background(4, 0, True, False)
+        background(4, 1, False, False)
+        signal(4, 0, False, False)
+        signal(4, 1, False, True)
+        signals(5)
         narrow(0, 0, 0, 0)
         scale(3)
         quantize_wt(0, 1)
+        background(5, 0, False, False)
         narrow(0, 0, 1, 1)
         quantize_h(2, 2)
         narrow(0, 1, 0, 2)
         narrow(0, 1, 1, 3)
-        round_y(0, 1 * SPAN, 1 * SPAN, nc.scalar.copy, part=range(MID))
+        round_y(0, SPAN, SPAN, nc.scalar.copy, part=range(MID))
+        background(5, 1, False, True)
         round_wt(1, 0, negate_on_vector)
         round_wt(1, 1, negate_on_vector)
         quantize_wt(1, 0)
         quantize_wt(1, 1)
-        round_y(0, 0 * SPAN, 1 * SPAN, nc.vector.tensor_copy, tag="wt_bf1_1")
-        signals(4)
-        backgrounds(4)
-        scale(4)
-        round_y(0, 1 * SPAN, 1 * SPAN, nc.vector.tensor_copy, part=range(MID, SPAN))
-        quantize_y(0, 0 * SPAN, 1 * SPAN)
-        store_words(slice(0, 1), slice(0, SPAN))
+        signals(6)
         wide(1, 0, 0, 0)
         wide(1, 0, 1, 1)
-        signals(5)
-        backgrounds(5)
-        scale(5)
-        quantize_y(0, 1 * SPAN, 1 * SPAN)
-        store_words(slice(0, 1), slice(SPAN, HALF))
-        quantize_h(4, 2)
+        background(6, 0, False, False)
         wide(1, 0, 2, 2)
-        signals(6)
         wide(1, 0, 3, 3)
-        backgrounds(6)
+        background(6, 1, False, True)
+        round_on_gpsimd(0, 0, "wt_bf1_1")
+        scale(4)
+        scale(5)
+        round_y(0, SPAN, SPAN, nc.vector.tensor_copy, part=range(MID, SPAN))
+        quantize_h(4, 2)
+        quantize_y(0, 0, SPAN)
+        quantize_y(0, SPAN, SPAN)
+        store_words(0, 0)
         signals(7)
+        narrow(1, 2, 0, 4)
+        narrow(1, 2, 1, 5)
         backgrounds(7)
-        narrow(0, 2, 0, 4)
-        narrow(0, 2, 1, 5)
-        narrow(1, 2, 0, 0)
-        narrow(1, 2, 1, 1)
-        y_bf[1, 0] = sb("y_bf1_0", [P, SPAN, PACK], BF16, tag="h_bf2")
-        nc.gpsimd.tensor_copy(y_bf[1, 0][:], y[0, 1][:, :, 0:SPAN].rearrange("p t j -> p j t"))
+        narrow(0, 2, 0, 0)
+        narrow(0, 2, 1, 1)
+        round_on_gpsimd(1, 0, "y_bf0_256")
         scale(6)
         scale(7)
+        round_y(1, SPAN, CHUNK, nc.vector.tensor_copy, tag="h_bf2")
         quantize_h(6, 2)
-        narrow(0, 3, 0, 2)
-        narrow(0, 3, 1, 3)
+        round_y(1, SPAN + CHUNK, CHUNK, nc.vector.tensor_copy, at=behind_h + 2048)
+        for u in range(2):
+            narrow(0, 3, u, 2 + u)
         narrow(1, 3, 0, 6)
         narrow(1, 3, 1, 7)
-        round_y(1, SPAN, SPAN, nc.vector.tensor_copy, tag="h_bf3")
+        quantize_y(1, SPAN, CHUNK, at=behind_h)
         quantize_y(1, 0, SPAN)
-        round_y(0, 2 * SPAN, 1 * SPAN, nc.vector.tensor_copy, tag="h_bf2")
-        quantize_y(1, SPAN, SPAN)
-        store_words(slice(1, 2), slice(0, HALF))
-        round_y(1, 2 * SPAN, 1 * SPAN, nc.vector.tensor_copy)
-        quantize_y(0, 2 * SPAN, 1 * SPAN)
-        round_y(0, 3 * SPAN, 1 * SPAN, nc.vector.tensor_copy)
-        quantize_y(1, 2 * SPAN, 1 * SPAN)
-        store_words(slice(0, GROUPS), slice(HALF, HALF + SPAN))
-        round_y(1, 3 * SPAN, 1 * SPAN, nc.scalar.copy, part=range(LAST))
-        round_y(1, 3 * SPAN, 1 * SPAN, nc.vector.tensor_copy, part=range(LAST, SPAN))
-        quantize_y(0, 3 * SPAN, 1 * SPAN)
-        quantize_y(1, 3 * SPAN, 1 * SPAN)
-        store_words(slice(0, GROUPS), slice(HALF + SPAN, S))
+        round_y(1, 2 * SPAN, SPAN, nc.vector.tensor_copy, tag="y_bf0_256")
+        quantize_y(1, SPAN + CHUNK, CHUNK)
+        store_words(0, 1)
+        round_y(0, 2 * SPAN, SPAN, nc.vector.tensor_copy)
+        quantize_y(1, 2 * SPAN, SPAN)
+        round_y(0, 3 * SPAN, SPAN, nc.vector.tensor_copy)
+        quantize_y(0, 2 * SPAN, SPAN)
+        round_y(1, 3 * SPAN, SPAN, nc.scalar.copy, part=range(LAST))
+        round_y(1, 3 * SPAN, SPAN, nc.vector.tensor_copy, part=range(LAST, SPAN))
+        quantize_y(0, 3 * SPAN, SPAN)
+        store_words(1, 0)
+        quantize_y(1, 3 * SPAN, SPAN)
+        store_words(1, 1)
 
         for r in range(4):
             nc.scalar.dma_start(

@@ -35,8 +35,10 @@ WQ_SC, WB_SC = S, S + PASSES * H
 ROW = S + 2 * PASSES * H
 ALIGN = 64
 MID = 96
-LAST = 128
+LAST = 160
 BIAS_PITCH = 8
+MID2 = 96
+WS_SHARE = 80
 
 
 def tile_list_hit_significance_tagging_kernel(
@@ -162,15 +164,19 @@ def tile_list_hit_significance_tagging_kernel(
                 wb_raw[:, a, :].bitcast(U16).rearrange("p (c i t) -> p c t i", t=PACK, i=8),
             )
 
-        deal_wq(1, nc.scalar.copy)
+        for u in range(2):
+            nc.scalar.copy(
+                wq[1][:].bitcast(U32).rearrange("p (t c i) -> p c t i", t=PACK, i=4)[:, :, 2 * u : 2 * u + 2, :],
+                wq_raw[1][:].bitcast(U32).rearrange("p (c i t) -> p c t i", t=PACK, i=4)[:, :, 2 * u : 2 * u + 2, :],
+            )
         for i in range(S // SPAN):
             gather(1, i)
         deal_wb(0, nc.vector.tensor_copy)
         deal_wb(1, nc.vector.tensor_copy)
 
-        def first_stage(acc, c, a, words, dtype, width, scales, start, stop):
+        def first_stage(acc, c, a, words, dtype, width, scales, start, stop, slices=range(PACK)):
             i, o = divmod(c * CHUNK, widths[a])
-            for t in range(PACK):
+            for t in slices:
                 nc.tensor.matmul_mx(
                     out=acc[:, t * CHUNK : (t + 1) * CHUNK],
                     lhsT=words[:, t * width : (t + 1) * width].bitcast(dtype),
@@ -238,6 +244,12 @@ def tile_list_hit_significance_tagging_kernel(
             ws_bf[a, u] = sb("ws_bf%d_%d" % (a, u), [P, 2 * P * PACK], BF16)
             negate(*dealt(ws_bf[a, u], ws_raw[a][:], u))
 
+        def round_ws_part(a, u, negate, part):
+            if (a, u) not in ws_bf:
+                ws_bf[a, u] = sb("ws_bf%d_%d" % (a, u), [P, 2 * P * PACK], BF16)
+            dst, src = dealt(ws_bf[a, u], ws_raw[a][:], u)
+            negate(dst[:, part.start : part.stop], src[:, part.start : part.stop])
+
         def quantize_ws(a, u):
             quantize_pair(ws_words[a], ws_sc[a], ws_bf[a, u], u)
 
@@ -249,6 +261,12 @@ def tile_list_hit_significance_tagging_kernel(
             wt_bf[g, u] = sb("wt_bf%d_%d" % (g, u), [P, 2 * P * PACK], BF16, tag=tag)
             copy(*dealt(wt_bf[g, u], wt_raw[g][:], u))
 
+        def round_wt_part(g, u, copy, part):
+            if (g, u) not in wt_bf:
+                wt_bf[g, u] = sb("wt_bf%d_%d" % (g, u), [P, 2 * P * PACK], BF16)
+            dst, src = dealt(wt_bf[g, u], wt_raw[g][:], u)
+            copy(dst[:, part.start : part.stop], src[:, part.start : part.stop])
+
         def quantize_wt(g, u):
             quantize_pair(wt_words[g], wt_sc[g], wt_bf[g, u], u)
 
@@ -257,7 +275,7 @@ def tile_list_hit_significance_tagging_kernel(
         h_bf.append(placed("h_bf3", [P, SPAN * PACK], BF16, behind_h + 1024))
         h_words = [sb("h_words%d" % half, [P, HALF], U32) for half in range(S // HALF)]
         h_sc = [sb("h_sc%d" % half, [P, HALF], U8) for half in range(S // HALF)]
-        y_sc = sb("y_sc", [P, GROUPS, S], U8)
+        y_sc = sb("y_sc", [P, S], U8)
         y_words = {}
         y = {}
         y_bf = {}
@@ -271,6 +289,9 @@ def tile_list_hit_significance_tagging_kernel(
             if start:
                 d_acc[c] = bank(c)
             first_stage(d_acc[c], c, a, ws_words[a][:], FP8X4, P, ws_sc[a][:], start, stop)
+
+        def signal_pair(c, a, u, stop):
+            first_stage(d_acc[c], c, a, ws_words[a][:], FP8X4, P, ws_sc[a][:], False, stop, range(2 * u, 2 * u + 2))
 
         def signals(c):
             signal(c, 1, True, False)
@@ -367,7 +388,7 @@ def tile_list_hit_significance_tagging_kernel(
                 y_words[half, g] = sb("y_words%d_%d" % (half, g), [P, HALF], U32, tag=tag)
             nc.vector.quantize_mx(
                 out=y_words[half, g][:, o : o + width].bitcast(FP8X4),
-                scales=y_sc[:, g, cols],
+                scales=y_sc[4 * g : P, cols],
                 in_=y_bf[g, first][:].rearrange("p j t -> p (j t)"),
             )
 
@@ -388,7 +409,8 @@ def tile_list_hit_significance_tagging_kernel(
         for u in range(2):
             quantize_ws(0, u)
         round_ws(1, 0, negate_on_vector)
-        round_ws(1, 1, negate_on_scalar)
+        round_ws_part(1, 1, negate_on_scalar, range(WS_SHARE))
+        round_ws_part(1, 1, negate_on_vector, range(WS_SHARE, P))
         exponentials(SPANS - 1)
         for u in range(2):
             quantize_ws(1, u)
@@ -397,10 +419,14 @@ def tile_list_hit_significance_tagging_kernel(
             background(c, 0, True, False)
         for c in first:
             background(c, 1, False, False)
-        for c in first:
+        for c in range(3):
             signal(c, 0, False, False)
-        for c in first:
-            signal(c, 1, False, True)
+        for u in range(2):
+            for c in range(2):
+                signal_pair(c, 1, u, True)
+        signal(2, 1, False, True)
+        signal(3, 1, False, False)
+        signal(3, 0, False, True)
         round_wt(0, 0, negate_on_scalar)
         round_wt(0, 1, negate_on_scalar)
         scale(0)
@@ -412,17 +438,16 @@ def tile_list_hit_significance_tagging_kernel(
         background(4, 1, False, False)
         signal(4, 0, False, False)
         signal(4, 1, False, True)
-        signals(5)
         narrow(0, 0, 0, 0)
         scale(3)
         quantize_wt(0, 1)
-        background(5, 0, False, False)
+        signals(5)
         narrow(0, 0, 1, 1)
         quantize_h(2, 2)
         narrow(0, 1, 0, 2)
         narrow(0, 1, 1, 3)
         round_y(0, SPAN, SPAN, nc.scalar.copy, part=range(MID))
-        background(5, 1, False, True)
+        backgrounds(5)
         round_wt(1, 0, negate_on_vector)
         round_wt(1, 1, negate_on_vector)
         quantize_wt(1, 0)
@@ -434,24 +459,24 @@ def tile_list_hit_significance_tagging_kernel(
         wide(1, 0, 2, 2)
         wide(1, 0, 3, 3)
         background(6, 1, False, True)
-        round_on_gpsimd(0, 0, "wt_bf1_1")
         scale(4)
         scale(5)
         round_y(0, SPAN, SPAN, nc.vector.tensor_copy, part=range(MID, SPAN))
         quantize_h(4, 2)
-        quantize_y(0, 0, SPAN)
+        round_y(0, 0, SPAN, nc.vector.tensor_copy, tag="h_bf2")
         quantize_y(0, SPAN, SPAN)
+        scale(6)
+        quantize_y(0, 0, SPAN)
         store_words(0, 0)
         signals(7)
+        backgrounds(7)
         narrow(1, 2, 0, 4)
         narrow(1, 2, 1, 5)
-        backgrounds(7)
         narrow(0, 2, 0, 0)
         narrow(0, 2, 1, 1)
-        round_on_gpsimd(1, 0, "y_bf0_256")
-        scale(6)
+        round_y(1, 2 * SPAN, SPAN, nc.scalar.copy, tag="h_bf2", part=range(MID2))
         scale(7)
-        round_y(1, SPAN, CHUNK, nc.vector.tensor_copy, tag="h_bf2")
+        round_y(1, SPAN, CHUNK, nc.vector.tensor_copy, tag="y_bf0_256")
         quantize_h(6, 2)
         round_y(1, SPAN + CHUNK, CHUNK, nc.vector.tensor_copy, at=behind_h + 2048)
         for u in range(2):
@@ -459,9 +484,10 @@ def tile_list_hit_significance_tagging_kernel(
         narrow(1, 3, 0, 6)
         narrow(1, 3, 1, 7)
         quantize_y(1, SPAN, CHUNK, at=behind_h)
-        quantize_y(1, 0, SPAN)
-        round_y(1, 2 * SPAN, SPAN, nc.vector.tensor_copy, tag="y_bf0_256")
+        round_y(1, 0, SPAN, nc.vector.tensor_copy, tag="y_bf0_256")
         quantize_y(1, SPAN + CHUNK, CHUNK)
+        round_y(1, 2 * SPAN, SPAN, nc.vector.tensor_copy, tag="h_bf2", part=range(MID2, SPAN))
+        quantize_y(1, 0, SPAN)
         store_words(0, 1)
         round_y(0, 2 * SPAN, SPAN, nc.vector.tensor_copy)
         quantize_y(1, 2 * SPAN, SPAN)
@@ -476,6 +502,6 @@ def tile_list_hit_significance_tagging_kernel(
 
         for r in range(4):
             nc.scalar.dma_start(
-                out=out_2[:, r:BLOCKS:4, :].rearrange("g q m -> q g m").bitcast(I32),
-                in_=y_sc[r:P:32, :, :].bitcast(I32),
+                out=out_2[:, 4 * r : 4 * r + 4, :].bitcast(I32),
+                in_=y_sc[32 * r : 32 * r + 4 * GROUPS, :].bitcast(I32),
             )

@@ -34,7 +34,7 @@ STAGED = slice(P - BLOCKS * PASSES, P)
 WQ_SC, WB_SC = S, S + PASSES * H
 ROW = S + 2 * PASSES * H
 ALIGN = 64
-MID = 96
+MID = 64
 LAST = 160
 BIAS_PITCH = 8
 MID2 = 96
@@ -358,6 +358,11 @@ def tile_list_hit_significance_tagging_kernel(
             kept(g, s, u, b)
             store_y(g, s * SPAN, SPAN, range(2 * u, 2 * u + 2))
 
+        def early(g, s, u, b):
+            kept(g, s, u, b)
+            for t in range(2 * u, 2 * u + 2):
+                store_y(g, s * SPAN, SPAN, range(t, t + 1))
+
         def wide(g, half, t, b):
             features(g, half * HALF, HALF, range(t, t + 1), b)
             store_y(g, half * HALF, HALF, range(t, t + 1))
@@ -419,14 +424,14 @@ def tile_list_hit_significance_tagging_kernel(
             background(c, 0, True, False)
         for c in first:
             background(c, 1, False, False)
-        for c in range(3):
+        for c in range(2):
             signal(c, 0, False, False)
         for u in range(2):
             for c in range(2):
                 signal_pair(c, 1, u, True)
-        signal(2, 1, False, True)
-        signal(3, 1, False, False)
-        signal(3, 0, False, True)
+        for c in range(2, 4):
+            signal(c, 1, False, False)
+            signal(c, 0, False, True)
         round_wt(0, 0, negate_on_scalar)
         round_wt(0, 1, negate_on_scalar)
         scale(0)
@@ -434,49 +439,50 @@ def tile_list_hit_significance_tagging_kernel(
         scale(2)
         quantize_h(0, 2)
         quantize_wt(0, 0)
-        background(4, 0, True, False)
-        background(4, 1, False, False)
-        signal(4, 0, False, False)
-        signal(4, 1, False, True)
-        narrow(0, 0, 0, 0)
+        signals(4)
+        backgrounds(4)
+        early(0, 0, 0, 0)
         scale(3)
         quantize_wt(0, 1)
         signals(5)
-        narrow(0, 0, 1, 1)
+        early(0, 0, 1, 1)
         quantize_h(2, 2)
-        narrow(0, 1, 0, 2)
+        early(0, 1, 0, 2)
         narrow(0, 1, 1, 3)
-        round_y(0, SPAN, SPAN, nc.scalar.copy, part=range(MID))
         backgrounds(5)
         round_wt(1, 0, negate_on_vector)
-        round_wt(1, 1, negate_on_vector)
+        round_wt_part(1, 1, negate_on_vector, range(P // 2))
         quantize_wt(1, 0)
+        round_wt_part(1, 1, negate_on_vector, range(P // 2, P))
+        scale(4)
         quantize_wt(1, 1)
-        signals(6)
+        signal(6, 1, True, False)
         wide(1, 0, 0, 0)
+        signal(6, 0, False, False)
         wide(1, 0, 1, 1)
         background(6, 0, False, False)
         wide(1, 0, 2, 2)
-        wide(1, 0, 3, 3)
         background(6, 1, False, True)
-        scale(4)
+        wide(1, 0, 3, 3)
         scale(5)
-        round_y(0, SPAN, SPAN, nc.vector.tensor_copy, part=range(MID, SPAN))
+        round_y(0, 0, SPAN, nc.vector.tensor_copy, tag="wt_bf1_1")
         quantize_h(4, 2)
-        round_y(0, 0, SPAN, nc.vector.tensor_copy, tag="h_bf2")
-        quantize_y(0, SPAN, SPAN)
-        scale(6)
+        round_y(0, SPAN, SPAN, nc.vector.tensor_copy, tag="h_bf2")
         quantize_y(0, 0, SPAN)
+        quantize_y(0, SPAN, SPAN)
         store_words(0, 0)
+        scale(6)
+        round_y(1, 0, CHUNK, nc.scalar.copy)
         signals(7)
-        backgrounds(7)
+        background(7, 0, False, False)
         narrow(1, 2, 0, 4)
+        background(7, 1, False, True)
         narrow(1, 2, 1, 5)
         narrow(0, 2, 0, 0)
         narrow(0, 2, 1, 1)
-        round_y(1, 2 * SPAN, SPAN, nc.scalar.copy, tag="h_bf2", part=range(MID2))
+        round_y(1, 2 * SPAN, SPAN, nc.scalar.copy, tag="wt_bf1_1", part=range(MID2))
         scale(7)
-        round_y(1, SPAN, CHUNK, nc.vector.tensor_copy, tag="y_bf0_256")
+        round_y(1, SPAN, CHUNK, nc.vector.tensor_copy, tag="h_bf2")
         quantize_h(6, 2)
         round_y(1, SPAN + CHUNK, CHUNK, nc.vector.tensor_copy, at=behind_h + 2048)
         for u in range(2):
@@ -484,10 +490,11 @@ def tile_list_hit_significance_tagging_kernel(
         narrow(1, 3, 0, 6)
         narrow(1, 3, 1, 7)
         quantize_y(1, SPAN, CHUNK, at=behind_h)
-        round_y(1, 0, SPAN, nc.vector.tensor_copy, tag="y_bf0_256")
+        round_y(1, CHUNK, CHUNK, nc.vector.tensor_copy, tag="h_bf2")
+        quantize_y(1, 0, CHUNK)
         quantize_y(1, SPAN + CHUNK, CHUNK)
-        round_y(1, 2 * SPAN, SPAN, nc.vector.tensor_copy, tag="h_bf2", part=range(MID2, SPAN))
-        quantize_y(1, 0, SPAN)
+        round_y(1, 2 * SPAN, SPAN, nc.vector.tensor_copy, tag="wt_bf1_1", part=range(MID2, SPAN))
+        quantize_y(1, CHUNK, CHUNK)
         store_words(0, 1)
         round_y(0, 2 * SPAN, SPAN, nc.vector.tensor_copy)
         quantize_y(1, 2 * SPAN, SPAN)

@@ -35,8 +35,9 @@ WQ_SC, WB_SC = S, S + PASSES * H
 ROW = S + 2 * PASSES * H
 ALIGN = 64
 MID = 64
-LAST = 160
+LAST = 144
 BIAS_PITCH = 8
+WT_SHARE = 32
 MID2 = 96
 WS_SHARE = 80
 
@@ -367,10 +368,10 @@ def tile_list_hit_significance_tagging_kernel(
             features(g, half * HALF, HALF, range(t, t + 1), b)
             store_y(g, half * HALF, HALF, range(t, t + 1))
 
-        def round_on_gpsimd(g, s, tag):
+        def round_on_gpsimd(g, s, tag, width=SPAN):
             half, o = divmod(s * SPAN, HALF)
-            y_bf[g, s * SPAN] = sb("y_bf%d_%d" % (g, s * SPAN), [P, SPAN, PACK], BF16, tag=tag)
-            nc.gpsimd.tensor_copy(y_bf[g, s * SPAN][:], y[half, g][:, :, o : o + SPAN].rearrange("p t j -> p j t"))
+            y_bf[g, s * SPAN] = sb("y_bf%d_%d" % (g, s * SPAN), [P, width, PACK], BF16, tag=tag)
+            nc.gpsimd.tensor_copy(y_bf[g, s * SPAN][:], y[half, g][:, :, o : o + width].rearrange("p t j -> p j t"))
 
         def round_y(g, first, width, copy, tag=None, part=None, at=None):
             half, o = divmod(first, HALF)
@@ -445,12 +446,13 @@ def tile_list_hit_significance_tagging_kernel(
         scale(3)
         quantize_wt(0, 1)
         signals(5)
+        round_wt_part(1, 0, negate_on_scalar, range(WT_SHARE))
         early(0, 0, 1, 1)
         quantize_h(2, 2)
         early(0, 1, 0, 2)
         narrow(0, 1, 1, 3)
         backgrounds(5)
-        round_wt(1, 0, negate_on_vector)
+        round_wt_part(1, 0, negate_on_vector, range(WT_SHARE, P))
         round_wt_part(1, 1, negate_on_vector, range(P // 2))
         quantize_wt(1, 0)
         round_wt_part(1, 1, negate_on_vector, range(P // 2, P))
@@ -468,35 +470,35 @@ def tile_list_hit_significance_tagging_kernel(
         round_y(0, 0, SPAN, nc.vector.tensor_copy, tag="wt_bf1_1")
         quantize_h(4, 2)
         round_y(0, SPAN, SPAN, nc.vector.tensor_copy, tag="h_bf2")
+        signal(7, 1, True, False)
+        narrow(1, 2, 0, 4)
+        signal(7, 0, False, False)
+        narrow(1, 2, 1, 5)
+        backgrounds(7)
+        round_y(1, 0, CHUNK, nc.scalar.copy)
         quantize_y(0, 0, SPAN)
         quantize_y(0, SPAN, SPAN)
         store_words(0, 0)
+        round_on_gpsimd(1, 1, "h_bf2", CHUNK)
         scale(6)
-        round_y(1, 0, CHUNK, nc.scalar.copy)
-        signals(7)
-        background(7, 0, False, False)
-        narrow(1, 2, 0, 4)
-        background(7, 1, False, True)
-        narrow(1, 2, 1, 5)
         narrow(0, 2, 0, 0)
         narrow(0, 2, 1, 1)
-        round_y(1, 2 * SPAN, SPAN, nc.scalar.copy, tag="wt_bf1_1", part=range(MID2))
         scale(7)
-        round_y(1, SPAN, CHUNK, nc.vector.tensor_copy, tag="h_bf2")
+        round_y(1, CHUNK, CHUNK, nc.vector.tensor_copy, tag="wt_bf1_1")
         quantize_h(6, 2)
-        round_y(1, SPAN + CHUNK, CHUNK, nc.vector.tensor_copy, at=behind_h + 2048)
+        round_y(1, 2 * SPAN, SPAN, nc.scalar.copy, part=range(MID2))
         for u in range(2):
             narrow(0, 3, u, 2 + u)
         narrow(1, 3, 0, 6)
         narrow(1, 3, 1, 7)
-        quantize_y(1, SPAN, CHUNK, at=behind_h)
-        round_y(1, CHUNK, CHUNK, nc.vector.tensor_copy, tag="h_bf2")
-        quantize_y(1, 0, CHUNK)
-        quantize_y(1, SPAN + CHUNK, CHUNK)
-        round_y(1, 2 * SPAN, SPAN, nc.vector.tensor_copy, tag="wt_bf1_1", part=range(MID2, SPAN))
+        quantize_y(1, 0, CHUNK, at=behind_h)
+        round_y(1, SPAN + CHUNK, CHUNK, nc.vector.tensor_copy, at=behind_h + 2048)
         quantize_y(1, CHUNK, CHUNK)
+        quantize_y(1, SPAN, CHUNK)
+        round_y(1, 2 * SPAN, SPAN, nc.vector.tensor_copy, part=range(MID2, SPAN))
+        quantize_y(1, SPAN + CHUNK, CHUNK)
         store_words(0, 1)
-        round_y(0, 2 * SPAN, SPAN, nc.vector.tensor_copy)
+        round_y(0, 2 * SPAN, SPAN, nc.vector.tensor_copy, tag="h_bf2")
         quantize_y(1, 2 * SPAN, SPAN)
         round_y(0, 3 * SPAN, SPAN, nc.vector.tensor_copy)
         quantize_y(0, 2 * SPAN, SPAN)

@@ -37,6 +37,11 @@ ALIGN = 64
 MID = 64
 LAST = 144
 BIAS_PITCH = 8
+MOVING_SC = 192
+FIXED_SC = 64
+MOVING = 128
+FIXED = 0
+SPREAD_START = 40960
 WT_SHARE = 32
 MID2 = 96
 WS_SHARE = 80
@@ -57,6 +62,13 @@ def tile_list_hit_significance_tagging_kernel(
         def placed(name, shape, dtype, offset):
             return late.tile(shape, dtype, name=name, tag=name, align_bytes=ALIGN, offset=offset)
 
+        spread_at = [SPREAD_START]
+
+        def spread(name, shape, dtype, size, place):
+            at = spread_at[-1] + place
+            spread_at.append(spread_at[-1] + size + 256)
+            return late.tile(shape, dtype, name=name, tag=name, align_bytes=256 if place == 0 else ALIGN, offset=at)
+
         def bank(b):
             return psum.tile([P, BANK], F32, name="bank%d" % b, tag="bank%d" % b)
 
@@ -65,7 +77,8 @@ def tile_list_hit_significance_tagging_kernel(
         nc.sync.dma_start(out=sc_window[STAGED, :].bitcast(I32), in_=tab_scales.rearrange("a q t -> (a q) t").bitcast(I32))
         nc.vector.memset(sc_window[0 : STAGED.start, :].bitcast(I32), 0)
         nc.sync.dma_start(offsets[:], offs)
-        stage = [sb("stage0", [P, ROW], U8), sb("stage1", [P, S], U8)]
+        stage = [spread("stage0", [P, ROW], U8, ROW, MOVING), sb("stage1", [P, S], U8)]
+        stage0_at = spread_at[-2] + MOVING
         for first, w_scales in ((WQ_SC, wq_scales), (WB_SC, wb_scales)):
             nc.sync.dma_start(
                 out=stage[0][STAGED.start : STAGED.start + BLOCKS, first : first + PASSES * H].bitcast(I32),
@@ -86,7 +99,7 @@ def tile_list_hit_significance_tagging_kernel(
         wq_raw = [sb("wq_raw0", [P, H], I32)]
         nc.sync.dma_start(out=wq_raw[0][:], in_=wq_words[0].rearrange("p c i -> p (c i)").bitcast(I32))
 
-        planes = sb("planes", [P, ROW + S], U8)
+        planes = spread("planes", [P, ROW + S], U8, ROW + S, MOVING_SC)
         nc.vector.memset(planes[:].bitcast(I32), 0)
 
         def hits(first, count):
@@ -114,12 +127,15 @@ def tile_list_hit_significance_tagging_kernel(
         v = [[None] * (S // widths[a]) for a in range(PASSES)]
 
         def gather(a, i):
-            v[a][i] = sb("v%d_%d" % (a, i), [P, widths[a]], U32, tag="stage0" if (a, i) == (0, 1) else None)
+            if (a, i) == (0, 1):
+                v[a][i] = placed("v0_1", [P, widths[a]], U32, stage0_at)
+            else:
+                v[a][i] = spread("v%d_%d" % (a, i), [P, widths[a]], U32, 4 * widths[a], MOVING)
             nc.vector.tensor_copy(v[a][i][:], tab[a][:].bitcast(U32).indirect(hits(i * widths[a], widths[a])))
 
-        wq = [sb("wq%d" % a, [P, H], I32) for a in range(PASSES)]
-        wb = [sb("wb%d" % a, [P, 2 * H], U8) for a in range(PASSES)]
-        w_sc = sb("w_sc", [P, PASSES * 2 * H], U8)
+        wq = [spread("wq%d" % a, [P, H], I32, 4 * H, FIXED) for a in range(PASSES)]
+        wb = [spread("wb%d" % a, [P, 2 * H], U8, 2 * H, FIXED) for a in range(PASSES)]
+        w_sc = spread("w_sc", [P, PASSES * 2 * H], U8, PASSES * 2 * H, FIXED_SC)
 
         def deal_wq(a, copy):
             copy(
@@ -231,8 +247,8 @@ def tile_list_hit_significance_tagging_kernel(
             cols = slice(2 * u * P, (2 * u + 2) * P)
             nc.vector.quantize_mx(out=words[:, cols].bitcast(FP8X4), scales=scales[:, cols], in_=rounded[:])
 
-        ws_words = [sb("ws_words%d" % a, [P, H], U32) for a in range(PASSES)]
-        ws_sc = [sb("ws_sc%d" % a, [P, H], U8) for a in range(PASSES)]
+        ws_words = [spread("ws_words%d" % a, [P, H], U32, 4 * H, FIXED) for a in range(PASSES)]
+        ws_sc = [spread("ws_sc%d" % a, [P, H], U8, H, FIXED_SC) for a in range(PASSES)]
         ws_bf = {}
 
         def negate_on_vector(dst, src):

@@ -37,6 +37,7 @@ ALIGN = 64
 MID = 64
 LAST = 144
 BIAS_PITCH = 8
+BURST = 256
 MOVING_SC = 192
 FIXED_SC = 64
 MOVING = 128
@@ -57,7 +58,7 @@ def tile_list_hit_significance_tagging_kernel(
         psum = ctx.enter_context(tc.psum_pool(name="psum", bufs=1))
 
         def sb(name, shape, dtype, tag=None):
-            return keep.tile(shape, dtype, name=name, tag=tag or name, align_bytes=ALIGN)
+            return keep.tile(shape, dtype, name=name, tag=tag or name, align_bytes=BURST)
 
         def placed(name, shape, dtype, offset):
             return late.tile(shape, dtype, name=name, tag=name, align_bytes=ALIGN, offset=offset)
@@ -86,10 +87,10 @@ def tile_list_hit_significance_tagging_kernel(
             )
 
         w_bytes = 4 * PACK * H
-        tab0_at = w_bytes - ALIGN
+        tab0_at = w_bytes - BURST
         wb_at = w_bytes
         bias_at = wb_at + PASSES * 2 * H
-        wq1_at = bias_at + ALIGN
+        wq1_at = bias_at + BURST
         ws0_at = wq1_at + 4 * H
         ws1_at = ws0_at + w_bytes
         last_noise = ws1_at + 2048
@@ -270,8 +271,8 @@ def tile_list_hit_significance_tagging_kernel(
         def quantize_ws(a, u):
             quantize_pair(ws_words[a], ws_sc[a], ws_bf[a, u], u)
 
-        wt_words = [sb("wt_words%d" % g, [P, PASS_ROWS], U32) for g in range(GROUPS)]
-        wt_sc = [sb("wt_sc%d" % g, [P, PASS_ROWS], U8) for g in range(GROUPS)]
+        wt_words = [spread("wt_words%d" % g, [P, PASS_ROWS], U32, 4 * PASS_ROWS, FIXED) for g in range(GROUPS)]
+        wt_sc = [spread("wt_sc%d" % g, [P, PASS_ROWS], U8, PASS_ROWS, FIXED_SC) for g in range(GROUPS)]
         wt_bf = {}
 
         def round_wt(g, u, copy, tag=None):
@@ -290,8 +291,8 @@ def tile_list_hit_significance_tagging_kernel(
         h_bf = [sb("h_bf%d" % s, [P, SPAN * PACK], BF16) for s in range(SPANS - 1)]
         behind_h = ws1_at + w_bytes
         h_bf.append(placed("h_bf3", [P, SPAN * PACK], BF16, behind_h + 1024))
-        h_words = [sb("h_words%d" % half, [P, HALF], U32) for half in range(S // HALF)]
-        h_sc = [sb("h_sc%d" % half, [P, HALF], U8) for half in range(S // HALF)]
+        h_words = [spread("h_words%d" % half, [P, HALF], U32, 4 * HALF, MOVING) for half in range(S // HALF)]
+        h_sc = [spread("h_sc%d" % half, [P, HALF], U8, HALF, MOVING_SC) for half in range(S // HALF)]
         y_sc = sb("y_sc", [P, S], U8)
         y_words = {}
         y = {}

@@ -506,8 +506,9 @@ def tile_list_hit_significance_tagging_kernel(
         round_y(1, 2 * SPAN, SPAN, nc.scalar.copy, part=range(MID2))
         for u in range(2):
             narrow(0, 3, u, 2 + u)
-        narrow(1, 3, 0, 6)
-        narrow(1, 3, 1, 7)
+        kept(1, 3, 0, 6)
+        kept(1, 3, 1, 7)
+        store_y(1, 3 * SPAN, SPAN, range(PACK))
         quantize_y(1, 0, CHUNK, at=behind_h)
         round_y(1, SPAN + CHUNK, CHUNK, nc.vector.tensor_copy, at=behind_h + 2048)
         quantize_y(1, CHUNK, CHUNK)

from contextlib import ExitStack

import concourse.mybir as mybir

K, T, S, H, N = 1024, 4096, 1024, 512, 1024
FLOPS = 2 * (3 * K * H * S + H * N * S)

F32 = mybir.dt.float32
BF16 = mybir.dt.bfloat16
I32 = mybir.dt.int32
U32 = mybir.dt.uint32
U16 = mybir.dt.uint16
U8 = mybir.dt.uint8
FP8X4 = mybir.dt.float8_e4m3fn_x4
FP4X4 = mybir.dt.float4_e2m1fn_x4
ACT = mybir.ActivationFunctionType
ALU = mybir.AluOpType

P = 128
PACK = 4
PASS_ROWS = P * PACK
PASSES = K // PASS_ROWS
GROUPS = N // PASS_ROWS
BLOCKS = PASS_ROWS // 32
CHUNK = 128
CHUNKS = S // CHUNK
RUN = 4
SPAN = 256
SPANS = S // SPAN
HALF = 512
BANK = 512
LIST_ROWS = 16
STAGED = slice(P - BLOCKS * PASSES, P)
WQ_SC, WB_SC = S, S + PASSES * H
ROW = S + 2 * PASSES * H
ALIGN = 64
MID = 64
LAST = 144
BIAS_PITCH = 8
BURST = 256
MOVING_SC = 192
FIXED_SC = 64
MOVING = 128
FIXED = 0
SPREAD_START = 40960
WT_SHARE = 32
MID2 = 96
WS_SHARE = 80


def tile_list_hit_significance_tagging_kernel(
    tc, tab_words, tab_scales, offs, ws, wb_words, wb_scales, wq_words, wq_scales, wt, bt, out_0, out_1, out_2
):
    nc = tc.nc
    with ExitStack() as ctx:
        keep = ctx.enter_context(tc.tile_pool(name="keep", bufs=1))
        late = ctx.enter_context(tc.tile_pool(name="late", bufs=1))
        psum = ctx.enter_context(tc.psum_pool(name="psum", bufs=1))

        def sb(name, shape, dtype, tag=None):
            return keep.tile(shape, dtype, name=name, tag=tag or name, align_bytes=BURST)

        def placed(name, shape, dtype, offset):
            return late.tile(shape, dtype, name=name, tag=name, align_bytes=ALIGN, offset=offset)

        spread_at = [SPREAD_START]

        def spread(name, shape, dtype, size, place):
            at = spread_at[-1] + place
            spread_at.append(spread_at[-1] + size + 256)
            return late.tile(shape, dtype, name=name, tag=name, align_bytes=256 if place == 0 else ALIGN, offset=at)

        def bank(b):
            return psum.tile([P, BANK], F32, name="bank%d" % b, tag="bank%d" % b)

        offsets = keep.tile([P, S // LIST_ROWS], U16, name="offsets")
        sc_window = sb("sc_window", [P, T], U8)
        nc.sync.dma_start(out=sc_window[STAGED, :].bitcast(I32), in_=tab_scales.rearrange("a q t -> (a q) t").bitcast(I32))
        nc.vector.memset(sc_window[0 : STAGED.start, :].bitcast(I32), 0)
        nc.sync.dma_start(offsets[:], offs)
        stage = [spread("stage0", [P, ROW], U8, ROW, MOVING), sb("stage1", [P, S], U8)]
        stage0_at = spread_at[-2] + MOVING
        for first, w_scales in ((WQ_SC, wq_scales), (WB_SC, wb_scales)):
            nc.sync.dma_start(
                out=stage[0][STAGED.start : STAGED.start + BLOCKS, first : first + PASSES * H].bitcast(I32),
                in_=w_scales.rearrange("a q c -> q a c").bitcast(I32),
            )

        w_bytes = 4 * PACK * H
        tab0_at = w_bytes - BURST
        wb_at = w_bytes
        bias_at = wb_at + PASSES * 2 * H
        wq1_at = bias_at + BURST
        ws0_at = wq1_at + 4 * H
        ws1_at = ws0_at + w_bytes
        last_noise = ws1_at + 2048

        tab = [placed("tab0", [P, T], I32, tab0_at)]
        nc.sync.dma_start(out=tab[0][:], in_=tab_words[0].rearrange("p t i -> p (t i)").bitcast(I32))
        wq_raw = [sb("wq_raw0", [P, H], I32)]
        nc.sync.dma_start(out=wq_raw[0][:], in_=wq_words[0].rearrange("p c i -> p (c i)").bitcast(I32))

        planes = spread("planes", [P, ROW + S], U8, ROW + S, MOVING_SC)
        nc.vector.memset(planes[:].bitcast(I32), 0)

        def hits(first, count):
            return offsets[:, first // LIST_ROWS : (first + count) // LIST_ROWS]

        picked = sb("sc_picked", [P, S], U8)
        nc.vector.tensor_copy(picked[:], sc_window[:].indirect(offsets[:]))
        for a in range(PASSES):
            nc.vector.tensor_copy(stage[a][STAGED, 0:S].bitcast(I32), picked[STAGED, :].bitcast(I32))

        def carry(a, width):
            first = STAGED.start + BLOCKS * a
            for r in range(4):
                nc.sync.dma_start(
                    out=planes[r:P:32, a * ROW : a * ROW + width].bitcast(I32),
                    in_=stage[a][first + r : first + BLOCKS : 4, 0:width].bitcast(I32),
                )

        carry(0, ROW)
        tab.append(sb("tab1", [P, T], I32, tag="sc_picked"))
        nc.sync.dma_start(out=tab[1][:], in_=tab_words[1].rearrange("p t i -> p (t i)").bitcast(I32))
        carry(1, S)

        widths = [HALF, SPAN]
        v = [[None] * (S // widths[a]) for a in range(PASSES)]

        def gather(a, i):
            if (a, i) == (0, 1):
                v[a][i] = placed("v0_1", [P, widths[a]], U32, stage0_at)
            else:
                v[a][i] = spread("v%d_%d" % (a, i), [P, widths[a]], U32, 4 * widths[a], MOVING)
            nc.vector.tensor_copy(v[a][i][:], tab[a][:].bitcast(U32).indirect(hits(i * widths[a], widths[a])))

        wq = [spread("wq%d" % a, [P, H], I32, 4 * H, FIXED) for a in range(PASSES)]
        wb = [spread("wb%d" % a, [P, 2 * H], U8, 2 * H, FIXED) for a in range(PASSES)]
        w_sc = spread("w_sc", [P, PASSES * 2 * H], U8, PASSES * 2 * H, FIXED_SC)

        def deal_wq(a, copy):
            copy(
                wq[a][:].bitcast(U32).rearrange("p (t c i) -> p c t i", t=PACK, i=4),
                wq_raw[a][:].bitcast(U32).rearrange("p (c i t) -> p c t i", t=PACK, i=4),
            )

        def deal_scales(first, count):
            nc.vector.tensor_copy(
                w_sc[:, first * H : (first + count) * H].rearrange("p (x t c i) -> p x c t i", x=count, t=PACK, i=16),
                planes[:, S + first * H : S + (first + count) * H].rearrange(
                    "p (x c i t) -> p x c t i", x=count, t=PACK, i=16
                ),
            )

        gather(0, 0)
        deal_wq(0, nc.vector.tensor_copy)
        deal_scales(0, 1)
        gather(0, 1)
        deal_scales(1, 1)
        deal_scales(2, 2)

        wq_raw.append(placed("wq_raw1", [P, H], I32, wq1_at))
        nc.sync.dma_start(out=wq_raw[1][:], in_=wq_words[1].rearrange("p c i -> p (c i)").bitcast(I32))
        wb_raw = placed("wb_raw", [P, PASSES, H // 2], I32, wb_at)
        nc.sync.dma_start(out=wb_raw[:], in_=wb_words.rearrange("a p c -> p a c").bitcast(I32))
        ws_rows = ws.rearrange("(a p j) c -> a p j c", a=PASSES, j=PACK)
        wt_rows = wt.rearrange("(p j) (g n) -> g p j n", j=PACK, g=GROUPS)
        ws_raw = []
        for a, at in enumerate((ws0_at, ws1_at)):
            ws_raw.append(placed("ws_raw%d" % a, [P, PACK, H], F32, at))
            nc.sync.dma_start(out=ws_raw[a][:], in_=ws_rows[a])
        wt_raw = [placed("wt_raw0", [P, PACK, PASS_ROWS], F32, 0)]
        nc.sync.dma_start(out=wt_raw[0][:], in_=wt_rows[0])
        bias = placed("bias", [P, GROUPS, BIAS_PITCH], F32, bias_at)
        nc.sync.dma_start(out=bias[:, :, 0:PACK], in_=bt.rearrange("(g p t) -> p g t", g=GROUPS, t=PACK))
        wt_raw.append(sb("wt_raw1", [P, PACK, PASS_ROWS], F32, tag="wq_raw0"))
        nc.sync.dma_start(out=wt_raw[1][:], in_=wt_rows[1])

        def deal_wb(a, copy):
            copy(
                wb[a][:].bitcast(U16).rearrange("p (t c i) -> p c t i", t=PACK, i=8),
                wb_raw[:, a, :].bitcast(U16).rearrange("p (c i t) -> p c t i", t=PACK, i=8),
            )

        for u in range(2):
            nc.scalar.copy(
                wq[1][:].bitcast(U32).rearrange("p (t c i) -> p c t i", t=PACK, i=4)[:, :, 2 * u : 2 * u + 2, :],
                wq_raw[1][:].bitcast(U32).rearrange("p (c i t) -> p c t i", t=PACK, i=4)[:, :, 2 * u : 2 * u + 2, :],
            )
        for i in range(S // SPAN):
            gather(1, i)
        deal_wb(0, nc.vector.tensor_copy)
        deal_wb(1, nc.vector.tensor_copy)

        def first_stage(acc, c, a, words, dtype, width, scales, start, stop, slices=range(PACK)):
            i, o = divmod(c * CHUNK, widths[a])
            for t in slices:
                nc.tensor.matmul_mx(
                    out=acc[:, t * CHUNK : (t + 1) * CHUNK],
                    lhsT=words[:, t * width : (t + 1) * width].bitcast(dtype),
                    lhsT_scale=scales[:, t * P : (t + 1) * P],
                    rhs=v[a][i][:, o : o + CHUNK].bitcast(FP8X4),
                    rhs_scale=planes[:, a * ROW + c * CHUNK : a * ROW + (c + 1) * CHUNK],
                    start=start and t == 0,
                    stop=stop and t == PACK - 1,
                )

        q_acc = {}
        d_acc = {}
        inv_noise = {}

        def noise(s, a):
            i, o = divmod(s * SPAN, widths[a])
            for t in range(PACK):
                u, place = divmod(t, 2)
                if a == 0 and place == 0:
                    q_acc[s, u] = bank(2 * s + u)
                nc.tensor.matmul_mx(
                    out=q_acc[s, u][:, place * SPAN : (place + 1) * SPAN],
                    lhsT=wq[a][:, t * P : (t + 1) * P].bitcast(FP8X4),
                    lhsT_scale=w_sc[:, a * H + t * P : a * H + (t + 1) * P],
                    rhs=v[a][i][:, o : o + SPAN].bitcast(FP8X4),
                    rhs_scale=planes[:, a * ROW + s * SPAN : a * ROW + (s + 1) * SPAN],
                    start=a == 0 and place == 0,
                    stop=a == PASSES - 1 and place == 1,
                )

        def exponentials(s):
            if s == SPANS - 1:
                inv_noise[s] = placed("inv_noise%d" % s, [P, PACK, SPAN], F32, last_noise)
            else:
                inv_noise[s] = sb("inv_noise%d" % s, [P, PACK, SPAN], F32)
            for u in range(2):
                nc.scalar.activation(
                    out=inv_noise[s][:, 2 * u : 2 * u + 2, :].rearrange("p t j -> p (t j)"),
                    in_=q_acc[s, u][:],
                    func=ACT.Exp,
                    scale=-1.0,
                )

        def dealt(rounded, raw, u):
            return (
                rounded[:].rearrange("p (t m j) -> p m j t", t=2, j=PACK),
                raw.rearrange("p j (m t) -> p m j t", t=PACK)[:, :, :, 2 * u : 2 * u + 2],
            )

        def quantize_pair(words, scales, rounded, u):
            cols = slice(2 * u * P, (2 * u + 2) * P)
            nc.vector.quantize_mx(out=words[:, cols].bitcast(FP8X4), scales=scales[:, cols], in_=rounded[:])

        ws_words = [spread("ws_words%d" % a, [P, H], U32, 4 * H, FIXED) for a in range(PASSES)]
        ws_sc = [spread("ws_sc%d" % a, [P, H], U8, H, FIXED_SC) for a in range(PASSES)]
        ws_bf = {}

        def negate_on_vector(dst, src):
            nc.vector.tensor_scalar(out=dst, in0=src, scalar1=-1.0, scalar2=None, op0=ALU.mult)

        def negate_on_scalar(dst, src):
            nc.scalar.activation(out=dst, in_=src, func=ACT.Copy, scale=-1.0)

        def round_ws(a, u, negate):
            ws_bf[a, u] = sb("ws_bf%d_%d" % (a, u), [P, 2 * P * PACK], BF16)
            negate(*dealt(ws_bf[a, u], ws_raw[a][:], u))

        def round_ws_part(a, u, negate, part):
            if (a, u) not in ws_bf:
                ws_bf[a, u] = sb("ws_bf%d_%d" % (a, u), [P, 2 * P * PACK], BF16)
            dst, src = dealt(ws_bf[a, u], ws_raw[a][:], u)
            negate(dst[:, part.start : part.stop], src[:, part.start : part.stop])

        def quantize_ws(a, u):
            quantize_pair(ws_words[a], ws_sc[a], ws_bf[a, u], u)

        wt_words = [spread("wt_words%d" % g, [P, PASS_ROWS], U32, 4 * PASS_ROWS, FIXED) for g in range(GROUPS)]
        wt_sc = [spread("wt_sc%d" % g, [P, PASS_ROWS], U8, PASS_ROWS, FIXED_SC) for g in range(GROUPS)]
        wt_bf = {}

        def round_wt(g, u, copy, tag=None):
            wt_bf[g, u] = sb("wt_bf%d_%d" % (g, u), [P, 2 * P * PACK], BF16, tag=tag)
            copy(*dealt(wt_bf[g, u], wt_raw[g][:], u))

        def round_wt_part(g, u, copy, part):
            if (g, u) not in wt_bf:
                wt_bf[g, u] = sb("wt_bf%d_%d" % (g, u), [P, 2 * P * PACK], BF16)
            dst, src = dealt(wt_bf[g, u], wt_raw[g][:], u)
            copy(dst[:, part.start : part.stop], src[:, part.start : part.stop])

        def quantize_wt(g, u):
            quantize_pair(wt_words[g], wt_sc[g], wt_bf[g, u], u)

        h_bf = [sb("h_bf%d" % s, [P, SPAN * PACK], BF16) for s in range(SPANS - 1)]
        behind_h = ws1_at + w_bytes
        h_bf.append(placed("h_bf3", [P, SPAN * PACK], BF16, behind_h + 1024))
        h_words = [spread("h_words%d" % half, [P, HALF], U32, 4 * HALF, MOVING) for half in range(S // HALF)]
        h_sc = [spread("h_sc%d" % half, [P, HALF], U8, HALF, MOVING_SC) for half in range(S // HALF)]
        y_sc = sb("y_sc", [P, S], U8)
        y_words = {}
        y = {}
        y_bf = {}

        def background(c, a, start, stop):
            if start:
                d_acc[c] = bank(c)
            first_stage(d_acc[c], c, a, wb[a][:], FP4X4, 2 * P, w_sc[:, (PASSES + a) * H : (PASSES + a + 1) * H], start, stop)

        def signal(c, a, start, stop):
            if start:
                d_acc[c] = bank(c)
            first_stage(d_acc[c], c, a, ws_words[a][:], FP8X4, P, ws_sc[a][:], start, stop)

        def signal_pair(c, a, u, stop):
            first_stage(d_acc[c], c, a, ws_words[a][:], FP8X4, P, ws_sc[a][:], False, stop, range(2 * u, 2 * u + 2))

        def signals(c):
            signal(c, 1, True, False)
            signal(c, 0, False, False)

        def backgrounds(c):
            background(c, 0, False, False)
            background(c, 1, False, True)

        def scale(c):
            s, i = divmod(c * CHUNK, SPAN)
            nc.vector.tensor_tensor(
                h_bf[s][:, i * PACK : (i + CHUNK) * PACK].rearrange("p (c i t) -> p c t i", t=PACK, i=RUN),
                inv_noise[s][:, :, i : i + CHUNK].rearrange("p t (c i) -> p c t i", i=RUN),
                d_acc[c][:].rearrange("p (t c i) -> p c t i", t=PACK, i=RUN),
                ALU.mult,
            )

        def quantize_h(c, count):
            half, o = divmod(c * CHUNK, HALF)
            w = count * CHUNK
            nc.vector.quantize_mx(
                out=h_words[half][:, o : o + w].bitcast(FP8X4),
                scales=h_sc[half][:, o : o + w],
                in_=h_bf[c // 2][:],
            )

        def features(g, first, width, slices, b):
            half, o = divmod(first, HALF)
            if (half, g) not in y:
                y[half, g] = sb("y%d_%d" % (half, g), [P, PACK, HALF], F32)
            acc = bank(b)
            cols = slice(o, o + width)
            for place, t in enumerate(slices):
                nc.tensor.matmul_mx(
                    out=acc[:, place * width : (place + 1) * width],
                    lhsT=wt_words[g][:, t * P : (t + 1) * P].bitcast(FP8X4),
                    lhsT_scale=wt_sc[g][:, t * P : (t + 1) * P],
                    rhs=h_words[half][:, cols].bitcast(FP8X4),
                    rhs_scale=h_sc[half][:, cols],
                    start=True,
                    stop=True,
                )
            for place, t in enumerate(slices):
                nc.scalar.activation(
                    out=y[half, g][:, t, cols],
                    in_=acc[:, place * width : (place + 1) * width],
                    func=ACT.Identity,
                    bias=bias[:, g, t : t + 1],
                )

        def store_y(g, first, width, slices):
            half, o = divmod(first, HALF)
            rows_out = out_0[PASS_ROWS * g : PASS_ROWS * (g + 1), first : first + width]
            nc.sync.dma_start(
                out=rows_out.rearrange("(p t) j -> p t j", t=PACK)[:, slices.start : slices.stop, :],
                in_=y[half, g][:, slices.start : slices.stop, o : o + width],
            )

        def kept(g, s, u, b):
            features(g, s * SPAN, SPAN, range(2 * u, 2 * u + 2), b)

        def narrow(g, s, u, b):
            kept(g, s, u, b)
            store_y(g, s * SPAN, SPAN, range(2 * u, 2 * u + 2))

        def early(g, s, u, b):
            kept(g, s, u, b)
            for t in range(2 * u, 2 * u + 2):
                store_y(g, s * SPAN, SPAN, range(t, t + 1))

        def wide(g, half, t, b):
            features(g, half * HALF, HALF, range(t, t + 1), b)
            store_y(g, half * HALF, HALF, range(t, t + 1))

        def round_on_gpsimd(g, s, tag, width=SPAN):
            half, o = divmod(s * SPAN, HALF)
            y_bf[g, s * SPAN] = sb("y_bf%d_%d" % (g, s * SPAN), [P, width, PACK], BF16, tag=tag)
            nc.gpsimd.tensor_copy(y_bf[g, s * SPAN][:], y[half, g][:, :, o : o + width].rearrange("p t j -> p j t"))

        def round_y(g, first, width, copy, tag=None, part=None, at=None):
            half, o = divmod(first, HALF)
            if at is not None:
                y_bf[g, first] = placed("y_bf%d_%d" % (g, first), [P, width, PACK], BF16, at)
            if (g, first) not in y_bf:
                y_bf[g, first] = sb("y_bf%d_%d" % (g, first), [P, width, PACK], BF16, tag=tag)
            part = part or range(width)
            copy(
                y_bf[g, first][:, part.start : part.stop, :].rearrange("p (c i) t -> p c t i", i=4),
                y[half, g][:, :, o + part.start : o + part.stop].rearrange("p t (c i) -> p c t i", i=4),
            )

        def quantize_y(g, first, width, tag=None, at=None):
            cols = slice(first, first + width)
            half, o = divmod(first, HALF)
            if at is not None:
                y_words[half, g] = placed("y_words%d_%d" % (half, g), [P, HALF], U32, at)
            if (half, g) not in y_words:
                y_words[half, g] = sb("y_words%d_%d" % (half, g), [P, HALF], U32, tag=tag)
            nc.vector.quantize_mx(
                out=y_words[half, g][:, o : o + width].bitcast(FP8X4),
                scales=y_sc[4 * g : P, cols],
                in_=y_bf[g, first][:].rearrange("p j t -> p (j t)"),
            )

        def store_words(half, g):
            nc.sync.dma_start(
                out=out_1[g].rearrange("p m t -> p (m t)").bitcast(I32)[:, half * HALF : (half + 1) * HALF],
                in_=y_words[half, g][:].bitcast(I32),
            )

        for s in range(SPANS):
            noise(s, 0)
        for s in range(SPANS):
            noise(s, 1)
            if s < SPANS - 1:
                exponentials(s)
        for u in range(2):
            round_ws(0, u, negate_on_vector)
        for u in range(2):
            quantize_ws(0, u)
        round_ws(1, 0, negate_on_vector)
        round_ws_part(1, 1, negate_on_scalar, range(WS_SHARE))
        round_ws_part(1, 1, negate_on_vector, range(WS_SHARE, P))
        exponentials(SPANS - 1)
        for u in range(2):
            quantize_ws(1, u)
        first = range(CHUNKS // 2)
        for c in first:
            background(c, 0, True, False)
        for c in first:
            background(c, 1, False, False)
        for c in range(2):
            signal(c, 0, False, False)
        for u in range(2):
            for c in range(2):
                signal_pair(c, 1, u, True)
        for c in range(2, 4):
            signal(c, 1, False, False)
            signal(c, 0, False, True)
        round_wt(0, 0, negate_on_scalar)
        round_wt(0, 1, negate_on_scalar)
        scale(0)
        scale(1)
        scale(2)
        quantize_h(0, 2)
        quantize_wt(0, 0)
        signals(4)
        backgrounds(4)
        early(0, 0, 0, 0)
        scale(3)
        quantize_wt(0, 1)
        signals(5)
        round_wt_part(1, 0, negate_on_scalar, range(WT_SHARE))
        early(0, 0, 1, 1)
        quantize_h(2, 2)
        early(0, 1, 0, 2)
        narrow(0, 1, 1, 3)
        backgrounds(5)
        round_wt_part(1, 0, negate_on_vector, range(WT_SHARE, P))
        round_wt_part(1, 1, negate_on_vector, range(P // 2))
        quantize_wt(1, 0)
        round_wt_part(1, 1, negate_on_vector, range(P // 2, P))
        scale(4)
        quantize_wt(1, 1)
        signal(6, 1, True, False)
        wide(1, 0, 0, 0)
        signal(6, 0, False, False)
        wide(1, 0, 1, 1)
        background(6, 0, False, False)
        wide(1, 0, 2, 2)
        background(6, 1, False, True)
        wide(1, 0, 3, 3)
        scale(5)
        round_y(0, 0, SPAN, nc.vector.tensor_copy, tag="wt_bf1_1")
        quantize_h(4, 2)
        round_y(0, SPAN, SPAN, nc.vector.tensor_copy, tag="h_bf2")
        signal(7, 1, True, False)
        narrow(1, 2, 0, 4)
        signal(7, 0, False, False)
        narrow(1, 2, 1, 5)
        backgrounds(7)
        round_y(1, 0, CHUNK, nc.scalar.copy)
        quantize_y(0, 0, SPAN)
        quantize_y(0, SPAN, SPAN)
        store_words(0, 0)
        round_on_gpsimd(1, 1, "h_bf2", CHUNK)
        scale(6)
        narrow(0, 2, 0, 0)
        narrow(0, 2, 1, 1)
        scale(7)
        round_y(1, CHUNK, CHUNK, nc.vector.tensor_copy, tag="wt_bf1_1")
        quantize_h(6, 2)
        round_y(1, 2 * SPAN, SPAN, nc.scalar.copy, part=range(MID2))
        for u in range(2):
            narrow(0, 3, u, 2 + u)
        kept(1, 3, 0, 6)
        kept(1, 3, 1, 7)
        store_y(1, 3 * SPAN, SPAN, range(PACK))
        quantize_y(1, 0, CHUNK, at=behind_h)
        round_y(1, SPAN + CHUNK, CHUNK, nc.vector.tensor_copy, at=behind_h + 2048)
        quantize_y(1, CHUNK, CHUNK)
        quantize_y(1, SPAN, CHUNK)
        round_y(1, 2 * SPAN, SPAN, nc.vector.tensor_copy, part=range(MID2, SPAN))
        quantize_y(1, SPAN + CHUNK, CHUNK)
        store_words(0, 1)
        round_y(0, 2 * SPAN, SPAN, nc.vector.tensor_copy, tag="h_bf2")
        quantize_y(1, 2 * SPAN, SPAN)
        round_y(0, 3 * SPAN, SPAN, nc.vector.tensor_copy)
        quantize_y(0, 2 * SPAN, SPAN)
        round_y(1, 3 * SPAN, SPAN, nc.scalar.copy, part=range(LAST))
        round_y(1, 3 * SPAN, SPAN, nc.vector.tensor_copy, part=range(LAST, SPAN))
        quantize_y(0, 3 * SPAN, SPAN)
        store_words(1, 0)
        quantize_y(1, 3 * SPAN, SPAN)
        store_words(1, 1)

        for r in range(4):
            nc.scalar.dma_start(
                out=out_2[:, 4 * r : 4 * r + 4, :].bitcast(I32),
                in_=y_sc[32 * r : 32 * r + 4 * GROUPS, :].bitcast(I32),
            )
